import numpy as np
import ml_dtypes


def mxq(x, axis, fmt="e4m3"):
    dtype, down = {"e4m3": (ml_dtypes.float8_e4m3fn, 7), "e5m2": (ml_dtypes.float8_e5m2, 14)}[fmt]
    v = np.moveaxis(np.asarray(x, np.float32).astype(ml_dtypes.bfloat16).astype(np.float64), axis, -1)
    blocks = v.reshape(v.shape[:-1] + (-1, 32))
    amax = np.abs(blocks).max(-1, keepdims=True)
    byte = np.maximum(np.where(amax > 0, np.frexp(amax)[1] - 1 + 127, 0) - down, 1)
    scale = np.exp2(byte - 127.0)
    codes = (blocks / scale).astype(np.float32).astype(dtype).astype(np.float64)
    return np.moveaxis((codes * scale).reshape(v.shape), -1, axis)


WIDE = False


def mx_kscale(k):
    if not WIDE:
        return np.ones(k)
    levels = np.array([24, -24, 12, -12, 0])
    if k % 512:
        return np.exp2(np.random.permutation(np.resize(levels, k // 32))).repeat(32)
    a = np.empty((k // 512, 16))
    for p in range(k // 512):
        a[p, :8] = np.random.permutation(np.resize(levels, 8))
        for g in range(8):
            far = levels[np.abs(levels - a[p, g]) >= 10]
            a[p, g + 8] = far[np.random.randint(len(far))]
    return np.exp2(a.ravel()).repeat(32)


def f64(x):
    return np.asarray(x).astype(np.float64)


def striped(idx):
    return np.tile(idx.reshape(-1, 16).T, (8, 1)).astype(np.uint16)


def unstriped(offs):
    return offs[:16].T.reshape(-1).astype(np.int64)


E2M1 = np.array([0.0, 0.5, 1.0, 1.5, 2.0, 3.0, 4.0, 6.0, -0.0, -0.5, -1.0, -1.5, -2.0, -3.0, -4.0, -6.0])


def pack_weight(w, fmt):
    k, n = w.shape
    w = f64(np.asarray(w, np.float32).astype(ml_dtypes.bfloat16)).reshape(k // 32, 32, n)
    amax = np.abs(w).max(1)
    if fmt == "e4m3":
        byte = np.frexp(amax)[1] - 1 + 127 - 7
    else:
        mant, ex = np.frexp(amax / 6.0)
        byte = np.where(mant > 0.5, ex, ex - 1) + 127
    byte = np.clip(np.where(amax > 0, byte, 1), 1, 254)
    scaled = (w * np.exp2(127.0 - byte)[:, None, :]).reshape(k, n).astype(np.float32)
    by_word = np.ascontiguousarray(scaled.reshape(k // 512, 128, 4, n).transpose(0, 1, 3, 2))
    if fmt == "e4m3":
        words = by_word.astype(ml_dtypes.float8_e4m3fn).view(np.uint8)
    else:
        c = by_word.astype(ml_dtypes.float4_e2m1fn).view(np.uint8) & 0xF
        words = (c[..., 0::2] | (c[..., 1::2] << 4)).reshape(k // 512, 128, 2 * n)
    return np.ascontiguousarray(words), np.ascontiguousarray(byte.astype(np.uint8).reshape(k // 512, 16, n))


def unpack_weight(words, scales, fmt):
    g, _, n = scales.shape
    words = np.ascontiguousarray(words).reshape(g, 128, n, -1)
    if fmt == "e4m3":
        vals = words.view(ml_dtypes.float8_e4m3fn).astype(np.float64)
    else:
        nib = np.empty((g, 128, n, 4), np.uint8)
        nib[..., 0::2] = words & 0xF
        nib[..., 1::2] = words >> 4
        vals = E2M1[nib]
    vals = vals * np.repeat(np.exp2(scales.astype(np.float64) - 127.0), 8, axis=1)[..., None]
    return vals.transpose(0, 1, 3, 2).reshape(g * 512, n)


def pack_table4(v):
    words, scales = pack_weight(v, "e2m1")
    g, t = words.shape[0] // 2, v.shape[1]
    return np.ascontiguousarray(words.reshape(g, 2, 128, t, 2).transpose(0, 2, 3, 1, 4).reshape(g, 128, t, 4)), scales


def unpack_table4(words, scales):
    g, _, t, _ = words.shape
    return unpack_weight(words.reshape(g, 128, t, 2, 2).transpose(0, 3, 1, 2, 4).reshape(2 * g, 128, 2 * t), scales, "e2m1")


def sigm(f):
    return 1.0 / (1.0 + np.exp(-np.maximum(f, -700.0)))


K, N, T, J = 1024, 256, 4096, 2048


def setup_inputs():
    n = np.random.standard_normal
    s = mx_kscale(K)[:, None]
    p_tab = pack_table4(n((K, T)) * s)
    p_wk4 = pack_weight(n((K, N)) / np.sqrt(K) / s, "e2m1")
    p_wv4 = pack_weight(n((K, N)) / np.sqrt(K) / s, "e2m1")
    return {
        "tab_words": p_tab[0],
        "tab_scales": p_tab[1],
        "wk4_words": p_wk4[0],
        "wk4_scales": p_wk4[1],
        "wkd": (0.4 * (n((K, N)) / np.sqrt(K) / s)).astype(np.float32),
        "wv4_words": p_wv4[0],
        "wv4_scales": p_wv4[1],
        "wvd": (0.4 * (n((K, N)) / np.sqrt(K) / s)).astype(np.float32),
        "st": (n((N, J))).astype(np.float32),
        "b": (0.3 * n(N)).astype(np.float32),
        "res": (n((N, J))).astype(np.float32),
        "offs": striped(np.random.permutation(T)[:J]),
    }


def reference(tab_words, tab_scales, wk4_words, wk4_scales, wkd, wv4_words, wv4_scales, wvd, st, b, res, offs):
    idx = unstriped(offs)
    tab_ = unpack_table4(tab_words, tab_scales)[:, idx]
    wk4_ = unpack_weight(wk4_words, wk4_scales, "e2m1")
    wkd_ = mxq(f64(wkd), 0, "e4m3")
    wv4_ = unpack_weight(wv4_words, wv4_scales, "e2m1")
    wvd_ = mxq(f64(wvd), 0, "e4m3")
    ke = wk4_.T @ tab_ + wkd_.T @ tab_
    ve = wv4_.T @ tab_ + wvd_.T @ tab_
    gate = sigm(ke * f64(st) + f64(b)[:, None])
    return f64(res) + gate * ve

@@ -1,0 +1,209 @@
+from contextlib import ExitStack
+
+import concourse.mybir as mybir
+
+K, N, T, J = 1024, 256, 4096, 2048
+FLOPS = 4 * 2 * K * N * J
+
+F32 = mybir.dt.float32
+BF16 = mybir.dt.bfloat16
+I32 = mybir.dt.int32
+U32 = mybir.dt.uint32
+U16 = mybir.dt.uint16
+U8 = mybir.dt.uint8
+FP8X4 = mybir.dt.float8_e4m3fn_x4
+FP4X4 = mybir.dt.float4_e2m1fn_x4
+MULT = mybir.AluOpType.mult
+ADD = mybir.AluOpType.add
+SIGMOID = mybir.ActivationFunctionType.Sigmoid
+
+P = 128
+PASSES = 2
+HALVES = 2
+CH = 512
+CHUNKS = J // CH
+SHIFT = 16
+
+
+def tile_list_engram_dl_dl_bsig_kernel(
+    tc, tab_words, tab_scales, wk4_words, wk4_scales, wkd, wv4_words, wv4_scales, wvd, st, b, res, offs, out
+):
+    nc = tc.nc
+    with ExitStack() as ctx:
+        keep = ctx.enter_context(tc.tile_pool(name="keep", bufs=1))
+        psum = ctx.enter_context(tc.psum_pool(name="psum", bufs=1))
+
+        offsets = keep.tile([P, J // 16], U16, name="offsets")
+        nc.sync.dma_start(offsets[:], offs)
+
+        tscale = keep.tile([P, T], U8, name="tscale", align_bytes=64)
+        nc.vector.memset(tscale[:].bitcast(I32), 0)
+        ts_rows = tab_scales.bitcast(I32).rearrange("a (q r) t -> r q a t", r=4)
+        for r in range(4):
+            nc.scalar.dma_start(tscale[:].bitcast(I32)[r:P:SHIFT, :], ts_rows[r])
+
+        table = keep.tile([P, T], I32, name="table", align_bytes=64)
+        nc.sync.dma_start(table[:], tab_words[0].rearrange("p t i -> p (t i)").bitcast(I32))
+
+        w4scale = keep.tile([P, 2 * PASSES * N], U8, name="w4scale", align_bytes=64)
+        nc.vector.memset(w4scale[:].bitcast(I32), 0)
+        plane1 = keep.tile([P, J], U8, name="plane1", align_bytes=64)
+        nc.vector.memset(plane1[:].bitcast(I32), 0)
+        warm = keep.tile([P, 2], F32, name="warm")
+        nc.vector.memset(warm[:, 0:1], 0.0)
+        nc.scalar.activation(warm[:, 1:2], warm[:, 0:1], SIGMOID)
+
+        w4 = []
+        for w, (words, scales) in enumerate(((wk4_words, wk4_scales), (wv4_words, wv4_scales))):
+            tl = keep.tile([P, PASSES * 2 * N], U8, name=f"w4_{w}", align_bytes=64)
+            nc.sync.dma_start(
+                tl[:].bitcast(I32).rearrange("p (a n) -> p a n", a=PASSES),
+                words.bitcast(I32).rearrange("a p n -> p a n"),
+            )
+            w4.append(tl)
+            rows = scales.bitcast(I32).rearrange("a (q r) n -> r q a n", r=4)
+            dst = w4scale[:, w * PASSES * N : (w + 1) * PASSES * N].bitcast(I32).rearrange("p (a n) -> p a n", a=PASSES)
+            for r in range(4):
+                nc.gpsimd.dma_start(dst[r:P:32], rows[r])
+
+        raw = {}
+        for w, wd in enumerate((wkd, wvd)):
+            for a in range(PASSES):
+                raw[w, a] = keep.tile([P, 4, N], F32, name=f"raw{w}{a}")
+                nc.sync.dma_start(raw[w, a][:], wd[a * 512 : (a + 1) * 512, :].rearrange("(p i) n -> p i n", i=4))
+        bias = keep.tile([P, HALVES], F32, name="bias")
+        with nc.allow_non_contiguous_dma(reason="one bias value a partition"):
+            nc.sync.dma_start(bias[:], b.rearrange("(h p) -> p h", p=P))
+        st_t, res_t = [], []
+        for c in range(CHUNKS):
+            cols = slice(c * CH, (c + 1) * CH)
+            s = keep.tile([P, HALVES, CH], F32, name=f"st{c}")
+            nc.sync.dma_start(s[:], st.rearrange("(h p) j -> p h j", p=P)[:, :, cols])
+            st_t.append(s)
+            s = keep.tile([P, HALVES, CH], F32, name=f"res{c}")
+            nc.sync.dma_start(s[:], res.rearrange("(h p) j -> p h j", p=P)[:, :, cols])
+            res_t.append(s)
+
+        plane0, parted, codes, dscale, bank, gate = {}, {}, {}, {}, {}, {}
+
+        def lst(c):
+            return offsets[:, c * CH // 16 : (c + 1) * CH // 16]
+
+        def gather_scales(c, tag):
+            plane0[c] = keep.tile([P, CH], U8, name=f"plane0_{c}", tag=tag, align_bytes=64)
+            nc.vector.tensor_copy(plane0[c][:], tscale[:].indirect(lst(c)))
+            nc.gpsimd.dma_start(
+                plane1[:, c * CH : (c + 1) * CH].bitcast(I32)[0 : P - SHIFT, :], plane0[c][:].bitcast(I32)[SHIFT:P, :]
+            )
+
+        def gather_words(c, tag):
+            gw = keep.tile([P, CH], U32, name=f"gw{c}", tag=tag, align_bytes=64)
+            nc.vector.tensor_copy(gw[:], table[:].bitcast(U32).indirect(lst(c)))
+            parted[c] = keep.tile([P, PASSES * 2 * CH], U8, name=f"parted{c}", align_bytes=64)
+            nc.vector.tensor_copy(
+                parted[c][:].bitcast(U16).rearrange("p (d j) -> p d j", d=PASSES),
+                gw[:].bitcast(U16).rearrange("p (j d) -> p d j", d=PASSES),
+            )
+
+        def quantise(w, a):
+            g = keep.tile([P, 4 * N], BF16, name=f"grouped{w}{a}", align_bytes=64)
+            nc.scalar.copy(
+                g[:].rearrange("p (c i t) -> p c t i", i=4, t=4),
+                raw[w, a][:].rearrange("p t (c i) -> p c t i", i=4),
+            )
+            codes[w, a] = keep.tile([P, N], U32, name=f"codes{w}{a}", align_bytes=64)
+            dscale[w, a] = keep.tile([P, N], U8, name=f"dscale{w}{a}", align_bytes=64)
+            nc.vector.quantize_mx(out=codes[w, a][:].bitcast(FP8X4), scales=dscale[w, a][:], in_=g[:])
+
+        def moving(c, a):
+            words = parted[c][:, a * 2 * CH : (a + 1) * 2 * CH].bitcast(FP4X4)
+            scale = plane0[c][:] if a == 0 else plane1[:, c * CH : (c + 1) * CH]
+            return words, scale
+
+        def base_pass(c, w, h, a):
+            if a == 0:
+                slot = (c % 2) * 4 + 2 * w + h
+                bank[c, w, h] = psum.tile([P, CH], F32, name=f"bank{c}{w}{h}", tag=f"bank{slot}")
+            words, scale = moving(c, a)
+            c0 = a * N + h * P
+            nc.tensor.matmul_mx(
+                out=bank[c, w, h][:],
+                lhsT=w4[w][:, 2 * c0 : 2 * (c0 + P)].bitcast(FP4X4),
+                lhsT_scale=w4scale[:, w * PASSES * N + c0 : w * PASSES * N + c0 + P],
+                rhs=words,
+                rhs_scale=scale,
+                start=(a == 0),
+                stop=False,
+            )
+
+        def delta_pass(c, w, h, a):
+            words, scale = moving(c, a)
+            nc.tensor.matmul_mx(
+                out=bank[c, w, h][:],
+                lhsT=codes[w, a][:, h * P : (h + 1) * P].bitcast(FP8X4),
+                lhsT_scale=dscale[w, a][:, h * P : (h + 1) * P],
+                rhs=words,
+                rhs_scale=scale,
+                start=False,
+                stop=(a == PASSES - 1),
+            )
+
+        def base(c, w):
+            for a in range(PASSES):
+                for h in range(HALVES):
+                    base_pass(c, w, h, a)
+
+        def delta(c, w):
+            for h in range(HALVES):
+                for a in range(PASSES):
+                    delta_pass(c, w, h, a)
+
+        def make_gate(c, h):
+            pre = keep.tile([P, CH], F32, name=f"pre{c}{h}")
+            nc.vector.tensor_tensor(pre[:], bank[c, 0, h][:], st_t[c][:, h, :], MULT)
+            gate[c, h] = keep.tile([P, CH], F32, name=f"gate{c}{h}")
+            nc.scalar.activation(gate[c, h][:], pre[:], SIGMOID, bias=bias[:, h : h + 1])
+
+        def finish(c, h):
+            u = keep.tile([P, CH], F32, name=f"u{c}{h}")
+            nc.vector.tensor_tensor(u[:], bank[c, 1, h][:], gate[c, h][:], MULT)
+            o = keep.tile([P, CH], F32, name=f"o{c}{h}")
+            eng = nc.vector if c == CHUNKS - 1 else nc.gpsimd
+            eng.tensor_tensor(o[:], u[:], res_t[c][:, h, :], ADD)
+            nc.sync.dma_start(out[h * P : (h + 1) * P, c * CH : (c + 1) * CH], o[:])
+
+        gather_scales(0, "g0")
+        gather_scales(1, "g1")
+        gather_words(0, "gw0")
+        for a in range(PASSES):
+            for w in range(2):
+                for h in range(HALVES):
+                    base_pass(0, w, h, a)
+        gather_words(1, "gw1")
+        quantise(0, 0)
+        quantise(0, 1)
+        delta(0, 0)
+        gather_scales(2, "gw0")
+        base(1, 0)
+        delta(1, 0)
+        base(1, 1)
+        quantise(1, 0)
+        quantise(1, 1)
+        delta(0, 1)
+        gather_scales(3, "gw1")
+        gather_words(2, "gw2")
+        delta(1, 1)
+        for h in range(HALVES):
+            make_gate(0, h)
+        for h in range(HALVES):
+            finish(0, h)
+        gather_words(3, "gw3")
+        for c in range(1, CHUNKS):
+            if c + 1 < CHUNKS:
+                for w in range(2):
+                    base(c + 1, w)
+                    delta(c + 1, w)
+            for h in range(HALVES):
+                make_gate(c, h)
+            for h in range(HALVES):
+                finish(c, h)

@@ -23,6 +23,7 @@ HALVES = 2
 CH = 512
 CHUNKS = J // CH
 SHIFT = 16
+KEY, VALUE = 0, 1
 
 
 def tile_list_engram_dl_dl_bsig_kernel(
@@ -37,68 +38,59 @@ def tile_list_engram_dl_dl_bsig_kernel(
         nc.sync.dma_start(offsets[:], offs)
 
         tscale = keep.tile([P, T], U8, name="tscale", align_bytes=64)
-        nc.vector.memset(tscale[:].bitcast(I32), 0)
-        ts_rows = tab_scales.bitcast(I32).rearrange("a (q r) t -> r q a t", r=4)
-        for r in range(4):
-            nc.scalar.dma_start(tscale[:].bitcast(I32)[r:P:SHIFT, :], ts_rows[r])
+        w4scale = [keep.tile([P, PASSES * N], U8, name=f"w4scale{w}", align_bytes=64) for w in range(2)]
+        plane0 = keep.tile([P, J], U8, name="plane0", align_bytes=64)
+        plane1 = keep.tile([P, J], U8, name="plane1", align_bytes=64)
 
-        table = keep.tile([P, T], I32, name="table", align_bytes=64)
+        with tc.tile_pool(name="early", bufs=1) as early:
+            warm = early.tile([P, 2], F32, name="warm")
+            nc.vector.memset(warm[:, 0:1], 0.0)
+            nc.vector.memset(tscale[:].bitcast(I32), 0)
+            ts_rows = tab_scales.bitcast(I32).rearrange("a (q r) t -> r q a t", r=4)
+            for r in range(4):
+                nc.sync.dma_start(tscale[:].bitcast(I32)[r:P:SHIFT, :], ts_rows[r])
+            nc.scalar.activation(warm[:, 1:2], warm[:, 0:1], SIGMOID)
+        late = ctx.enter_context(tc.tile_pool(name="late", bufs=1))
+
+        for w in range(2):
+            nc.vector.memset(w4scale[w][:].bitcast(I32), 0)
+        nc.vector.memset(plane1[:].bitcast(I32), 0)
+
+        table = late.tile([P, T], I32, name="table", align_bytes=64)
         nc.sync.dma_start(table[:], tab_words[0].rearrange("p t i -> p (t i)").bitcast(I32))
 
-        w4scale = keep.tile([P, 2 * PASSES * N], U8, name="w4scale", align_bytes=64)
-        nc.vector.memset(w4scale[:].bitcast(I32), 0)
-        plane1 = keep.tile([P, J], U8, name="plane1", align_bytes=64)
-        nc.vector.memset(plane1[:].bitcast(I32), 0)
-        warm = keep.tile([P, 2], F32, name="warm")
-        nc.vector.memset(warm[:, 0:1], 0.0)
-        nc.scalar.activation(warm[:, 1:2], warm[:, 0:1], SIGMOID)
+        w4, raw, st_t, res_t = {}, {}, {}, {}
+        parted, codes, dscale, bank, gate, prod = {}, {}, {}, {}, {}, {}
 
-        w4 = []
-        for w, (words, scales) in enumerate(((wk4_words, wk4_scales), (wv4_words, wv4_scales))):
-            tl = keep.tile([P, PASSES * 2 * N], U8, name=f"w4_{w}", align_bytes=64)
+        def load_base_words(w, words):
+            w4[w] = late.tile([P, PASSES * 2 * N], U8, name=f"w4_{w}", align_bytes=64)
             nc.sync.dma_start(
-                tl[:].bitcast(I32).rearrange("p (a n) -> p a n", a=PASSES),
+                w4[w][:].bitcast(I32).rearrange("p (a n) -> p a n", a=PASSES),
                 words.bitcast(I32).rearrange("a p n -> p a n"),
             )
-            w4.append(tl)
+
+        def load_base_scales(w, scales):
             rows = scales.bitcast(I32).rearrange("a (q r) n -> r q a n", r=4)
-            dst = w4scale[:, w * PASSES * N : (w + 1) * PASSES * N].bitcast(I32).rearrange("p (a n) -> p a n", a=PASSES)
+            dst = w4scale[w][:].bitcast(I32).rearrange("p (a n) -> p a n", a=PASSES)
             for r in range(4):
-                nc.gpsimd.dma_start(dst[r:P:32], rows[r])
+                nc.sync.dma_start(dst[r:P:32], rows[r])
 
-        raw = {}
-        for w, wd in enumerate((wkd, wvd)):
-            for a in range(PASSES):
-                raw[w, a] = keep.tile([P, 4, N], F32, name=f"raw{w}{a}")
-                nc.sync.dma_start(raw[w, a][:], wd[a * 512 : (a + 1) * 512, :].rearrange("(p i) n -> p i n", i=4))
-        bias = keep.tile([P, HALVES], F32, name="bias")
-        with nc.allow_non_contiguous_dma(reason="one bias value a partition"):
-            nc.sync.dma_start(bias[:], b.rearrange("(h p) -> p h", p=P))
-        st_t, res_t = [], []
-        for c in range(CHUNKS):
-            cols = slice(c * CH, (c + 1) * CH)
-            s = keep.tile([P, HALVES, CH], F32, name=f"st{c}")
-            nc.sync.dma_start(s[:], st.rearrange("(h p) j -> p h j", p=P)[:, :, cols])
-            st_t.append(s)
-            s = keep.tile([P, HALVES, CH], F32, name=f"res{c}")
-            nc.sync.dma_start(s[:], res.rearrange("(h p) j -> p h j", p=P)[:, :, cols])
-            res_t.append(s)
+        def load_delta(w, wd, a):
+            raw[w, a] = late.tile([P, 4, N], F32, name=f"raw{w}{a}")
+            nc.sync.dma_start(raw[w, a][:], wd[a * 512 : (a + 1) * 512, :].rearrange("(p i) n -> p i n", i=4))
 
-        plane0, parted, codes, dscale, bank, gate = {}, {}, {}, {}, {}, {}
+        def load_cols(dst, src, c, name):
+            dst[c] = late.tile([P, HALVES, CH], F32, name=f"{name}{c}")
+            nc.sync.dma_start(dst[c][:], src.rearrange("(h p) j -> p h j", p=P)[:, :, c * CH : (c + 1) * CH])
 
-        def lst(c):
-            return offsets[:, c * CH // 16 : (c + 1) * CH // 16]
-
-        def gather_scales(c, tag):
-            plane0[c] = keep.tile([P, CH], U8, name=f"plane0_{c}", tag=tag, align_bytes=64)
-            nc.vector.tensor_copy(plane0[c][:], tscale[:].indirect(lst(c)))
-            nc.gpsimd.dma_start(
-                plane1[:, c * CH : (c + 1) * CH].bitcast(I32)[0 : P - SHIFT, :], plane0[c][:].bitcast(I32)[SHIFT:P, :]
-            )
+        def gather_scales(c0, c1):
+            cols = slice(c0 * CH, c1 * CH)
+            nc.vector.tensor_copy(plane0[:, cols], tscale[:].indirect(offsets[:, c0 * CH // 16 : c1 * CH // 16]))
+            nc.sync.dma_start(plane1[:, cols].bitcast(I32)[0 : P - SHIFT, :], plane0[:, cols].bitcast(I32)[SHIFT:P, :])
 
         def gather_words(c, tag):
             gw = keep.tile([P, CH], U32, name=f"gw{c}", tag=tag, align_bytes=64)
-            nc.vector.tensor_copy(gw[:], table[:].bitcast(U32).indirect(lst(c)))
+            nc.vector.tensor_copy(gw[:], table[:].bitcast(U32).indirect(offsets[:, c * CH // 16 : (c + 1) * CH // 16]))
             parted[c] = keep.tile([P, PASSES * 2 * CH], U8, name=f"parted{c}", align_bytes=64)
             nc.vector.tensor_copy(
                 parted[c][:].bitcast(U16).rearrange("p (d j) -> p d j", d=PASSES),
@@ -106,19 +98,15 @@ def tile_list_engram_dl_dl_bsig_kernel(
             )
 
         def quantise(w, a):
-            g = keep.tile([P, 4 * N], BF16, name=f"grouped{w}{a}", align_bytes=64)
-            nc.scalar.copy(
-                g[:].rearrange("p (c i t) -> p c t i", i=4, t=4),
-                raw[w, a][:].rearrange("p t (c i) -> p c t i", i=4),
-            )
+            g = keep.tile([P, 4 * N], BF16, name=f"grouped{w}{a}", tag=f"grouped{w}{a}", align_bytes=64)
+            nc.scalar.copy(g[:].rearrange("p (n i) -> p n i", i=4), raw[w, a][:].rearrange("p i n -> p n i"))
             codes[w, a] = keep.tile([P, N], U32, name=f"codes{w}{a}", align_bytes=64)
             dscale[w, a] = keep.tile([P, N], U8, name=f"dscale{w}{a}", align_bytes=64)
             nc.vector.quantize_mx(out=codes[w, a][:].bitcast(FP8X4), scales=dscale[w, a][:], in_=g[:])
 
         def moving(c, a):
             words = parted[c][:, a * 2 * CH : (a + 1) * 2 * CH].bitcast(FP4X4)
-            scale = plane0[c][:] if a == 0 else plane1[:, c * CH : (c + 1) * CH]
-            return words, scale
+            return words, (plane0, plane1)[a][:, c * CH : (c + 1) * CH]
 
         def base_pass(c, w, h, a):
             if a == 0:
@@ -129,7 +117,7 @@ def tile_list_engram_dl_dl_bsig_kernel(
             nc.tensor.matmul_mx(
                 out=bank[c, w, h][:],
                 lhsT=w4[w][:, 2 * c0 : 2 * (c0 + P)].bitcast(FP4X4),
-                lhsT_scale=w4scale[:, w * PASSES * N + c0 : w * PASSES * N + c0 + P],
+                lhsT_scale=w4scale[w][:, c0 : c0 + P],
                 rhs=words,
                 rhs_scale=scale,
                 start=(a == 0),
@@ -148,62 +136,98 @@ def tile_list_engram_dl_dl_bsig_kernel(
                 stop=(a == PASSES - 1),
             )
 
-        def base(c, w):
-            for a in range(PASSES):
-                for h in range(HALVES):
+        def base(c, w, halves=range(HALVES)):
+            for h in halves:
+                for a in range(PASSES):
                     base_pass(c, w, h, a)
 
-        def delta(c, w):
-            for h in range(HALVES):
+        def delta(c, w, halves=range(HALVES)):
+            for h in halves:
                 for a in range(PASSES):
                     delta_pass(c, w, h, a)
 
-        def make_gate(c, h):
-            pre = keep.tile([P, CH], F32, name=f"pre{c}{h}")
-            nc.vector.tensor_tensor(pre[:], bank[c, 0, h][:], st_t[c][:, h, :], MULT)
-            gate[c, h] = keep.tile([P, CH], F32, name=f"gate{c}{h}")
-            nc.scalar.activation(gate[c, h][:], pre[:], SIGMOID, bias=bias[:, h : h + 1])
+        def make_gates(c):
+            for h in range(HALVES):
+                pre = keep.tile([P, CH], F32, name=f"pre{c}{h}", tag=f"pre{c}{h}", align_bytes=64)
+                nc.vector.tensor_tensor(pre[:], bank[c, KEY, h][:], st_t[c][:, h, :], MULT)
+                gate[c, h] = keep.tile([P, CH], F32, name=f"gate{c}{h}")
+                nc.scalar.activation(gate[c, h][:], pre[:], SIGMOID, bias=bias[:, h : h + 1])
 
-        def finish(c, h):
-            u = keep.tile([P, CH], F32, name=f"u{c}{h}")
-            nc.vector.tensor_tensor(u[:], bank[c, 1, h][:], gate[c, h][:], MULT)
-            o = keep.tile([P, CH], F32, name=f"o{c}{h}")
-            eng = nc.vector if c == CHUNKS - 1 else nc.gpsimd
-            eng.tensor_tensor(o[:], u[:], res_t[c][:, h, :], ADD)
-            nc.sync.dma_start(out[h * P : (h + 1) * P, c * CH : (c + 1) * CH], o[:])
+        def gated(c, h, q):
+            nc.vector.tensor_tensor(prod[c, h][:, q], bank[c, VALUE, h][:, q], gate[c, h][:, q], MULT)
 
-        gather_scales(0, "g0")
-        gather_scales(1, "g1")
-        gather_words(0, "gw0")
-        for a in range(PASSES):
-            for w in range(2):
+        def add_store(c, h, q, eng):
+            o = keep.tile([P, q.stop - q.start], F32, name=f"o{c}{h}{q.start}")
+            eng.tensor_tensor(o[:], prod[c, h][:, q], res_t[c][:, h, q], ADD)
+            nc.sync.dma_start(out[h * P : (h + 1) * P, c * CH + q.start : c * CH + q.stop], o[:])
+
+        def finish(c):
+            whole = slice(0, CH)
+            for h in range(HALVES):
+                prod[c, h] = keep.tile([P, CH], F32, name=f"prod{c}{h}")
+            if c < CHUNKS - 1:
                 for h in range(HALVES):
-                    base_pass(0, w, h, a)
+                    gated(c, h, whole)
+                for h in range(HALVES):
+                    add_store(c, h, whole, nc.vector)
+            else:
+                gated(c, 0, whole)
+                add_store(c, 0, whole, nc.vector)
+                parts = [slice(0, CH // 2), slice(CH // 2, CH)]
+                for q in parts:
+                    gated(c, 1, q)
+                for q in parts:
+                    add_store(c, 1, q, nc.vector)
+
+        load_base_words(KEY, wk4_words)
+        load_base_scales(KEY, wk4_scales)
+        load_delta(KEY, wkd, 0)
+        load_base_words(VALUE, wv4_words)
+        gather_scales(0, CHUNKS)
+        load_delta(KEY, wkd, 1)
+        load_base_scales(VALUE, wv4_scales)
+        load_delta(VALUE, wvd, 0)
+        load_delta(VALUE, wvd, 1)
+        bias = late.tile([P, HALVES], F32, name="bias")
+        with nc.allow_non_contiguous_dma(reason="one bias value a partition"):
+            nc.sync.dma_start(bias[:], b.rearrange("(h p) -> p h", p=P))
+        for c in range(CHUNKS):
+            load_cols(st_t, st, c, "st")
+            load_cols(res_t, res, c, "res")
+
+        gather_words(0, "gw0")
+        for h in range(HALVES):
+            base_pass(0, KEY, h, 0)
         gather_words(1, "gw1")
-        quantise(0, 0)
-        quantise(0, 1)
-        delta(0, 0)
-        gather_scales(2, "gw0")
-        base(1, 0)
-        delta(1, 0)
-        base(1, 1)
-        quantise(1, 0)
-        quantise(1, 1)
-        delta(0, 1)
-        gather_scales(3, "gw1")
-        gather_words(2, "gw2")
-        delta(1, 1)
+        quantise(KEY, 0)
         for h in range(HALVES):
-            make_gate(0, h)
-        for h in range(HALVES):
-            finish(0, h)
-        gather_words(3, "gw3")
+            base_pass(0, VALUE, h, 0)
+        for w in range(2):
+            for h in range(HALVES):
+                base_pass(0, w, h, 1)
+        quantise(KEY, 1)
+        delta(0, KEY)
+        gather_words(2, "grouped01")
+        base(1, KEY)
+        base(1, VALUE)
+        quantise(VALUE, 0)
+        quantise(VALUE, 1)
+        delta(0, VALUE)
+        gather_words(3, "grouped11")
+        make_gates(0)
+        delta(1, KEY)
+        delta(1, VALUE)
+        finish(0)
         for c in range(1, CHUNKS):
             if c + 1 < CHUNKS:
-                for w in range(2):
-                    base(c + 1, w)
-                    delta(c + 1, w)
-            for h in range(HALVES):
-                make_gate(c, h)
-            for h in range(HALVES):
-                finish(c, h)
+                base(c + 1, KEY)
+                delta(c + 1, KEY)
+            make_gates(c)
+            if c + 2 < CHUNKS:
+                base(c + 1, VALUE)
+                delta(c + 1, VALUE)
+            elif c + 1 < CHUNKS:
+                for h in range(HALVES):
+                    base(c + 1, VALUE, [h])
+                    delta(c + 1, VALUE, [h])
+            finish(c)

@@ -60,10 +60,10 @@ def tile_list_engram_dl_dl_bsig_kernel(
         nc.sync.dma_start(table[:], tab_words[0].rearrange("p t i -> p (t i)").bitcast(I32))
 
         w4, raw, st_t, res_t = {}, {}, {}, {}
-        parted, codes, dscale, bank, gate, prod = {}, {}, {}, {}, {}, {}
+        picked, parted, codes, dscale, bank, gate, prod = {}, {}, {}, {}, {}, {}, {}
 
         def load_base_words(w, words):
-            w4[w] = late.tile([P, PASSES * 2 * N], U8, name=f"w4_{w}", align_bytes=64)
+            w4[w] = keep.tile([P, PASSES * 2 * N], U8, name=f"w4_{w}", align_bytes=64)
             nc.sync.dma_start(
                 w4[w][:].bitcast(I32).rearrange("p (a n) -> p a n", a=PASSES),
                 words.bitcast(I32).rearrange("a p n -> p a n"),
@@ -89,12 +89,16 @@ def tile_list_engram_dl_dl_bsig_kernel(
             nc.sync.dma_start(plane1[:, cols].bitcast(I32)[0 : P - SHIFT, :], plane0[:, cols].bitcast(I32)[SHIFT:P, :])
 
         def gather_words(c, tag):
-            gw = keep.tile([P, CH], U32, name=f"gw{c}", tag=tag, align_bytes=64)
-            nc.vector.tensor_copy(gw[:], table[:].bitcast(U32).indirect(offsets[:, c * CH // 16 : (c + 1) * CH // 16]))
+            picked[c] = keep.tile([P, CH], U32, name=f"picked{c}", tag=tag, align_bytes=64)
+            nc.vector.tensor_copy(
+                picked[c][:], table[:].bitcast(U32).indirect(offsets[:, c * CH // 16 : (c + 1) * CH // 16])
+            )
+
+        def part_words(c):
             parted[c] = keep.tile([P, PASSES * 2 * CH], U8, name=f"parted{c}", align_bytes=64)
             nc.vector.tensor_copy(
                 parted[c][:].bitcast(U16).rearrange("p (d j) -> p d j", d=PASSES),
-                gw[:].bitcast(U16).rearrange("p (j d) -> p d j", d=PASSES),
+                picked[c][:].bitcast(U16).rearrange("p (j d) -> p d j", d=PASSES),
             )
 
         def quantise(w, a):
@@ -180,42 +184,46 @@ def tile_list_engram_dl_dl_bsig_kernel(
                     add_store(c, 1, q, nc.vector)
 
         load_base_words(KEY, wk4_words)
-        load_base_scales(KEY, wk4_scales)
-        load_delta(KEY, wkd, 0)
         load_base_words(VALUE, wv4_words)
-        gather_scales(0, CHUNKS)
+        load_delta(KEY, wkd, 0)
+        load_base_scales(KEY, wk4_scales)
         load_delta(KEY, wkd, 1)
-        load_base_scales(VALUE, wv4_scales)
         load_delta(VALUE, wvd, 0)
+        gather_scales(0, CHUNKS)
+        load_base_scales(VALUE, wv4_scales)
         load_delta(VALUE, wvd, 1)
+        load_cols(st_t, st, 0, "st")
         bias = late.tile([P, HALVES], F32, name="bias")
         with nc.allow_non_contiguous_dma(reason="one bias value a partition"):
             nc.sync.dma_start(bias[:], b.rearrange("(h p) -> p h", p=P))
-        for c in range(CHUNKS):
+        load_cols(res_t, res, 0, "res")
+        for c in range(1, CHUNKS):
             load_cols(st_t, st, c, "st")
             load_cols(res_t, res, c, "res")
 
-        gather_words(0, "gw0")
+        gather_words(0, "picked0")
+        part_words(0)
         for h in range(HALVES):
             base_pass(0, KEY, h, 0)
-        gather_words(1, "gw1")
+        gather_words(1, "picked1")
         quantise(KEY, 0)
+        part_words(1)
         for h in range(HALVES):
-            base_pass(0, VALUE, h, 0)
-        for w in range(2):
-            for h in range(HALVES):
-                base_pass(0, w, h, 1)
+            base_pass(0, KEY, h, 1)
+        base(0, VALUE)
         quantise(KEY, 1)
         delta(0, KEY)
         gather_words(2, "grouped01")
-        base(1, KEY)
-        base(1, VALUE)
         quantise(VALUE, 0)
+        part_words(2)
+        base(1, KEY)
         quantise(VALUE, 1)
         delta(0, VALUE)
         gather_words(3, "grouped11")
         make_gates(0)
+        part_words(3)
         delta(1, KEY)
+        base(1, VALUE)
         delta(1, VALUE)
         finish(0)
         for c in range(1, CHUNKS):

@@ -18,12 +18,19 @@ ADD = mybir.AluOpType.add
 SIGMOID = mybir.ActivationFunctionType.Sigmoid
 
 P = 128
-PASSES = 2
-HALVES = 2
+PACK = 4
+K_PASS = P * PACK
+PASSES = K // K_PASS
+HALVES = N // P
 CH = 512
 CHUNKS = J // CH
+LAST = CHUNKS - 1
+GROUP = 16
+QUADRANT = 32
+LIVE = 4
 SHIFT = 16
 KEY, VALUE = 0, 1
+WARM_PASSES = 5
 
 
 def tile_list_engram_dl_dl_bsig_kernel(
@@ -34,11 +41,11 @@ def tile_list_engram_dl_dl_bsig_kernel(
         keep = ctx.enter_context(tc.tile_pool(name="keep", bufs=1))
         psum = ctx.enter_context(tc.psum_pool(name="psum", bufs=1))
 
-        offsets = keep.tile([P, J // 16], U16, name="offsets")
+        offsets = keep.tile([P, J // GROUP], U16, name="offsets")
         nc.sync.dma_start(offsets[:], offs)
 
         tscale = keep.tile([P, T], U8, name="tscale", align_bytes=64)
-        w4scale = [keep.tile([P, PASSES * N], U8, name=f"w4scale{w}", align_bytes=64) for w in range(2)]
+        w4scale = [keep.tile([P, PASSES * N], U8, name=f"w4scale{w}", align_bytes=64) for w in (KEY, VALUE)]
         plane0 = keep.tile([P, J], U8, name="plane0", align_bytes=64)
         plane1 = keep.tile([P, J], U8, name="plane1", align_bytes=64)
 
@@ -46,13 +53,13 @@ def tile_list_engram_dl_dl_bsig_kernel(
             warm = early.tile([P, 2], F32, name="warm")
             nc.vector.memset(warm[:, 0:1], 0.0)
             nc.vector.memset(tscale[:].bitcast(I32), 0)
-            ts_rows = tab_scales.bitcast(I32).rearrange("a (q r) t -> r q a t", r=4)
-            for r in range(4):
+            ts_rows = tab_scales.bitcast(I32).rearrange("a (q r) t -> r q a t", r=LIVE)
+            for r in range(LIVE):
                 nc.sync.dma_start(tscale[:].bitcast(I32)[r:P:SHIFT, :], ts_rows[r])
             nc.scalar.activation(warm[:, 1:2], warm[:, 0:1], SIGMOID)
         late = ctx.enter_context(tc.tile_pool(name="late", bufs=1))
 
-        for w in range(2):
+        for w in (KEY, VALUE):
             nc.vector.memset(w4scale[w][:].bitcast(I32), 0)
         nc.vector.memset(plane1[:].bitcast(I32), 0)
 
@@ -70,43 +77,45 @@ def tile_list_engram_dl_dl_bsig_kernel(
             )
 
         def load_base_scales(w, scales):
-            rows = scales.bitcast(I32).rearrange("a (q r) n -> r q a n", r=4)
+            rows = scales.bitcast(I32).rearrange("a (q r) n -> r q a n", r=LIVE)
             dst = w4scale[w][:].bitcast(I32).rearrange("p (a n) -> p a n", a=PASSES)
-            for r in range(4):
-                nc.sync.dma_start(dst[r:P:32], rows[r])
+            for r in range(LIVE):
+                nc.sync.dma_start(dst[r:P:QUADRANT], rows[r])
 
         def load_delta(w, wd, a):
-            raw[w, a] = late.tile([P, 4, N], F32, name=f"raw{w}{a}")
-            nc.sync.dma_start(raw[w, a][:], wd[a * 512 : (a + 1) * 512, :].rearrange("(p i) n -> p i n", i=4))
+            raw[w, a] = late.tile([P, PACK, N], F32, name=f"raw{w}{a}")
+            rows = wd[a * K_PASS : (a + 1) * K_PASS, :]
+            nc.sync.dma_start(raw[w, a][:], rows.rearrange("(p i) n -> p i n", i=PACK))
 
         def load_cols(dst, src, c, name):
             dst[c] = late.tile([P, HALVES, CH], F32, name=f"{name}{c}")
             nc.sync.dma_start(dst[c][:], src.rearrange("(h p) j -> p h j", p=P)[:, :, c * CH : (c + 1) * CH])
 
-        def gather_scales(c0, c1):
-            cols = slice(c0 * CH, c1 * CH)
-            nc.vector.tensor_copy(plane0[:, cols], tscale[:].indirect(offsets[:, c0 * CH // 16 : c1 * CH // 16]))
-            nc.sync.dma_start(plane1[:, cols].bitcast(I32)[0 : P - SHIFT, :], plane0[:, cols].bitcast(I32)[SHIFT:P, :])
+        def gather_scales():
+            nc.vector.tensor_copy(plane0[:], tscale[:].indirect(offsets[:]))
+            nc.sync.dma_start(plane1[:].bitcast(I32)[0 : P - SHIFT, :], plane0[:].bitcast(I32)[SHIFT:P, :])
 
         def gather_words(c, tag):
             picked[c] = keep.tile([P, CH], U32, name=f"picked{c}", tag=tag, align_bytes=64)
-            nc.vector.tensor_copy(
-                picked[c][:], table[:].bitcast(U32).indirect(offsets[:, c * CH // 16 : (c + 1) * CH // 16])
-            )
+            entries = offsets[:, c * CH // GROUP : (c + 1) * CH // GROUP]
+            nc.vector.tensor_copy(picked[c][:], table[:].bitcast(U32).indirect(entries))
 
         def part_words(c):
             parted[c] = keep.tile([P, PASSES * 2 * CH], U8, name=f"parted{c}", align_bytes=64)
-            nc.vector.tensor_copy(
-                parted[c][:].bitcast(U16).rearrange("p (d j) -> p d j", d=PASSES),
-                picked[c][:].bitcast(U16).rearrange("p (j d) -> p d j", d=PASSES),
-            )
+            dst = parted[c][:].bitcast(U16).rearrange("p (a j) -> p a j", a=PASSES)
+            src = picked[c][:].bitcast(U16).rearrange("p (j a) -> p a j", a=PASSES)
+            if c == 0:
+                for a in range(PASSES):
+                    nc.vector.tensor_copy(dst[:, a, :], src[:, a, :])
+            else:
+                nc.vector.tensor_copy(dst, src)
 
         def quantise(w, a):
-            g = keep.tile([P, 4 * N], BF16, name=f"grouped{w}{a}", tag=f"grouped{w}{a}", align_bytes=64)
-            nc.scalar.copy(g[:].rearrange("p (n i) -> p n i", i=4), raw[w, a][:].rearrange("p i n -> p n i"))
+            grouped = keep.tile([P, PACK * N], BF16, name=f"grouped{w}{a}", tag=f"grouped{w}{a}", align_bytes=64)
+            nc.scalar.copy(grouped[:].rearrange("p (n i) -> p n i", i=PACK), raw[w, a][:].rearrange("p i n -> p n i"))
             codes[w, a] = keep.tile([P, N], U32, name=f"codes{w}{a}", align_bytes=64)
             dscale[w, a] = keep.tile([P, N], U8, name=f"dscale{w}{a}", align_bytes=64)
-            nc.vector.quantize_mx(out=codes[w, a][:].bitcast(FP8X4), scales=dscale[w, a][:], in_=g[:])
+            nc.vector.quantize_mx(out=codes[w, a][:].bitcast(FP8X4), scales=dscale[w, a][:], in_=grouped[:])
 
         def moving(c, a):
             words = parted[c][:, a * 2 * CH : (a + 1) * 2 * CH].bitcast(FP4X4)
@@ -117,11 +126,11 @@ def tile_list_engram_dl_dl_bsig_kernel(
                 slot = (c % 2) * 4 + 2 * w + h
                 bank[c, w, h] = psum.tile([P, CH], F32, name=f"bank{c}{w}{h}", tag=f"bank{slot}")
             words, scale = moving(c, a)
-            c0 = a * N + h * P
+            n0 = a * N + h * P
             nc.tensor.matmul_mx(
                 out=bank[c, w, h][:],
-                lhsT=w4[w][:, 2 * c0 : 2 * (c0 + P)].bitcast(FP4X4),
-                lhsT_scale=w4scale[w][:, c0 : c0 + P],
+                lhsT=w4[w][:, 2 * n0 : 2 * (n0 + P)].bitcast(FP4X4),
+                lhsT_scale=w4scale[w][:, n0 : n0 + P],
                 rhs=words,
                 rhs_scale=scale,
                 start=(a == 0),
@@ -153,35 +162,35 @@ def tile_list_engram_dl_dl_bsig_kernel(
         def make_gates(c):
             for h in range(HALVES):
                 pre = keep.tile([P, CH], F32, name=f"pre{c}{h}", tag=f"pre{c}{h}", align_bytes=64)
-                nc.vector.tensor_tensor(pre[:], bank[c, KEY, h][:], st_t[c][:, h, :], MULT)
+                nc.vector.tensor_tensor(pre[:], st_t[c][:, h, :], bank[c, KEY, h][:], MULT)
                 gate[c, h] = keep.tile([P, CH], F32, name=f"gate{c}{h}")
                 nc.scalar.activation(gate[c, h][:], pre[:], SIGMOID, bias=bias[:, h : h + 1])
 
-        def gated(c, h, q):
-            nc.vector.tensor_tensor(prod[c, h][:, q], bank[c, VALUE, h][:, q], gate[c, h][:, q], MULT)
+        def gated(c, h, cols):
+            nc.vector.tensor_tensor(prod[c, h][:, cols], gate[c, h][:, cols], bank[c, VALUE, h][:, cols], MULT)
 
-        def add_store(c, h, q, eng):
-            o = keep.tile([P, q.stop - q.start], F32, name=f"o{c}{h}{q.start}")
-            eng.tensor_tensor(o[:], prod[c, h][:, q], res_t[c][:, h, q], ADD)
-            nc.sync.dma_start(out[h * P : (h + 1) * P, c * CH + q.start : c * CH + q.stop], o[:])
+        def add_store(c, h, cols, engine):
+            total = keep.tile([P, cols.stop - cols.start], F32, name=f"o{c}{h}{cols.start}")
+            engine.tensor_tensor(total[:], prod[c, h][:, cols], res_t[c][:, h, cols], ADD)
+            nc.sync.dma_start(out[h * P : (h + 1) * P, c * CH + cols.start : c * CH + cols.stop], total[:])
 
         def finish(c):
             whole = slice(0, CH)
             for h in range(HALVES):
                 prod[c, h] = keep.tile([P, CH], F32, name=f"prod{c}{h}")
-            if c < CHUNKS - 1:
+            if c < LAST:
                 for h in range(HALVES):
                     gated(c, h, whole)
                 for h in range(HALVES):
-                    add_store(c, h, whole, nc.vector)
+                    add_store(c, h, whole, nc.gpsimd)
             else:
                 gated(c, 0, whole)
                 add_store(c, 0, whole, nc.vector)
                 parts = [slice(0, CH // 2), slice(CH // 2, CH)]
-                for q in parts:
-                    gated(c, 1, q)
-                for q in parts:
-                    add_store(c, 1, q, nc.vector)
+                for cols in parts:
+                    gated(c, 1, cols)
+                for cols in parts:
+                    add_store(c, 1, cols, nc.vector)
 
         load_base_words(KEY, wk4_words)
         load_base_words(VALUE, wv4_words)
@@ -189,7 +198,7 @@ def tile_list_engram_dl_dl_bsig_kernel(
         load_base_scales(KEY, wk4_scales)
         load_delta(KEY, wkd, 1)
         load_delta(VALUE, wvd, 0)
-        gather_scales(0, CHUNKS)
+        gather_scales()
         load_base_scales(VALUE, wv4_scales)
         load_delta(VALUE, wvd, 1)
         load_cols(st_t, st, 0, "st")
@@ -200,6 +209,18 @@ def tile_list_engram_dl_dl_bsig_kernel(
         for c in range(1, CHUNKS):
             load_cols(st_t, st, c, "st")
             load_cols(res_t, res, c, "res")
+
+        spare = psum.tile([P, CH], F32, name="spare", tag="bank7")
+        for i in range(WARM_PASSES):
+            nc.tensor.matmul_mx(
+                out=spare[:],
+                lhsT=w4[KEY][:, 0 : 2 * P].bitcast(FP4X4),
+                lhsT_scale=plane0[:, 0:P],
+                rhs=w4[KEY][:].bitcast(FP4X4),
+                rhs_scale=plane0[:, 0:CH],
+                start=True,
+                stop=True,
+            )
 
         gather_words(0, "picked0")
         part_words(0)
@@ -213,29 +234,30 @@ def tile_list_engram_dl_dl_bsig_kernel(
         base(0, VALUE)
         quantise(KEY, 1)
         delta(0, KEY)
-        gather_words(2, "grouped01")
+        gather_words(2, f"grouped{KEY}1")
         quantise(VALUE, 0)
         part_words(2)
         base(1, KEY)
         quantise(VALUE, 1)
         delta(0, VALUE)
-        gather_words(3, "grouped11")
+        gather_words(3, f"grouped{VALUE}1")
         make_gates(0)
         part_words(3)
         delta(1, KEY)
         base(1, VALUE)
         delta(1, VALUE)
         finish(0)
+
         for c in range(1, CHUNKS):
-            if c + 1 < CHUNKS:
+            if c < LAST:
                 base(c + 1, KEY)
                 delta(c + 1, KEY)
             make_gates(c)
-            if c + 2 < CHUNKS:
+            if c + 1 < LAST:
                 base(c + 1, VALUE)
                 delta(c + 1, VALUE)
-            elif c + 1 < CHUNKS:
+            elif c + 1 == LAST:
                 for h in range(HALVES):
-                    base(c + 1, VALUE, [h])
-                    delta(c + 1, VALUE, [h])
+                    base(LAST, VALUE, [h])
+                    delta(LAST, VALUE, [h])
             finish(c)

@@ -24,13 +24,13 @@ PASSES = K // K_PASS
 HALVES = N // P
 CH = 512
 CHUNKS = J // CH
-LAST = CHUNKS - 1
+PAIR = 2 * CH
 GROUP = 16
 QUADRANT = 32
+QUADS = P // QUADRANT
 LIVE = 4
-SHIFT = 16
+ROWS0 = P - QUADRANT
 KEY, VALUE = 0, 1
-WARM_PASSES = 5
 
 
 def tile_list_engram_dl_dl_bsig_kernel(
@@ -41,62 +41,38 @@ def tile_list_engram_dl_dl_bsig_kernel(
         keep = ctx.enter_context(tc.tile_pool(name="keep", bufs=1))
         psum = ctx.enter_context(tc.psum_pool(name="psum", bufs=1))
 
+        def compact(scales):
+            return scales.bitcast(I32).rearrange("a q n -> q a n")
+
+        def spread(planes, rows):
+            dst = planes[:].bitcast(I32).rearrange("p (a n) -> p a n", a=PASSES)
+            src = rows[:].bitcast(I32)
+            for q in range(QUADS):
+                first = ROWS0 + q * LIVE * PASSES
+                nc.sync.dma_start(dst[q * QUADRANT : q * QUADRANT + LIVE], src[first : first + LIVE * PASSES, :])
+
         offsets = keep.tile([P, J // GROUP], U16, name="offsets")
-        nc.sync.dma_start(offsets[:], offs)
+        table = keep.tile([P, T], I32, name="table", align_bytes=64)
+        first_w = PAIR + 2 * N
+        stage = keep.tile([P, first_w], U8, name="stage", align_bytes=64)
+        planes = keep.tile([P, PASSES * first_w], U8, name="planes", align_bytes=64)
+        later_planes = {c: keep.tile([P, PASSES * CH], U8, name=f"planes{c}", align_bytes=64) for c in (2, 3)}
+        w4 = [keep.tile([P, PASSES * 2 * N], U8, name=f"w4_{w}", align_bytes=64) for w in (KEY, VALUE)]
 
-        tscale = keep.tile([P, T], U8, name="tscale", align_bytes=64)
-        w4scale = [keep.tile([P, PASSES * N], U8, name=f"w4scale{w}", align_bytes=64) for w in (KEY, VALUE)]
-        plane0 = keep.tile([P, J], U8, name="plane0", align_bytes=64)
-        plane1 = keep.tile([P, J], U8, name="plane1", align_bytes=64)
-
-        with tc.tile_pool(name="early", bufs=1) as early:
-            warm = early.tile([P, 2], F32, name="warm")
-            nc.vector.memset(warm[:, 0:1], 0.0)
-            nc.vector.memset(tscale[:].bitcast(I32), 0)
-            ts_rows = tab_scales.bitcast(I32).rearrange("a (q r) t -> r q a t", r=LIVE)
-            for r in range(LIVE):
-                nc.sync.dma_start(tscale[:].bitcast(I32)[r:P:SHIFT, :], ts_rows[r])
-            nc.scalar.activation(warm[:, 1:2], warm[:, 0:1], SIGMOID)
-        late = ctx.enter_context(tc.tile_pool(name="late", bufs=1))
-
-        for w in (KEY, VALUE):
-            nc.vector.memset(w4scale[w][:].bitcast(I32), 0)
-        nc.vector.memset(plane1[:].bitcast(I32), 0)
-
-        table = late.tile([P, T], I32, name="table", align_bytes=64)
-        nc.sync.dma_start(table[:], tab_words[0].rearrange("p t i -> p (t i)").bitcast(I32))
-
-        w4, raw, st_t, res_t = {}, {}, {}, {}
+        raw, st_t, res_t = {}, {}, {}
         picked, parted, codes, dscale, bank, gate, prod = {}, {}, {}, {}, {}, {}, {}
 
-        def load_base_words(w, words):
-            w4[w] = keep.tile([P, PASSES * 2 * N], U8, name=f"w4_{w}", align_bytes=64)
-            nc.sync.dma_start(
-                w4[w][:].bitcast(I32).rearrange("p (a n) -> p a n", a=PASSES),
-                words.bitcast(I32).rearrange("a p n -> p a n"),
-            )
-
-        def load_base_scales(w, scales):
-            rows = scales.bitcast(I32).rearrange("a (q r) n -> r q a n", r=LIVE)
-            dst = w4scale[w][:].bitcast(I32).rearrange("p (a n) -> p a n", a=PASSES)
-            for r in range(LIVE):
-                nc.sync.dma_start(dst[r:P:QUADRANT], rows[r])
-
-        def load_delta(w, wd, a):
-            raw[w, a] = late.tile([P, PACK, N], F32, name=f"raw{w}{a}")
+        def load_delta(pool, w, wd, a):
+            raw[w, a] = pool.tile([P, PACK, N], F32, name=f"raw{w}{a}")
             rows = wd[a * K_PASS : (a + 1) * K_PASS, :]
             nc.sync.dma_start(raw[w, a][:], rows.rearrange("(p i) n -> p i n", i=PACK))
 
-        def load_cols(dst, src, c, name):
-            dst[c] = late.tile([P, HALVES, CH], F32, name=f"{name}{c}")
-            nc.sync.dma_start(dst[c][:], src.rearrange("(h p) j -> p h j", p=P)[:, :, c * CH : (c + 1) * CH])
+        def load_rows(pool, dst, src, g, name):
+            dst[g] = pool.tile([P, HALVES, PAIR], F32, name=f"{name}{g}")
+            nc.sync.dma_start(dst[g][:], src.rearrange("(h p) j -> p h j", p=P)[:, :, g * PAIR : (g + 1) * PAIR])
 
-        def gather_scales():
-            nc.vector.tensor_copy(plane0[:], tscale[:].indirect(offsets[:]))
-            nc.sync.dma_start(plane1[:].bitcast(I32)[0 : P - SHIFT, :], plane0[:].bitcast(I32)[SHIFT:P, :])
-
-        def gather_words(c, tag):
-            picked[c] = keep.tile([P, CH], U32, name=f"picked{c}", tag=tag, align_bytes=64)
+        def gather_words(c, pool, tag):
+            picked[c] = pool.tile([P, CH], U32, name=f"picked{c}", tag=tag, align_bytes=64)
             entries = offsets[:, c * CH // GROUP : (c + 1) * CH // GROUP]
             nc.vector.tensor_copy(picked[c][:], table[:].bitcast(U32).indirect(entries))
 
@@ -119,18 +95,21 @@ def tile_list_engram_dl_dl_bsig_kernel(
 
         def moving(c, a):
             words = parted[c][:, a * 2 * CH : (a + 1) * 2 * CH].bitcast(FP4X4)
-            return words, (plane0, plane1)[a][:, c * CH : (c + 1) * CH]
+            if c < 2:
+                return words, planes[:, a * first_w + c * CH : a * first_w + (c + 1) * CH]
+            return words, later_planes[c][:, a * CH : (a + 1) * CH]
 
         def base_pass(c, w, h, a):
             if a == 0:
-                slot = (c % 2) * 4 + 2 * w + h
+                slot = (2 * w + c if c < 2 else 2 * (c - 2) + w) * HALVES + h
                 bank[c, w, h] = psum.tile([P, CH], F32, name=f"bank{c}{w}{h}", tag=f"bank{slot}")
             words, scale = moving(c, a)
             n0 = a * N + h * P
+            s0 = a * first_w + PAIR + w * N + h * P
             nc.tensor.matmul_mx(
                 out=bank[c, w, h][:],
                 lhsT=w4[w][:, 2 * n0 : 2 * (n0 + P)].bitcast(FP4X4),
-                lhsT_scale=w4scale[w][:, n0 : n0 + P],
+                lhsT_scale=planes[:, s0 : s0 + P],
                 rhs=words,
                 rhs_scale=scale,
                 start=(a == 0),
@@ -149,40 +128,131 @@ def tile_list_engram_dl_dl_bsig_kernel(
                 stop=(a == PASSES - 1),
             )
 
-        def base(c, w, halves=range(HALVES)):
-            for h in halves:
-                for a in range(PASSES):
-                    base_pass(c, w, h, a)
-
-        def delta(c, w, halves=range(HALVES)):
-            for h in halves:
-                for a in range(PASSES):
-                    delta_pass(c, w, h, a)
+        def cols_of(c):
+            return slice((c % 2) * CH, (c % 2 + 1) * CH)
 
         def make_gates(c):
             for h in range(HALVES):
-                pre = keep.tile([P, CH], F32, name=f"pre{c}{h}", tag=f"pre{c}{h}", align_bytes=64)
-                nc.vector.tensor_tensor(pre[:], st_t[c][:, h, :], bank[c, KEY, h][:], MULT)
-                gate[c, h] = keep.tile([P, CH], F32, name=f"gate{c}{h}")
+                tag = f"gate2{h}" if c == CHUNKS - 1 else f"pre{c}{h}"
+                pre = keep.tile([P, CH], F32, name=f"pre{c}{h}", tag=tag, align_bytes=64)
+                nc.vector.tensor_tensor(pre[:], st_t[c // 2][:, h, cols_of(c)], bank[c, KEY, h][:], MULT)
+                gate[c, h] = keep.tile([P, CH], F32, name=f"gate{c}{h}", tag=f"gate{c}{h}", align_bytes=64)
                 nc.scalar.activation(gate[c, h][:], pre[:], SIGMOID, bias=bias[:, h : h + 1])
 
         def gated(c, h, cols):
+            if cols.start == 0:
+                tag = "prod21" if (c, h) == (CHUNKS - 1, 0) else f"prod{c}{h}"
+                prod[c, h] = keep.tile([P, CH], F32, name=f"prod{c}{h}", tag=tag)
             nc.vector.tensor_tensor(prod[c, h][:, cols], gate[c, h][:, cols], bank[c, VALUE, h][:, cols], MULT)
 
         def add_store(c, h, cols, engine):
             total = keep.tile([P, cols.stop - cols.start], F32, name=f"o{c}{h}{cols.start}")
-            engine.tensor_tensor(total[:], prod[c, h][:, cols], res_t[c][:, h, cols], ADD)
+            j0 = (c % 2) * CH
+            engine.tensor_tensor(total[:], prod[c, h][:, cols], res_t[1][:, h, j0 + cols.start : j0 + cols.stop], ADD)
             nc.sync.dma_start(out[h * P : (h + 1) * P, c * CH + cols.start : c * CH + cols.stop], total[:])
 
-        def finish(c):
-            whole = slice(0, CH)
+        def gather_rows(c, pool, tag):
+            rows = pool.tile([P, CH], U8, name=f"rows{c}", tag=tag, align_bytes=64)
+            nc.vector.tensor_copy(rows[:], srows[:].indirect(offsets[:, c * CH // GROUP : (c + 1) * CH // GROUP]))
+            spread(later_planes[c], rows)
+
+        def first_steps():
+            gather_words(0, keep, "picked")
+            part_words(0)
+            for a in range(PASSES):
+                for w in (KEY, VALUE):
+                    for h in range(HALVES):
+                        base_pass(0, w, h, a)
+            gather_words(1, keep, "picked")
+            part_words(1)
+            for w in (KEY, VALUE):
+                for h in range(HALVES):
+                    for a in range(PASSES):
+                        base_pass(1, w, h, a)
+            quantise(KEY, 0)
+            gather_words(2, keep, f"grouped{KEY}0")
+            quantise(KEY, 1)
+            part_words(2)
+            quantise(VALUE, 0)
+
+        with tc.tile_pool(name="window", bufs=1, side="right") as window:
+            srows = window.tile([P, T], U8, name="srows", align_bytes=64)
+            nc.sync.dma_start(srows[:].bitcast(I32)[ROWS0:P, :], compact(tab_scales))
+            nc.sync.dma_start(offsets[:], offs)
+            nc.sync.dma_start(table[:], tab_words[0].rearrange("p t i -> p (t i)").bitcast(I32))
+            for w, scales in ((KEY, wk4_scales), (VALUE, wv4_scales)):
+                cols = slice((PAIR + w * N) // 4, (PAIR + (w + 1) * N) // 4)
+                nc.scalar.dma_start(stage[:].bitcast(I32)[ROWS0:P, cols], compact(scales))
+            for w, words in ((KEY, wk4_words), (VALUE, wv4_words)):
+                nc.sync.dma_start(
+                    w4[w][:].bitcast(I32).rearrange("p (a n) -> p a n", a=PASSES),
+                    words.bitcast(I32).rearrange("a p n -> p a n"),
+                )
+            warm = keep.tile([P, 2], F32, name="warm")
+            nc.gpsimd.memset(warm[:, 0:1], 0.0)
+            nc.scalar.activation(warm[:, 1:2], warm[:, 0:1], SIGMOID)
+            nc.vector.memset(srows[:].bitcast(I32)[0:ROWS0, :], 0)
+            nc.vector.memset(planes[:].bitcast(I32), 0)
+            for c in (2, 3):
+                nc.gpsimd.memset(later_planes[c][:].bitcast(I32), 0)
+
+            with tc.tile_pool(name="early", bufs=1) as early:
+                picked_rows0 = early.tile([P, PAIR], U8, name="picked_rows0", align_bytes=64)
+                nc.vector.tensor_copy(picked_rows0[:], srows[:].indirect(offsets[:, 0 : PAIR // GROUP]))
+                nc.vector.tensor_copy(
+                    stage[:].bitcast(I32)[ROWS0:P, 0 : PAIR // 4], picked_rows0[:].bitcast(I32)[ROWS0:P, :]
+                )
+            spread(planes, stage)
+            late1 = ctx.enter_context(tc.tile_pool(name="late1", bufs=1))
+            for w, wd in ((KEY, wkd), (VALUE, wvd)):
+                for a in range(PASSES):
+                    load_delta(late1, w, wd, a)
+            load_rows(late1, st_t, st, 0, "st")
+            gather_rows(2, late1, "rows2")
+            bias = late1.tile([P, HALVES], F32, name="bias")
+            with nc.allow_non_contiguous_dma(reason="one bias value a partition"):
+                nc.sync.dma_start(bias[:], b.rearrange("(h p) -> p h", p=P))
+            load_rows(late1, res_t, res, 0, "res")
+            first_steps()
+            gather_rows(3, keep, f"grouped{VALUE}0")
+        late2 = ctx.enter_context(tc.tile_pool(name="late2", bufs=1, side="right"))
+        for dst, src, name in ((st_t, st, "st"), (res_t, res, "res")):
+            load_rows(late2, dst, src, 1, name)
+
+        whole = slice(0, CH)
+
+        quantise(VALUE, 1)
+        for w in (KEY, VALUE):
+            for c in range(2):
+                for h in range(HALVES):
+                    for a in range(PASSES):
+                        delta_pass(c, w, h, a)
+        for c in range(2):
+            make_gates(c)
+        gather_words(3, keep, "pre01")
+        part_words(3)
+        first_out = [keep.tile([P, PAIR], F32, name=f"first_out{h}") for h in range(HALVES)]
+        for c in range(2):
             for h in range(HALVES):
-                prod[c, h] = keep.tile([P, CH], F32, name=f"prod{c}{h}")
-            if c < LAST:
+                gated(c, h, whole)
+                nc.gpsimd.tensor_tensor(first_out[h][:, cols_of(c)], prod[c, h][:], res_t[0][:, h, cols_of(c)], ADD)
+        for h in range(HALVES):
+            nc.sync.dma_start(out[h * P : (h + 1) * P, 0:PAIR], first_out[h][:])
+
+        for c in range(2, CHUNKS):
+            for w in (KEY, VALUE):
+                for h in range(HALVES):
+                    for a in range(PASSES):
+                        base_pass(c, w, h, a)
+                    for a in range(PASSES):
+                        delta_pass(c, w, h, a)
+                if w == KEY:
+                    make_gates(c)
+            if c < CHUNKS - 1:
                 for h in range(HALVES):
                     gated(c, h, whole)
                 for h in range(HALVES):
-                    add_store(c, h, whole, nc.gpsimd)
+                    add_store(c, h, whole, nc.gpsimd if h == 0 else nc.vector)
             else:
                 gated(c, 0, whole)
                 add_store(c, 0, whole, nc.vector)
@@ -191,73 +261,3 @@ def tile_list_engram_dl_dl_bsig_kernel(
                     gated(c, 1, cols)
                 for cols in parts:
                     add_store(c, 1, cols, nc.vector)
-
-        load_base_words(KEY, wk4_words)
-        load_base_words(VALUE, wv4_words)
-        load_delta(KEY, wkd, 0)
-        load_base_scales(KEY, wk4_scales)
-        load_delta(KEY, wkd, 1)
-        load_delta(VALUE, wvd, 0)
-        gather_scales()
-        load_base_scales(VALUE, wv4_scales)
-        load_delta(VALUE, wvd, 1)
-        load_cols(st_t, st, 0, "st")
-        bias = late.tile([P, HALVES], F32, name="bias")
-        with nc.allow_non_contiguous_dma(reason="one bias value a partition"):
-            nc.sync.dma_start(bias[:], b.rearrange("(h p) -> p h", p=P))
-        load_cols(res_t, res, 0, "res")
-        for c in range(1, CHUNKS):
-            load_cols(st_t, st, c, "st")
-            load_cols(res_t, res, c, "res")
-
-        spare = psum.tile([P, CH], F32, name="spare", tag="bank7")
-        for i in range(WARM_PASSES):
-            nc.tensor.matmul_mx(
-                out=spare[:],
-                lhsT=w4[KEY][:, 0 : 2 * P].bitcast(FP4X4),
-                lhsT_scale=plane0[:, 0:P],
-                rhs=w4[KEY][:].bitcast(FP4X4),
-                rhs_scale=plane0[:, 0:CH],
-                start=True,
-                stop=True,
-            )
-
-        gather_words(0, "picked0")
-        part_words(0)
-        for h in range(HALVES):
-            base_pass(0, KEY, h, 0)
-        gather_words(1, "picked1")
-        quantise(KEY, 0)
-        part_words(1)
-        for h in range(HALVES):
-            base_pass(0, KEY, h, 1)
-        base(0, VALUE)
-        quantise(KEY, 1)
-        delta(0, KEY)
-        gather_words(2, f"grouped{KEY}1")
-        quantise(VALUE, 0)
-        part_words(2)
-        base(1, KEY)
-        quantise(VALUE, 1)
-        delta(0, VALUE)
-        gather_words(3, f"grouped{VALUE}1")
-        make_gates(0)
-        part_words(3)
-        delta(1, KEY)
-        base(1, VALUE)
-        delta(1, VALUE)
-        finish(0)
-
-        for c in range(1, CHUNKS):
-            if c < LAST:
-                base(c + 1, KEY)
-                delta(c + 1, KEY)
-            make_gates(c)
-            if c + 1 < LAST:
-                base(c + 1, VALUE)
-                delta(c + 1, VALUE)
-            elif c + 1 == LAST:
-                for h in range(HALVES):
-                    base(LAST, VALUE, [h])
-                    delta(LAST, VALUE, [h])
-            finish(c)

@@ -31,6 +31,7 @@ QUADS = P // QUADRANT
 LIVE = 4
 ROWS0 = P - QUADRANT
 KEY, VALUE = 0, 1
+WARM_PASSES = 6
 
 
 def tile_list_engram_dl_dl_bsig_kernel(
@@ -199,10 +200,19 @@ def tile_list_engram_dl_dl_bsig_kernel(
             with tc.tile_pool(name="early", bufs=1) as early:
                 picked_rows0 = early.tile([P, PAIR], U8, name="picked_rows0", align_bytes=64)
                 nc.vector.tensor_copy(picked_rows0[:], srows[:].indirect(offsets[:, 0 : PAIR // GROUP]))
-                nc.vector.tensor_copy(
-                    stage[:].bitcast(I32)[ROWS0:P, 0 : PAIR // 4], picked_rows0[:].bitcast(I32)[ROWS0:P, :]
-                )
+                nc.vector.tensor_copy(stage[:].bitcast(I32)[:, 0 : PAIR // 4], picked_rows0[:].bitcast(I32))
             spread(planes, stage)
+            spare = psum.tile([P, CH], F32, name="spare", tag="bank7")
+            for i in range(WARM_PASSES):
+                nc.tensor.matmul_mx(
+                    out=spare[:],
+                    lhsT=stage[:, 0 : 2 * P].bitcast(FP4X4),
+                    lhsT_scale=stage[:, 0:P],
+                    rhs=stage[:, 0 : 2 * CH].bitcast(FP4X4),
+                    rhs_scale=stage[:, 0:CH],
+                    start=True,
+                    stop=True,
+                )
             late1 = ctx.enter_context(tc.tile_pool(name="late1", bufs=1))
             for w, wd in ((KEY, wkd), (VALUE, wvd)):
                 for a in range(PASSES):

@@ -48,7 +48,7 @@ def tile_list_engram_dl_dl_bsig_kernel(
         def spread(planes, rows):
             dst = planes[:].bitcast(I32).rearrange("p (a n) -> p a n", a=PASSES)
             src = rows[:].bitcast(I32)
-            for q in range(QUADS):
+            for q in (0, 2, 1, 3):
                 first = ROWS0 + q * LIVE * PASSES
                 nc.sync.dma_start(dst[q * QUADRANT : q * QUADRANT + LIVE], src[first : first + LIVE * PASSES, :])
 
@@ -57,14 +57,15 @@ def tile_list_engram_dl_dl_bsig_kernel(
         first_w = PAIR + 2 * N
         stage = keep.tile([P, first_w], U8, name="stage", align_bytes=64)
         planes = keep.tile([P, PASSES * first_w], U8, name="planes", align_bytes=64)
-        later_planes = {c: keep.tile([P, PASSES * CH], U8, name=f"planes{c}", align_bytes=64) for c in (2, 3)}
+        planes23 = keep.tile([P, PASSES * PAIR], U8, name="planes23", align_bytes=64)
+        rows23 = keep.tile([P, PAIR], U8, name="rows23", align_bytes=64)
         w4 = [keep.tile([P, PASSES * 2 * N], U8, name=f"w4_{w}", align_bytes=64) for w in (KEY, VALUE)]
 
         raw, st_t, res_t = {}, {}, {}
         picked, parted, codes, dscale, bank, gate, prod = {}, {}, {}, {}, {}, {}, {}
 
         def load_delta(pool, w, wd, a):
-            raw[w, a] = pool.tile([P, PACK, N], F32, name=f"raw{w}{a}")
+            raw[w, a] = pool.tile([P, PACK, N], F32, name=f"raw{w}{a}", tag=f"raw{w}{a}", align_bytes=64)
             rows = wd[a * K_PASS : (a + 1) * K_PASS, :]
             nc.sync.dma_start(raw[w, a][:], rows.rearrange("(p i) n -> p i n", i=PACK))
 
@@ -78,7 +79,8 @@ def tile_list_engram_dl_dl_bsig_kernel(
             nc.vector.tensor_copy(picked[c][:], table[:].bitcast(U32).indirect(entries))
 
         def part_words(c):
-            parted[c] = keep.tile([P, PASSES * 2 * CH], U8, name=f"parted{c}", align_bytes=64)
+            tag = f"grouped{KEY}1" if c == 2 else f"parted{c}"
+            parted[c] = keep.tile([P, PASSES * 2 * CH], U8, name=f"parted{c}", tag=tag, align_bytes=64)
             dst = parted[c][:].bitcast(U16).rearrange("p (a j) -> p a j", a=PASSES)
             src = picked[c][:].bitcast(U16).rearrange("p (j a) -> p a j", a=PASSES)
             if c == 0:
@@ -89,7 +91,10 @@ def tile_list_engram_dl_dl_bsig_kernel(
 
         def quantise(w, a):
             grouped = keep.tile([P, PACK * N], BF16, name=f"grouped{w}{a}", tag=f"grouped{w}{a}", align_bytes=64)
-            nc.scalar.copy(grouped[:].rearrange("p (n i) -> p n i", i=PACK), raw[w, a][:].rearrange("p i n -> p n i"))
+            nc.scalar.copy(
+                grouped[:].rearrange("p (m u i) -> p m i u", u=4, i=PACK),
+                raw[w, a][:].rearrange("p i (m u) -> p m i u", u=4),
+            )
             codes[w, a] = keep.tile([P, N], U32, name=f"codes{w}{a}", align_bytes=64)
             dscale[w, a] = keep.tile([P, N], U8, name=f"dscale{w}{a}", align_bytes=64)
             nc.vector.quantize_mx(out=codes[w, a][:].bitcast(FP8X4), scales=dscale[w, a][:], in_=grouped[:])
@@ -98,7 +103,7 @@ def tile_list_engram_dl_dl_bsig_kernel(
             words = parted[c][:, a * 2 * CH : (a + 1) * 2 * CH].bitcast(FP4X4)
             if c < 2:
                 return words, planes[:, a * first_w + c * CH : a * first_w + (c + 1) * CH]
-            return words, later_planes[c][:, a * CH : (a + 1) * CH]
+            return words, planes23[:, a * PAIR + (c - 2) * CH : a * PAIR + (c - 1) * CH]
 
         def base_pass(c, w, h, a):
             if a == 0:
@@ -142,20 +147,14 @@ def tile_list_engram_dl_dl_bsig_kernel(
 
         def gated(c, h, cols):
             if cols.start == 0:
-                tag = "prod21" if (c, h) == (CHUNKS - 1, 0) else f"prod{c}{h}"
-                prod[c, h] = keep.tile([P, CH], F32, name=f"prod{c}{h}", tag=tag)
+                prod[c, h] = keep.tile([P, CH], F32, name=f"prod{c}{h}")
             nc.vector.tensor_tensor(prod[c, h][:, cols], gate[c, h][:, cols], bank[c, VALUE, h][:, cols], MULT)
 
         def add_store(c, h, cols, engine):
             total = keep.tile([P, cols.stop - cols.start], F32, name=f"o{c}{h}{cols.start}")
             j0 = (c % 2) * CH
-            engine.tensor_tensor(total[:], prod[c, h][:, cols], res_t[1][:, h, j0 + cols.start : j0 + cols.stop], ADD)
+            engine.tensor_tensor(total[:], prod[c, h][:, cols], res_t[c // 2][:, h, j0 + cols.start : j0 + cols.stop], ADD)
             nc.sync.dma_start(out[h * P : (h + 1) * P, c * CH + cols.start : c * CH + cols.stop], total[:])
-
-        def gather_rows(c, pool, tag):
-            rows = pool.tile([P, CH], U8, name=f"rows{c}", tag=tag, align_bytes=64)
-            nc.vector.tensor_copy(rows[:], srows[:].indirect(offsets[:, c * CH // GROUP : (c + 1) * CH // GROUP]))
-            spread(later_planes[c], rows)
 
         def first_steps():
             gather_words(0, keep, "picked")
@@ -173,7 +172,9 @@ def tile_list_engram_dl_dl_bsig_kernel(
             quantise(KEY, 0)
             gather_words(2, keep, f"grouped{KEY}0")
             quantise(KEY, 1)
+            gather_words(3, late1, f"raw{KEY}1")
             part_words(2)
+            part_words(3)
             quantise(VALUE, 0)
 
         with tc.tile_pool(name="window", bufs=1, side="right") as window:
@@ -194,8 +195,7 @@ def tile_list_engram_dl_dl_bsig_kernel(
             nc.scalar.activation(warm[:, 1:2], warm[:, 0:1], SIGMOID)
             nc.vector.memset(srows[:].bitcast(I32)[0:ROWS0, :], 0)
             nc.vector.memset(planes[:].bitcast(I32), 0)
-            for c in (2, 3):
-                nc.gpsimd.memset(later_planes[c][:].bitcast(I32), 0)
+            nc.gpsimd.memset(planes23[:].bitcast(I32), 0)
 
             with tc.tile_pool(name="early", bufs=1) as early:
                 picked_rows0 = early.tile([P, PAIR], U8, name="picked_rows0", align_bytes=64)
@@ -218,16 +218,17 @@ def tile_list_engram_dl_dl_bsig_kernel(
                 for a in range(PASSES):
                     load_delta(late1, w, wd, a)
             load_rows(late1, st_t, st, 0, "st")
-            gather_rows(2, late1, "rows2")
+            for c in (2, 3):
+                entries = offsets[:, c * CH // GROUP : (c + 1) * CH // GROUP]
+                nc.vector.tensor_copy(rows23[:, cols_of(c)], srows[:].indirect(entries))
+            spread(planes23, rows23)
             bias = late1.tile([P, HALVES], F32, name="bias")
             with nc.allow_non_contiguous_dma(reason="one bias value a partition"):
                 nc.sync.dma_start(bias[:], b.rearrange("(h p) -> p h", p=P))
             load_rows(late1, res_t, res, 0, "res")
-            first_steps()
-            gather_rows(3, keep, f"grouped{VALUE}0")
-        late2 = ctx.enter_context(tc.tile_pool(name="late2", bufs=1, side="right"))
-        for dst, src, name in ((st_t, st, "st"), (res_t, res, "res")):
-            load_rows(late2, dst, src, 1, name)
+            for dst, src, name in ((st_t, st, "st"), (res_t, res, "res")):
+                load_rows(late1, dst, src, 1, name)
+        first_steps()
 
         whole = slice(0, CH)
 
@@ -239,15 +240,10 @@ def tile_list_engram_dl_dl_bsig_kernel(
                         delta_pass(c, w, h, a)
         for c in range(2):
             make_gates(c)
-        gather_words(3, keep, "pre01")
-        part_words(3)
-        first_out = [keep.tile([P, PAIR], F32, name=f"first_out{h}") for h in range(HALVES)]
         for c in range(2):
             for h in range(HALVES):
                 gated(c, h, whole)
-                nc.gpsimd.tensor_tensor(first_out[h][:, cols_of(c)], prod[c, h][:], res_t[0][:, h, cols_of(c)], ADD)
-        for h in range(HALVES):
-            nc.sync.dma_start(out[h * P : (h + 1) * P, 0:PAIR], first_out[h][:])
+                add_store(c, h, whole, nc.gpsimd)
 
         for c in range(2, CHUNKS):
             for w in (KEY, VALUE):
@@ -262,7 +258,7 @@ def tile_list_engram_dl_dl_bsig_kernel(
                 for h in range(HALVES):
                     gated(c, h, whole)
                 for h in range(HALVES):
-                    add_store(c, h, whole, nc.gpsimd if h == 0 else nc.vector)
+                    add_store(c, h, whole, nc.gpsimd)
             else:
                 gated(c, 0, whole)
                 add_store(c, 0, whole, nc.vector)

@@ -59,7 +59,14 @@ def tile_list_engram_dl_dl_bsig_kernel(
         planes = keep.tile([P, PASSES * first_w], U8, name="planes", align_bytes=64)
         planes23 = keep.tile([P, PASSES * PAIR], U8, name="planes23", align_bytes=64)
         rows23 = keep.tile([P, PAIR], U8, name="rows23", align_bytes=64)
-        w4 = [keep.tile([P, PASSES * 2 * N], U8, name=f"w4_{w}", align_bytes=64) for w in (KEY, VALUE)]
+        w4 = {}
+
+        def load_base(pool, w, words):
+            w4[w] = pool.tile([P, PASSES * 2 * N], U8, name=f"w4_{w}", align_bytes=64)
+            nc.sync.dma_start(
+                w4[w][:].bitcast(I32).rearrange("p (a n) -> p a n", a=PASSES),
+                words.bitcast(I32).rearrange("a p n -> p a n"),
+            )
 
         raw, st_t, res_t = {}, {}, {}
         picked, parted, codes, dscale, bank, gate, prod = {}, {}, {}, {}, {}, {}, {}
@@ -79,7 +86,7 @@ def tile_list_engram_dl_dl_bsig_kernel(
             nc.vector.tensor_copy(picked[c][:], table[:].bitcast(U32).indirect(entries))
 
         def part_words(c):
-            tag = f"grouped{KEY}1" if c == 2 else f"parted{c}"
+            tag = f"grouped{c - 2}1" if c >= 2 else f"parted{c}"
             parted[c] = keep.tile([P, PASSES * 2 * CH], U8, name=f"parted{c}", tag=tag, align_bytes=64)
             dst = parted[c][:].bitcast(U16).rearrange("p (a j) -> p a j", a=PASSES)
             src = picked[c][:].bitcast(U16).rearrange("p (j a) -> p a j", a=PASSES)
@@ -147,7 +154,8 @@ def tile_list_engram_dl_dl_bsig_kernel(
 
         def gated(c, h, cols):
             if cols.start == 0:
-                prod[c, h] = keep.tile([P, CH], F32, name=f"prod{c}{h}")
+                tag = "prod21" if (c, h) == (CHUNKS - 1, 0) else f"prod{c}{h}"
+                prod[c, h] = keep.tile([P, CH], F32, name=f"prod{c}{h}", tag=tag)
             nc.vector.tensor_tensor(prod[c, h][:, cols], gate[c, h][:, cols], bank[c, VALUE, h][:, cols], MULT)
 
         def add_store(c, h, cols, engine):
@@ -159,8 +167,8 @@ def tile_list_engram_dl_dl_bsig_kernel(
         def first_steps():
             gather_words(0, keep, "picked")
             part_words(0)
-            for a in range(PASSES):
-                for w in (KEY, VALUE):
+            for w in (KEY, VALUE):
+                for a in range(PASSES):
                     for h in range(HALVES):
                         base_pass(0, w, h, a)
             gather_words(1, keep, "picked")
@@ -174,7 +182,6 @@ def tile_list_engram_dl_dl_bsig_kernel(
             quantise(KEY, 1)
             gather_words(3, late1, f"raw{KEY}1")
             part_words(2)
-            part_words(3)
             quantise(VALUE, 0)
 
         with tc.tile_pool(name="window", bufs=1, side="right") as window:
@@ -185,11 +192,7 @@ def tile_list_engram_dl_dl_bsig_kernel(
             for w, scales in ((KEY, wk4_scales), (VALUE, wv4_scales)):
                 cols = slice((PAIR + w * N) // 4, (PAIR + (w + 1) * N) // 4)
                 nc.scalar.dma_start(stage[:].bitcast(I32)[ROWS0:P, cols], compact(scales))
-            for w, words in ((KEY, wk4_words), (VALUE, wv4_words)):
-                nc.sync.dma_start(
-                    w4[w][:].bitcast(I32).rearrange("p (a n) -> p a n", a=PASSES),
-                    words.bitcast(I32).rearrange("a p n -> p a n"),
-                )
+            load_base(keep, KEY, wk4_words)
             warm = keep.tile([P, 2], F32, name="warm")
             nc.gpsimd.memset(warm[:, 0:1], 0.0)
             nc.scalar.activation(warm[:, 1:2], warm[:, 0:1], SIGMOID)
@@ -214,6 +217,7 @@ def tile_list_engram_dl_dl_bsig_kernel(
                     stop=True,
                 )
             late1 = ctx.enter_context(tc.tile_pool(name="late1", bufs=1))
+            load_base(late1, VALUE, wv4_words)
             for w, wd in ((KEY, wkd), (VALUE, wvd)):
                 for a in range(PASSES):
                     load_delta(late1, w, wd, a)
@@ -233,6 +237,7 @@ def tile_list_engram_dl_dl_bsig_kernel(
         whole = slice(0, CH)
 
         quantise(VALUE, 1)
+        part_words(3)
         for w in (KEY, VALUE):
             for c in range(2):
                 for h in range(HALVES):
@@ -258,12 +263,11 @@ def tile_list_engram_dl_dl_bsig_kernel(
                 for h in range(HALVES):
                     gated(c, h, whole)
                 for h in range(HALVES):
-                    add_store(c, h, whole, nc.gpsimd)
+                    add_store(c, h, whole, nc.gpsimd if h == 0 else nc.vector)
             else:
-                gated(c, 0, whole)
-                add_store(c, 0, whole, nc.vector)
                 parts = [slice(0, CH // 2), slice(CH // 2, CH)]
-                for cols in parts:
-                    gated(c, 1, cols)
-                for cols in parts:
-                    add_store(c, 1, cols, nc.vector)
+                for h in range(HALVES):
+                    for cols in parts:
+                        gated(c, h, cols)
+                    for cols in parts:
+                        add_store(c, h, cols, nc.gpsimd if h == 0 else nc.vector)

@@ -58,11 +58,10 @@ def tile_list_engram_dl_dl_bsig_kernel(
         stage = keep.tile([P, first_w], U8, name="stage", align_bytes=64)
         planes = keep.tile([P, PASSES * first_w], U8, name="planes", align_bytes=64)
         planes23 = keep.tile([P, PASSES * PAIR], U8, name="planes23", align_bytes=64)
-        rows23 = keep.tile([P, PAIR], U8, name="rows23", align_bytes=64)
         w4 = {}
 
-        def load_base(pool, w, words):
-            w4[w] = pool.tile([P, PASSES * 2 * N], U8, name=f"w4_{w}", align_bytes=64)
+        def load_base(tile, w, words):
+            w4[w] = tile
             nc.sync.dma_start(
                 w4[w][:].bitcast(I32).rearrange("p (a n) -> p a n", a=PASSES),
                 words.bitcast(I32).rearrange("a p n -> p a n"),
@@ -71,33 +70,34 @@ def tile_list_engram_dl_dl_bsig_kernel(
         raw, st_t, res_t = {}, {}, {}
         picked, parted, codes, dscale, bank, gate, prod = {}, {}, {}, {}, {}, {}, {}
 
-        def load_delta(pool, w, wd, a):
-            raw[w, a] = pool.tile([P, PACK, N], F32, name=f"raw{w}{a}", tag=f"raw{w}{a}", align_bytes=64)
+        def load_delta(tile, w, wd, a):
+            raw[w, a] = tile
             rows = wd[a * K_PASS : (a + 1) * K_PASS, :]
-            nc.sync.dma_start(raw[w, a][:], rows.rearrange("(p i) n -> p i n", i=PACK))
+            nc.sync.dma_start(tile[:], rows.rearrange("(p i) n -> p i n", i=PACK))
 
-        def load_rows(pool, dst, src, g, name):
-            dst[g] = pool.tile([P, HALVES, PAIR], F32, name=f"{name}{g}")
-            nc.sync.dma_start(dst[g][:], src.rearrange("(h p) j -> p h j", p=P)[:, :, g * PAIR : (g + 1) * PAIR])
+        def load_rows(tile, dst, src, g):
+            dst[g] = tile
+            nc.sync.dma_start(tile[:], src.rearrange("(h p) j -> p h j", p=P)[:, :, g * PAIR : (g + 1) * PAIR])
 
-        def gather_words(c, pool, tag):
-            picked[c] = pool.tile([P, CH], U32, name=f"picked{c}", tag=tag, align_bytes=64)
-            entries = offsets[:, c * CH // GROUP : (c + 1) * CH // GROUP]
-            nc.vector.tensor_copy(picked[c][:], table[:].bitcast(U32).indirect(entries))
+        def entries(c, chunks=1):
+            return offsets[:, c * CH // GROUP : (c + chunks) * CH // GROUP]
 
-        def part_words(c):
-            tag = f"grouped{c - 2}1" if c >= 2 else f"parted{c}"
-            parted[c] = keep.tile([P, PASSES * 2 * CH], U8, name=f"parted{c}", tag=tag, align_bytes=64)
-            dst = parted[c][:].bitcast(U16).rearrange("p (a j) -> p a j", a=PASSES)
+        def gather_words(c, tile):
+            picked[c] = tile
+            nc.vector.tensor_copy(tile[:], table[:].bitcast(U32).indirect(entries(c)))
+
+        def part_words(c, tile, by_pass):
+            parted[c] = tile
+            dst = tile[:].bitcast(U16).rearrange("p (a j) -> p a j", a=PASSES)
             src = picked[c][:].bitcast(U16).rearrange("p (j a) -> p a j", a=PASSES)
-            if c == 0:
+            if by_pass:
                 for a in range(PASSES):
                     nc.vector.tensor_copy(dst[:, a, :], src[:, a, :])
             else:
                 nc.vector.tensor_copy(dst, src)
 
         def quantise(w, a):
-            grouped = keep.tile([P, PACK * N], BF16, name=f"grouped{w}{a}", tag=f"grouped{w}{a}", align_bytes=64)
+            grouped = keep.tile([P, PACK * N], BF16, name=f"grouped{w}{a}", align_bytes=64)
             nc.scalar.copy(
                 grouped[:].rearrange("p (m u i) -> p m i u", u=4, i=PACK),
                 raw[w, a][:].rearrange("p i (m u) -> p m i u", u=4),
@@ -164,84 +164,85 @@ def tile_list_engram_dl_dl_bsig_kernel(
             engine.tensor_tensor(total[:], prod[c, h][:, cols], res_t[c // 2][:, h, j0 + cols.start : j0 + cols.stop], ADD)
             nc.sync.dma_start(out[h * P : (h + 1) * P, c * CH + cols.start : c * CH + cols.stop], total[:])
 
-        def first_steps():
-            gather_words(0, keep, "picked")
-            part_words(0)
-            for w in (KEY, VALUE):
-                for a in range(PASSES):
+        srows = keep.tile([P, T], U8, name="srows", align_bytes=64)
+        nc.sync.dma_start(srows[:].bitcast(I32)[ROWS0:P, :], compact(tab_scales))
+        nc.sync.dma_start(offsets[:], offs)
+        for w, scales in ((KEY, wk4_scales), (VALUE, wv4_scales)):
+            cols = slice((PAIR + w * N) // 4, (PAIR + (w + 1) * N) // 4)
+            nc.sync.dma_start(stage[:].bitcast(I32)[ROWS0:P, cols], compact(scales))
+        nc.sync.dma_start(table[:], tab_words[0].rearrange("p t i -> p (t i)").bitcast(I32))
+        load_base(keep.tile([P, PASSES * 2 * N], U8, name="w4k", align_bytes=64), KEY, wk4_words)
+        load_base(keep.tile([P, PASSES * 2 * N], U8, name="w4v", align_bytes=64), VALUE, wv4_words)
+        warm = keep.tile([P, 2], F32, name="warm")
+        nc.gpsimd.memset(warm[:, 0:1], 0.0)
+        nc.scalar.activation(warm[:, 1:2], warm[:, 0:1], SIGMOID)
+        nc.vector.memset(srows[:].bitcast(I32)[0:ROWS0, :], 0)
+        nc.vector.memset(planes[:].bitcast(I32), 0)
+        nc.gpsimd.memset(planes23[:].bitcast(I32), 0)
+
+        with tc.tile_pool(name="early", bufs=1) as early:
+            rows01 = early.tile([P, PAIR], U8, name="rows01", align_bytes=64)
+            nc.vector.tensor_copy(rows01[:], srows[:].indirect(entries(0, 2)))
+            nc.vector.tensor_copy(stage[:].bitcast(I32)[:, 0 : PAIR // 4], rows01[:].bitcast(I32))
+        spread(planes, stage)
+        spare = psum.tile([P, CH], F32, name="spare", tag="bank7")
+        for i in range(WARM_PASSES):
+            nc.tensor.matmul_mx(
+                out=spare[:],
+                lhsT=stage[:, 0 : 2 * P].bitcast(FP4X4),
+                lhsT_scale=stage[:, 0:P],
+                rhs=stage[:, 0 : 2 * CH].bitcast(FP4X4),
+                rhs_scale=stage[:, 0:CH],
+                start=True,
+                stop=True,
+            )
+        late = ctx.enter_context(tc.tile_pool(name="late", bufs=1))
+
+        def late_tile(name, shape, dtype, kib):
+            return late.tile(shape, dtype, name=name, align_bytes=64, offset=int(kib * 1024))
+
+        rows2 = late_tile("rows2", [P, CH], U8, 42)
+        nc.vector.tensor_copy(rows2[:], srows[:].indirect(entries(2)))
+        load_delta(late_tile("raw00", [P, PACK, N], F32, 6), KEY, wkd, 0)
+        load_delta(late_tile("raw01", [P, PACK, N], F32, 16), KEY, wkd, 1)
+        load_delta(late_tile("raw10", [P, PACK, N], F32, 20), VALUE, wvd, 0)
+        load_delta(late_tile("raw11", [P, PACK, N], F32, 30), VALUE, wvd, 1)
+        load_rows(late_tile("st0", [P, HALVES, PAIR], F32, 34), st_t, st, 0)
+        bias = late_tile("bias", [P, HALVES], F32, 43)
+        with nc.allow_non_contiguous_dma(reason="one bias value a partition"):
+            nc.sync.dma_start(bias[:], b.rearrange("(h p) -> p h", p=P))
+
+        for c in range(2):
+            gather_words(c, keep.tile([P, CH], U32, name=f"picked{c}", tag="picked", align_bytes=64))
+            part_words(c, keep.tile([P, PASSES * 2 * CH], U8, name=f"parted{c}", align_bytes=64), True)
+            for a in range(PASSES):
+                for w in (KEY, VALUE):
                     for h in range(HALVES):
-                        base_pass(0, w, h, a)
-            gather_words(1, keep, "picked")
-            part_words(1)
-            for w in (KEY, VALUE):
-                for h in range(HALVES):
-                    for a in range(PASSES):
-                        base_pass(1, w, h, a)
-            quantise(KEY, 0)
-            gather_words(2, keep, f"grouped{KEY}0")
-            quantise(KEY, 1)
-            gather_words(3, late1, f"raw{KEY}1")
-            part_words(2)
-            quantise(VALUE, 0)
-
-        with tc.tile_pool(name="window", bufs=1, side="right") as window:
-            srows = window.tile([P, T], U8, name="srows", align_bytes=64)
-            nc.sync.dma_start(srows[:].bitcast(I32)[ROWS0:P, :], compact(tab_scales))
-            nc.sync.dma_start(offsets[:], offs)
-            nc.sync.dma_start(table[:], tab_words[0].rearrange("p t i -> p (t i)").bitcast(I32))
-            for w, scales in ((KEY, wk4_scales), (VALUE, wv4_scales)):
-                cols = slice((PAIR + w * N) // 4, (PAIR + (w + 1) * N) // 4)
-                nc.scalar.dma_start(stage[:].bitcast(I32)[ROWS0:P, cols], compact(scales))
-            load_base(keep, KEY, wk4_words)
-            warm = keep.tile([P, 2], F32, name="warm")
-            nc.gpsimd.memset(warm[:, 0:1], 0.0)
-            nc.scalar.activation(warm[:, 1:2], warm[:, 0:1], SIGMOID)
-            nc.vector.memset(srows[:].bitcast(I32)[0:ROWS0, :], 0)
-            nc.vector.memset(planes[:].bitcast(I32), 0)
-            nc.gpsimd.memset(planes23[:].bitcast(I32), 0)
-
-            with tc.tile_pool(name="early", bufs=1) as early:
-                picked_rows0 = early.tile([P, PAIR], U8, name="picked_rows0", align_bytes=64)
-                nc.vector.tensor_copy(picked_rows0[:], srows[:].indirect(offsets[:, 0 : PAIR // GROUP]))
-                nc.vector.tensor_copy(stage[:].bitcast(I32)[:, 0 : PAIR // 4], picked_rows0[:].bitcast(I32))
-            spread(planes, stage)
-            spare = psum.tile([P, CH], F32, name="spare", tag="bank7")
-            for i in range(WARM_PASSES):
-                nc.tensor.matmul_mx(
-                    out=spare[:],
-                    lhsT=stage[:, 0 : 2 * P].bitcast(FP4X4),
-                    lhsT_scale=stage[:, 0:P],
-                    rhs=stage[:, 0 : 2 * CH].bitcast(FP4X4),
-                    rhs_scale=stage[:, 0:CH],
-                    start=True,
-                    stop=True,
-                )
-            late1 = ctx.enter_context(tc.tile_pool(name="late1", bufs=1))
-            load_base(late1, VALUE, wv4_words)
-            for w, wd in ((KEY, wkd), (VALUE, wvd)):
-                for a in range(PASSES):
-                    load_delta(late1, w, wd, a)
-            load_rows(late1, st_t, st, 0, "st")
-            for c in (2, 3):
-                entries = offsets[:, c * CH // GROUP : (c + 1) * CH // GROUP]
-                nc.vector.tensor_copy(rows23[:, cols_of(c)], srows[:].indirect(entries))
-            spread(planes23, rows23)
-            bias = late1.tile([P, HALVES], F32, name="bias")
-            with nc.allow_non_contiguous_dma(reason="one bias value a partition"):
-                nc.sync.dma_start(bias[:], b.rearrange("(h p) -> p h", p=P))
-            load_rows(late1, res_t, res, 0, "res")
-            for dst, src, name in ((st_t, st, "st"), (res_t, res, "res")):
-                load_rows(late1, dst, src, 1, name)
-        first_steps()
+                        base_pass(c, w, h, a)
+        quantise(KEY, 0)
+        rows3 = late_tile("rows3", [P, CH], U8, 7.75)
+        nc.vector.tensor_copy(rows3[:], srows[:].indirect(entries(3)))
+        quantise(KEY, 1)
+        rows23 = late_tile("rows23", [P, PAIR], U8, 16)
+        nc.vector.tensor_copy(rows23[:].bitcast(I32)[:, 0 : CH // 4], rows2[:].bitcast(I32))
+        nc.vector.tensor_copy(rows23[:].bitcast(I32)[:, CH // 4 : PAIR // 4], rows3[:].bitcast(I32))
+        spread(planes23, rows23)
+        load_rows(late_tile("res0", [P, HALVES, PAIR], F32, 0), res_t, res, 0)
+        load_rows(late_tile("st1", [P, HALVES, PAIR], F32, 8), st_t, st, 1)
+        gather_words(2, late_tile("picked2", [P, CH], U32, 17))
+        quantise(VALUE, 0)
+        load_rows(late_tile("res1", [P, HALVES, PAIR], F32, 22), res_t, res, 1)
+        part_words(2, late_tile("parted2", [P, PASSES * 2 * CH], U8, 20), False)
+        quantise(VALUE, 1)
+        gather_words(3, late_tile("picked3", [P, CH], U32, 30))
+        part_words(3, keep.tile([P, PASSES * 2 * CH], U8, name="parted3", align_bytes=64), False)
 
         whole = slice(0, CH)
 
-        quantise(VALUE, 1)
-        part_words(3)
         for w in (KEY, VALUE):
-            for c in range(2):
-                for h in range(HALVES):
-                    for a in range(PASSES):
+            for a in range(PASSES):
+                for c in range(2):
+                    for h in range(HALVES):
                         delta_pass(c, w, h, a)
         for c in range(2):
             make_gates(c)

@@ -31,7 +31,7 @@ QUADS = P // QUADRANT
 LIVE = 4
 ROWS0 = P - QUADRANT
 KEY, VALUE = 0, 1
-WARM_PASSES = 6
+WARM_PASSES = 4
 
 
 def tile_list_engram_dl_dl_bsig_kernel(
@@ -54,10 +54,11 @@ def tile_list_engram_dl_dl_bsig_kernel(
 
         offsets = keep.tile([P, J // GROUP], U16, name="offsets")
         table = keep.tile([P, T], I32, name="table", align_bytes=64)
-        first_w = PAIR + 2 * N
+        first_w = CH + 2 * N
+        rest_w = J - CH
         stage = keep.tile([P, first_w], U8, name="stage", align_bytes=64)
         planes = keep.tile([P, PASSES * first_w], U8, name="planes", align_bytes=64)
-        planes23 = keep.tile([P, PASSES * PAIR], U8, name="planes23", align_bytes=64)
+        planes_rest = keep.tile([P, PASSES * rest_w], U8, name="planes_rest", align_bytes=64)
         w4 = {}
 
         def load_base(tile, w, words):
@@ -96,21 +97,21 @@ def tile_list_engram_dl_dl_bsig_kernel(
             else:
                 nc.vector.tensor_copy(dst, src)
 
-        def quantise(w, a):
+        def quantise(w, a, tile=None):
             grouped = keep.tile([P, PACK * N], BF16, name=f"grouped{w}{a}", align_bytes=64)
             nc.scalar.copy(
                 grouped[:].rearrange("p (m u i) -> p m i u", u=4, i=PACK),
                 raw[w, a][:].rearrange("p i (m u) -> p m i u", u=4),
             )
-            codes[w, a] = keep.tile([P, N], U32, name=f"codes{w}{a}", align_bytes=64)
+            codes[w, a] = tile if tile is not None else keep.tile([P, N], U32, name=f"codes{w}{a}", align_bytes=64)
             dscale[w, a] = keep.tile([P, N], U8, name=f"dscale{w}{a}", align_bytes=64)
             nc.vector.quantize_mx(out=codes[w, a][:].bitcast(FP8X4), scales=dscale[w, a][:], in_=grouped[:])
 
         def moving(c, a):
             words = parted[c][:, a * 2 * CH : (a + 1) * 2 * CH].bitcast(FP4X4)
-            if c < 2:
-                return words, planes[:, a * first_w + c * CH : a * first_w + (c + 1) * CH]
-            return words, planes23[:, a * PAIR + (c - 2) * CH : a * PAIR + (c - 1) * CH]
+            if c == 0:
+                return words, planes[:, a * first_w : a * first_w + CH]
+            return words, planes_rest[:, a * rest_w + (c - 1) * CH : a * rest_w + c * CH]
 
         def base_pass(c, w, h, a):
             if a == 0:
@@ -118,7 +119,7 @@ def tile_list_engram_dl_dl_bsig_kernel(
                 bank[c, w, h] = psum.tile([P, CH], F32, name=f"bank{c}{w}{h}", tag=f"bank{slot}")
             words, scale = moving(c, a)
             n0 = a * N + h * P
-            s0 = a * first_w + PAIR + w * N + h * P
+            s0 = a * first_w + CH + w * N + h * P
             nc.tensor.matmul_mx(
                 out=bank[c, w, h][:],
                 lhsT=w4[w][:, 2 * n0 : 2 * (n0 + P)].bitcast(FP4X4),
@@ -164,53 +165,61 @@ def tile_list_engram_dl_dl_bsig_kernel(
             engine.tensor_tensor(total[:], prod[c, h][:, cols], res_t[c // 2][:, h, j0 + cols.start : j0 + cols.stop], ADD)
             nc.sync.dma_start(out[h * P : (h + 1) * P, c * CH + cols.start : c * CH + cols.stop], total[:])
 
-        srows = keep.tile([P, T], U8, name="srows", align_bytes=64)
-        nc.sync.dma_start(srows[:].bitcast(I32)[ROWS0:P, :], compact(tab_scales))
-        nc.sync.dma_start(offsets[:], offs)
-        for w, scales in ((KEY, wk4_scales), (VALUE, wv4_scales)):
-            cols = slice((PAIR + w * N) // 4, (PAIR + (w + 1) * N) // 4)
-            nc.sync.dma_start(stage[:].bitcast(I32)[ROWS0:P, cols], compact(scales))
-        nc.sync.dma_start(table[:], tab_words[0].rearrange("p t i -> p (t i)").bitcast(I32))
-        load_base(keep.tile([P, PASSES * 2 * N], U8, name="w4k", align_bytes=64), KEY, wk4_words)
-        load_base(keep.tile([P, PASSES * 2 * N], U8, name="w4v", align_bytes=64), VALUE, wv4_words)
-        warm = keep.tile([P, 2], F32, name="warm")
-        nc.gpsimd.memset(warm[:, 0:1], 0.0)
-        nc.scalar.activation(warm[:, 1:2], warm[:, 0:1], SIGMOID)
-        nc.vector.memset(srows[:].bitcast(I32)[0:ROWS0, :], 0)
-        nc.vector.memset(planes[:].bitcast(I32), 0)
-        nc.gpsimd.memset(planes23[:].bitcast(I32), 0)
+        with tc.tile_pool(name="window", bufs=1, side="right") as window:
+            srows = window.tile([P, T], U8, name="srows", align_bytes=64)
+            nc.sync.dma_start(srows[:].bitcast(I32)[ROWS0:P, :], compact(tab_scales))
+            nc.sync.dma_start(offsets[:], offs)
+            for w, scales in ((KEY, wk4_scales), (VALUE, wv4_scales)):
+                cols = slice((CH + w * N) // 4, (CH + (w + 1) * N) // 4)
+                nc.sync.dma_start(stage[:].bitcast(I32)[ROWS0:P, cols], compact(scales))
+            nc.sync.dma_start(table[:], tab_words[0].rearrange("p t i -> p (t i)").bitcast(I32))
+            load_base(keep.tile([P, PASSES * 2 * N], U8, name="w4k", align_bytes=64), KEY, wk4_words)
+            load_base(keep.tile([P, PASSES * 2 * N], U8, name="w4v", align_bytes=64), VALUE, wv4_words)
+            warm = keep.tile([P, 2], F32, name="warm")
+            nc.gpsimd.memset(warm[:, 0:1], 0.0)
+            nc.scalar.activation(warm[:, 1:2], warm[:, 0:1], SIGMOID)
+            nc.vector.memset(srows[:].bitcast(I32)[0:ROWS0, :], 0)
+            nc.vector.memset(planes[:].bitcast(I32), 0)
+            nc.gpsimd.memset(planes_rest[:].bitcast(I32), 0)
 
-        with tc.tile_pool(name="early", bufs=1) as early:
-            rows01 = early.tile([P, PAIR], U8, name="rows01", align_bytes=64)
-            nc.vector.tensor_copy(rows01[:], srows[:].indirect(entries(0, 2)))
-            nc.vector.tensor_copy(stage[:].bitcast(I32)[:, 0 : PAIR // 4], rows01[:].bitcast(I32))
-        spread(planes, stage)
+            with tc.tile_pool(name="early", bufs=1) as early:
+                rows0 = early.tile([P, CH], U8, name="rows0", align_bytes=64)
+                nc.vector.tensor_copy(rows0[:], srows[:].indirect(entries(0)))
+                nc.vector.tensor_copy(stage[:].bitcast(I32)[:, 0 : CH // 4], rows0[:].bitcast(I32))
+            spread(planes, stage)
+            mid = ctx.enter_context(tc.tile_pool(name="mid", bufs=1))
+
+            def mid_tile(name, shape, dtype, offset):
+                return mid.tile(shape, dtype, name=name, align_bytes=64, offset=offset)
+
+            raw_bytes = PACK * N * 4
+            load_delta(mid_tile("raw00", [P, PACK, N], F32, 0), KEY, wkd, 0)
+            load_delta(mid_tile("raw01", [P, PACK, N], F32, raw_bytes + rest_w), KEY, wkd, 1)
+            rows_rest = mid_tile("rows_rest", [P, rest_w], U8, raw_bytes)
+            nc.vector.tensor_copy(rows_rest[:], srows[:].indirect(entries(1, CHUNKS - 1)))
+            spread(planes_rest, rows_rest)
+        late = ctx.enter_context(tc.tile_pool(name="late", bufs=1, side="right"))
+        for a in range(PASSES):
+            load_delta(late.tile([P, PACK, N], F32, name=f"raw1{a}", tag=f"raw1{a}", align_bytes=64), VALUE, wvd, a)
+        load_rows(late.tile([P, HALVES, PAIR], F32, name="st0"), st_t, st, 0)
+        bias = late.tile([P, HALVES], F32, name="bias")
+        with nc.allow_non_contiguous_dma(reason="one bias value a partition"):
+            nc.sync.dma_start(bias[:], b.rearrange("(h p) -> p h", p=P))
+        load_rows(late.tile([P, HALVES, PAIR], F32, name="res0"), res_t, res, 0)
+        load_rows(late.tile([P, HALVES, PAIR], F32, name="st1"), st_t, st, 1)
+        load_rows(late.tile([P, HALVES, PAIR], F32, name="res1"), res_t, res, 1)
+
         spare = psum.tile([P, CH], F32, name="spare", tag="bank7")
         for i in range(WARM_PASSES):
             nc.tensor.matmul_mx(
                 out=spare[:],
                 lhsT=stage[:, 0 : 2 * P].bitcast(FP4X4),
                 lhsT_scale=stage[:, 0:P],
-                rhs=stage[:, 0 : 2 * CH].bitcast(FP4X4),
+                rhs=table[:].bitcast(U8)[:, 0 : 2 * CH].bitcast(FP4X4),
                 rhs_scale=stage[:, 0:CH],
                 start=True,
                 stop=True,
             )
-        late = ctx.enter_context(tc.tile_pool(name="late", bufs=1))
-
-        def late_tile(name, shape, dtype, kib):
-            return late.tile(shape, dtype, name=name, align_bytes=64, offset=int(kib * 1024))
-
-        rows2 = late_tile("rows2", [P, CH], U8, 42)
-        nc.vector.tensor_copy(rows2[:], srows[:].indirect(entries(2)))
-        load_delta(late_tile("raw00", [P, PACK, N], F32, 6), KEY, wkd, 0)
-        load_delta(late_tile("raw01", [P, PACK, N], F32, 16), KEY, wkd, 1)
-        load_delta(late_tile("raw10", [P, PACK, N], F32, 20), VALUE, wvd, 0)
-        load_delta(late_tile("raw11", [P, PACK, N], F32, 30), VALUE, wvd, 1)
-        load_rows(late_tile("st0", [P, HALVES, PAIR], F32, 34), st_t, st, 0)
-        bias = late_tile("bias", [P, HALVES], F32, 43)
-        with nc.allow_non_contiguous_dma(reason="one bias value a partition"):
-            nc.sync.dma_start(bias[:], b.rearrange("(h p) -> p h", p=P))
 
         for c in range(2):
             gather_words(c, keep.tile([P, CH], U32, name=f"picked{c}", tag="picked", align_bytes=64))
@@ -219,23 +228,14 @@ def tile_list_engram_dl_dl_bsig_kernel(
                 for w in (KEY, VALUE):
                     for h in range(HALVES):
                         base_pass(c, w, h, a)
-        quantise(KEY, 0)
-        rows3 = late_tile("rows3", [P, CH], U8, 7.75)
-        nc.vector.tensor_copy(rows3[:], srows[:].indirect(entries(3)))
+        gather_words(2, keep.tile([P, CH], U32, name="picked2", tag="picked", align_bytes=64))
+        quantise(KEY, 0, mid_tile("codes00", [P, N], U32, raw_bytes + 256))
+        part_words(2, mid_tile("parted2", [P, PASSES * 2 * CH], U8, raw_bytes + 256 - 4 * CH), False)
         quantise(KEY, 1)
-        rows23 = late_tile("rows23", [P, PAIR], U8, 16)
-        nc.vector.tensor_copy(rows23[:].bitcast(I32)[:, 0 : CH // 4], rows2[:].bitcast(I32))
-        nc.vector.tensor_copy(rows23[:].bitcast(I32)[:, CH // 4 : PAIR // 4], rows3[:].bitcast(I32))
-        spread(planes23, rows23)
-        load_rows(late_tile("res0", [P, HALVES, PAIR], F32, 0), res_t, res, 0)
-        load_rows(late_tile("st1", [P, HALVES, PAIR], F32, 8), st_t, st, 1)
-        gather_words(2, late_tile("picked2", [P, CH], U32, 17))
+        gather_words(3, mid_tile("picked3", [P, CH], U32, raw_bytes + 256 + 4 * N))
         quantise(VALUE, 0)
-        load_rows(late_tile("res1", [P, HALVES, PAIR], F32, 22), res_t, res, 1)
-        part_words(2, late_tile("parted2", [P, PASSES * 2 * CH], U8, 20), False)
+        part_words(3, late.tile([P, PASSES * 2 * CH], U8, name="parted3", tag="raw10", align_bytes=64), False)
         quantise(VALUE, 1)
-        gather_words(3, late_tile("picked3", [P, CH], U32, 30))
-        part_words(3, keep.tile([P, PASSES * 2 * CH], U8, name="parted3", align_bytes=64), False)
 
         whole = slice(0, CH)
 

@@ -31,7 +31,7 @@ QUADS = P // QUADRANT
 LIVE = 4
 ROWS0 = P - QUADRANT
 KEY, VALUE = 0, 1
-WARM_PASSES = 4
+WARM_PASSES = 6
 
 
 def tile_list_engram_dl_dl_bsig_kernel(
@@ -56,7 +56,7 @@ def tile_list_engram_dl_dl_bsig_kernel(
         table = keep.tile([P, T], I32, name="table", align_bytes=64)
         first_w = CH + 2 * N
         rest_w = J - CH
-        stage = keep.tile([P, first_w], U8, name="stage", align_bytes=64)
+        stage = keep.tile([P, first_w], U8, name="stage", tag="stage", align_bytes=64)
         planes = keep.tile([P, PASSES * first_w], U8, name="planes", align_bytes=64)
         planes_rest = keep.tile([P, PASSES * rest_w], U8, name="planes_rest", align_bytes=64)
         w4 = {}
@@ -98,7 +98,7 @@ def tile_list_engram_dl_dl_bsig_kernel(
                 nc.vector.tensor_copy(dst, src)
 
         def quantise(w, a, tile=None):
-            grouped = keep.tile([P, PACK * N], BF16, name=f"grouped{w}{a}", align_bytes=64)
+            grouped = keep.tile([P, PACK * N], BF16, name=f"grouped{w}{a}", tag=f"grouped{w}{a}", align_bytes=64)
             nc.scalar.copy(
                 grouped[:].rearrange("p (m u i) -> p m i u", u=4, i=PACK),
                 raw[w, a][:].rearrange("p i (m u) -> p m i u", u=4),
@@ -165,16 +165,16 @@ def tile_list_engram_dl_dl_bsig_kernel(
             engine.tensor_tensor(total[:], prod[c, h][:, cols], res_t[c // 2][:, h, j0 + cols.start : j0 + cols.stop], ADD)
             nc.sync.dma_start(out[h * P : (h + 1) * P, c * CH + cols.start : c * CH + cols.stop], total[:])
 
+        raw_bytes = PACK * N * 4
         with tc.tile_pool(name="window", bufs=1, side="right") as window:
             srows = window.tile([P, T], U8, name="srows", align_bytes=64)
             nc.sync.dma_start(srows[:].bitcast(I32)[ROWS0:P, :], compact(tab_scales))
             nc.sync.dma_start(offsets[:], offs)
+            nc.sync.dma_start(table[:], tab_words[0].rearrange("p t i -> p (t i)").bitcast(I32))
             for w, scales in ((KEY, wk4_scales), (VALUE, wv4_scales)):
                 cols = slice((CH + w * N) // 4, (CH + (w + 1) * N) // 4)
-                nc.sync.dma_start(stage[:].bitcast(I32)[ROWS0:P, cols], compact(scales))
-            nc.sync.dma_start(table[:], tab_words[0].rearrange("p t i -> p (t i)").bitcast(I32))
+                nc.scalar.dma_start(stage[:].bitcast(I32)[ROWS0:P, cols], compact(scales))
             load_base(keep.tile([P, PASSES * 2 * N], U8, name="w4k", align_bytes=64), KEY, wk4_words)
-            load_base(keep.tile([P, PASSES * 2 * N], U8, name="w4v", align_bytes=64), VALUE, wv4_words)
             warm = keep.tile([P, 2], F32, name="warm")
             nc.gpsimd.memset(warm[:, 0:1], 0.0)
             nc.scalar.activation(warm[:, 1:2], warm[:, 0:1], SIGMOID)
@@ -182,25 +182,24 @@ def tile_list_engram_dl_dl_bsig_kernel(
             nc.vector.memset(planes[:].bitcast(I32), 0)
             nc.gpsimd.memset(planes_rest[:].bitcast(I32), 0)
 
-            with tc.tile_pool(name="early", bufs=1) as early:
-                rows0 = early.tile([P, CH], U8, name="rows0", align_bytes=64)
-                nc.vector.tensor_copy(rows0[:], srows[:].indirect(entries(0)))
-                nc.vector.tensor_copy(stage[:].bitcast(I32)[:, 0 : CH // 4], rows0[:].bitcast(I32))
+            shared = ctx.enter_context(tc.tile_pool(name="shared", bufs=1))
+
+            def shared_tile(name, shape, dtype, offset):
+                return shared.tile(shape, dtype, name=name, align_bytes=64, offset=offset)
+
+            rows0 = shared_tile("rows0", [P, CH], U8, 768)
+            nc.vector.tensor_copy(rows0[:], srows[:].indirect(entries(0)))
+            nc.vector.tensor_copy(stage[:].bitcast(I32)[:, 0 : CH // 4], rows0[:].bitcast(I32))
             spread(planes, stage)
-            mid = ctx.enter_context(tc.tile_pool(name="mid", bufs=1))
-
-            def mid_tile(name, shape, dtype, offset):
-                return mid.tile(shape, dtype, name=name, align_bytes=64, offset=offset)
-
-            raw_bytes = PACK * N * 4
-            load_delta(mid_tile("raw00", [P, PACK, N], F32, 0), KEY, wkd, 0)
-            load_delta(mid_tile("raw01", [P, PACK, N], F32, raw_bytes + rest_w), KEY, wkd, 1)
-            rows_rest = mid_tile("rows_rest", [P, rest_w], U8, raw_bytes)
-            nc.vector.tensor_copy(rows_rest[:], srows[:].indirect(entries(1, CHUNKS - 1)))
+            load_base(shared_tile("w4v", [P, PASSES * 2 * N], U8, 0), VALUE, wv4_words)
+            load_delta(shared_tile("raw00", [P, PACK, N], F32, 1024), KEY, wkd, 0)
+            rows_rest = shared_tile("rows_rest", [P, rest_w], U8, 1024 + raw_bytes)
+            for c in range(1, CHUNKS):
+                nc.vector.tensor_copy(rows_rest[:, (c - 1) * CH : c * CH], srows[:].indirect(entries(c)))
             spread(planes_rest, rows_rest)
         late = ctx.enter_context(tc.tile_pool(name="late", bufs=1, side="right"))
-        for a in range(PASSES):
-            load_delta(late.tile([P, PACK, N], F32, name=f"raw1{a}", tag=f"raw1{a}", align_bytes=64), VALUE, wvd, a)
+        for w, wd, a in ((KEY, wkd, 1), (VALUE, wvd, 0), (VALUE, wvd, 1)):
+            load_delta(late.tile([P, PACK, N], F32, name=f"raw{w}{a}", tag=f"raw{w}{a}", align_bytes=64), w, wd, a)
         load_rows(late.tile([P, HALVES, PAIR], F32, name="st0"), st_t, st, 0)
         bias = late.tile([P, HALVES], F32, name="bias")
         with nc.allow_non_contiguous_dma(reason="one bias value a partition"):
@@ -213,29 +212,29 @@ def tile_list_engram_dl_dl_bsig_kernel(
         for i in range(WARM_PASSES):
             nc.tensor.matmul_mx(
                 out=spare[:],
-                lhsT=stage[:, 0 : 2 * P].bitcast(FP4X4),
-                lhsT_scale=stage[:, 0:P],
-                rhs=table[:].bitcast(U8)[:, 0 : 2 * CH].bitcast(FP4X4),
-                rhs_scale=stage[:, 0:CH],
+                lhsT=rows_rest[:, CH : CH + 2 * P].bitcast(FP4X4),
+                lhsT_scale=rows_rest[:, 0:P],
+                rhs=rows_rest[:, 0 : 2 * CH].bitcast(FP4X4),
+                rhs_scale=rows_rest[:, 0:CH],
                 start=True,
                 stop=True,
             )
 
-        for c in range(2):
-            gather_words(c, keep.tile([P, CH], U32, name=f"picked{c}", tag="picked", align_bytes=64))
+        for c, tag in ((0, "picked0"), (1, "stage")):
+            gather_words(c, keep.tile([P, CH], U32, name=f"picked{c}", tag=tag, align_bytes=64))
             part_words(c, keep.tile([P, PASSES * 2 * CH], U8, name=f"parted{c}", align_bytes=64), True)
-            for a in range(PASSES):
-                for w in (KEY, VALUE):
+            for w in (KEY, VALUE):
+                for a in range(PASSES):
                     for h in range(HALVES):
                         base_pass(c, w, h, a)
-        gather_words(2, keep.tile([P, CH], U32, name="picked2", tag="picked", align_bytes=64))
-        quantise(KEY, 0, mid_tile("codes00", [P, N], U32, raw_bytes + 256))
-        part_words(2, mid_tile("parted2", [P, PASSES * 2 * CH], U8, raw_bytes + 256 - 4 * CH), False)
+        quantise(KEY, 0, shared_tile("codes00", [P, N], U32, 1024 + raw_bytes + 256))
+        gather_words(2, shared_tile("picked2", [P, CH], U32, 1024 + raw_bytes + 256 - 4 * CH))
         quantise(KEY, 1)
-        gather_words(3, mid_tile("picked3", [P, CH], U32, raw_bytes + 256 + 4 * N))
+        gather_words(3, late.tile([P, CH], U32, name="picked3", tag="raw01", align_bytes=64))
+        part_words(2, keep.tile([P, PASSES * 2 * CH], U8, name="parted2", tag="grouped01", align_bytes=64), False)
         quantise(VALUE, 0)
-        part_words(3, late.tile([P, PASSES * 2 * CH], U8, name="parted3", tag="raw10", align_bytes=64), False)
         quantise(VALUE, 1)
+        part_words(3, late.tile([P, PASSES * 2 * CH], U8, name="parted3", tag="raw11", align_bytes=64), False)
 
         whole = slice(0, CH)
 

@@ -97,13 +97,13 @@ def tile_list_engram_dl_dl_bsig_kernel(
             else:
                 nc.vector.tensor_copy(dst, src)
 
-        def quantise(w, a, tile=None):
+        def quantise(w, a):
             grouped = keep.tile([P, PACK * N], BF16, name=f"grouped{w}{a}", tag=f"grouped{w}{a}", align_bytes=64)
             nc.scalar.copy(
                 grouped[:].rearrange("p (m u i) -> p m i u", u=4, i=PACK),
                 raw[w, a][:].rearrange("p i (m u) -> p m i u", u=4),
             )
-            codes[w, a] = tile if tile is not None else keep.tile([P, N], U32, name=f"codes{w}{a}", align_bytes=64)
+            codes[w, a] = keep.tile([P, N], U32, name=f"codes{w}{a}", align_bytes=64)
             dscale[w, a] = keep.tile([P, N], U8, name=f"dscale{w}{a}", align_bytes=64)
             nc.vector.quantize_mx(out=codes[w, a][:].bitcast(FP8X4), scales=dscale[w, a][:], in_=grouped[:])
 
@@ -220,19 +220,26 @@ def tile_list_engram_dl_dl_bsig_kernel(
                 stop=True,
             )
 
-        for c, tag in ((0, "picked0"), (1, "stage")):
-            gather_words(c, keep.tile([P, CH], U32, name=f"picked{c}", tag=tag, align_bytes=64))
-            part_words(c, keep.tile([P, PASSES * 2 * CH], U8, name=f"parted{c}", align_bytes=64), True)
+        def base_passes(c):
             for w in (KEY, VALUE):
                 for a in range(PASSES):
                     for h in range(HALVES):
                         base_pass(c, w, h, a)
-        quantise(KEY, 0, shared_tile("codes00", [P, N], U32, 1024 + raw_bytes + 256))
-        gather_words(2, shared_tile("picked2", [P, CH], U32, 1024 + raw_bytes + 256 - 4 * CH))
+
+        gather_words(0, keep.tile([P, CH], U32, name="picked0", align_bytes=64))
+        part_words(0, keep.tile([P, PASSES * 2 * CH], U8, name="parted0", align_bytes=64), True)
+        base_passes(0)
+        gather_words(1, keep.tile([P, CH], U32, name="picked1", tag="stage", align_bytes=64))
+        quantise(KEY, 0)
+        for h in range(HALVES):
+            delta_pass(0, KEY, h, 0)
+        part_words(1, shared_tile("parted1", [P, PASSES * 2 * CH], U8, 1024), True)
+        base_passes(1)
+        gather_words(2, shared_tile("picked2", [P, CH], U32, 1024 + 4 * CH))
         quantise(KEY, 1)
         gather_words(3, late.tile([P, CH], U32, name="picked3", tag="raw01", align_bytes=64))
-        part_words(2, keep.tile([P, PASSES * 2 * CH], U8, name="parted2", tag="grouped01", align_bytes=64), False)
         quantise(VALUE, 0)
+        part_words(2, late.tile([P, PASSES * 2 * CH], U8, name="parted2", tag="raw10", align_bytes=64), False)
         quantise(VALUE, 1)
         part_words(3, late.tile([P, PASSES * 2 * CH], U8, name="parted3", tag="raw11", align_bytes=64), False)
 
@@ -242,7 +249,8 @@ def tile_list_engram_dl_dl_bsig_kernel(
             for a in range(PASSES):
                 for c in range(2):
                     for h in range(HALVES):
-                        delta_pass(c, w, h, a)
+                        if (c, w, a) != (0, KEY, 0):
+                            delta_pass(c, w, h, a)
         for c in range(2):
             make_gates(c)
         for c in range(2):

@@ -155,15 +155,15 @@ def tile_list_engram_dl_dl_bsig_kernel(
 
         def gated(c, h, cols):
             if cols.start == 0:
-                tag = "prod21" if (c, h) == (CHUNKS - 1, 0) else f"prod{c}{h}"
-                prod[c, h] = keep.tile([P, CH], F32, name=f"prod{c}{h}", tag=tag)
+                prod[c, h] = keep.tile([P, CH], F32, name=f"prod{c}{h}")
             nc.vector.tensor_tensor(prod[c, h][:, cols], gate[c, h][:, cols], bank[c, VALUE, h][:, cols], MULT)
 
-        def add_store(c, h, cols, engine):
-            total = keep.tile([P, cols.stop - cols.start], F32, name=f"o{c}{h}{cols.start}")
+        def add_store(c, h, cols, engine, total=None):
+            if total is None:
+                total = keep.tile([P, cols.stop - cols.start], F32, name=f"o{c}{h}{cols.start}")[:]
             j0 = (c % 2) * CH
-            engine.tensor_tensor(total[:], prod[c, h][:, cols], res_t[c // 2][:, h, j0 + cols.start : j0 + cols.stop], ADD)
-            nc.sync.dma_start(out[h * P : (h + 1) * P, c * CH + cols.start : c * CH + cols.stop], total[:])
+            engine.tensor_tensor(total, prod[c, h][:, cols], res_t[c // 2][:, h, j0 + cols.start : j0 + cols.stop], ADD)
+            nc.sync.dma_start(out[h * P : (h + 1) * P, c * CH + cols.start : c * CH + cols.stop], total)
 
         raw_bytes = PACK * N * 4
         with tc.tile_pool(name="window", bufs=1, side="right") as window:
@@ -191,8 +191,8 @@ def tile_list_engram_dl_dl_bsig_kernel(
             nc.vector.tensor_copy(rows0[:], srows[:].indirect(entries(0)))
             nc.vector.tensor_copy(stage[:].bitcast(I32)[:, 0 : CH // 4], rows0[:].bitcast(I32))
             spread(planes, stage)
-            load_base(shared_tile("w4v", [P, PASSES * 2 * N], U8, 0), VALUE, wv4_words)
             load_delta(shared_tile("raw00", [P, PACK, N], F32, 1024), KEY, wkd, 0)
+            load_base(shared_tile("w4v", [P, PASSES * 2 * N], U8, 0), VALUE, wv4_words)
             rows_rest = shared_tile("rows_rest", [P, rest_w], U8, 1024 + raw_bytes)
             for c in range(1, CHUNKS):
                 nc.vector.tensor_copy(rows_rest[:, (c - 1) * CH : c * CH], srows[:].indirect(entries(c)))
@@ -256,26 +256,31 @@ def tile_list_engram_dl_dl_bsig_kernel(
         for c in range(2):
             for h in range(HALVES):
                 gated(c, h, whole)
-                add_store(c, h, whole, nc.gpsimd)
+                if c == 0:
+                    add_store(c, h, whole, nc.gpsimd)
 
-        for c in range(2, CHUNKS):
-            for w in (KEY, VALUE):
-                for h in range(HALVES):
-                    for a in range(PASSES):
-                        base_pass(c, w, h, a)
-                    for a in range(PASSES):
-                        delta_pass(c, w, h, a)
-                if w == KEY:
-                    make_gates(c)
-            if c < CHUNKS - 1:
-                for h in range(HALVES):
-                    gated(c, h, whole)
-                for h in range(HALVES):
-                    add_store(c, h, whole, nc.gpsimd if h == 0 else nc.vector)
-            else:
-                parts = [slice(0, CH // 2), slice(CH // 2, CH)]
-                for h in range(HALVES):
-                    for cols in parts:
-                        gated(c, h, cols)
-                    for cols in parts:
-                        add_store(c, h, cols, nc.gpsimd if h == 0 else nc.vector)
+        def all_passes(c, w):
+            for h in range(HALVES):
+                for a in range(PASSES):
+                    base_pass(c, w, h, a)
+                for a in range(PASSES):
+                    delta_pass(c, w, h, a)
+
+        all_passes(2, KEY)
+        make_gates(2)
+        all_passes(2, VALUE)
+        after_values = keep.tile([P, CH], F32, name="after_values", tag="pre21", align_bytes=64)
+        for h, total in enumerate((st_t[1][:, 0, cols_of(2)], after_values[:])):
+            add_store(1, h, whole, nc.vector, total=total)
+            gated(2, h, whole)
+        for h in range(HALVES):
+            add_store(2, h, whole, nc.gpsimd)
+        all_passes(3, KEY)
+        make_gates(3)
+        all_passes(3, VALUE)
+        parts = [slice(0, CH // 2), slice(CH // 2, CH)]
+        for h in range(HALVES):
+            for cols in parts:
+                gated(3, h, cols)
+            for cols in parts:
+                add_store(3, h, cols, nc.vector)

@@ -23,15 +23,15 @@ K_PASS = P * PACK
 PASSES = K // K_PASS
 HALVES = N // P
 CH = 512
-CHUNKS = J // CH
+HC = CH // 2
 PAIR = 2 * CH
 GROUP = 16
 QUADRANT = 32
-QUADS = P // QUADRANT
 LIVE = 4
 ROWS0 = P - QUADRANT
 KEY, VALUE = 0, 1
 WARM_PASSES = 6
+KIB = 1024
 
 
 def tile_list_engram_dl_dl_bsig_kernel(
@@ -40,7 +40,11 @@ def tile_list_engram_dl_dl_bsig_kernel(
     nc = tc.nc
     with ExitStack() as ctx:
         keep = ctx.enter_context(tc.tile_pool(name="keep", bufs=1))
+        ring = ctx.enter_context(tc.tile_pool(name="ring", bufs=1))
         psum = ctx.enter_context(tc.psum_pool(name="psum", bufs=1))
+
+        def placed(name, shape, dtype, offset):
+            return ring.tile(shape, dtype, name=name, align_bytes=64, offset=offset)
 
         def compact(scales):
             return scales.bitcast(I32).rearrange("a q n -> q a n")
@@ -52,45 +56,99 @@ def tile_list_engram_dl_dl_bsig_kernel(
                 first = ROWS0 + q * LIVE * PASSES
                 nc.sync.dma_start(dst[q * QUADRANT : q * QUADRANT + LIVE], src[first : first + LIVE * PASSES, :])
 
+        def entries(j0, n):
+            return offsets[:, j0 // GROUP : (j0 + n) // GROUP]
+
         offsets = keep.tile([P, J // GROUP], U16, name="offsets")
         table = keep.tile([P, T], I32, name="table", align_bytes=64)
-        first_w = CH + 2 * N
-        rest_w = J - CH
-        stage = keep.tile([P, first_w], U8, name="stage", tag="stage", align_bytes=64)
+        srows = keep.tile([P, T], U8, name="srows", align_bytes=64)
+        first_w = PAIR + 2 * N
+        stage = keep.tile([P, first_w], U8, name="stage", align_bytes=64)
         planes = keep.tile([P, PASSES * first_w], U8, name="planes", align_bytes=64)
-        planes_rest = keep.tile([P, PASSES * rest_w], U8, name="planes_rest", align_bytes=64)
-        w4 = {}
+        planes2 = keep.tile([P, PASSES * PAIR], U8, name="planes2", align_bytes=64)
+        w4, raw, st_of, res_of = {}, {}, {}, {}
+        parted, codes, dscale, bank, gate, prod = {}, {}, {}, {}, {}, {}
 
-        def load_base(tile, w, words):
-            w4[w] = tile
+        def load_base(pool, w, words):
+            w4[w] = pool.tile([P, PASSES * 2 * N], U8, name=f"w4{w}", align_bytes=64)
             nc.sync.dma_start(
                 w4[w][:].bitcast(I32).rearrange("p (a n) -> p a n", a=PASSES),
                 words.bitcast(I32).rearrange("a p n -> p a n"),
             )
 
-        raw, st_t, res_t = {}, {}, {}
-        picked, parted, codes, dscale, bank, gate, prod = {}, {}, {}, {}, {}, {}, {}
+        def load_rows(name, dst, src, c0, chunks):
+            tile = late.tile([P, HALVES, chunks * CH], F32, name=name)
+            nc.sync.dma_start(tile[:], src.rearrange("(h p) j -> p h j", p=P)[:, :, c0 * CH : (c0 + chunks) * CH])
+            for c in range(chunks):
+                dst[c0 + c] = (tile, c * CH)
 
-        def load_delta(tile, w, wd, a):
-            raw[w, a] = tile
-            rows = wd[a * K_PASS : (a + 1) * K_PASS, :]
-            nc.sync.dma_start(tile[:], rows.rearrange("(p i) n -> p i n", i=PACK))
+        def rows_of(held, j0, n, h):
+            tile, first = held[j0 // CH]
+            return tile[:, h, first + j0 % CH : first + j0 % CH + n]
 
-        def load_rows(tile, dst, src, g):
-            dst[g] = tile
-            nc.sync.dma_start(tile[:], src.rearrange("(h p) j -> p h j", p=P)[:, :, g * PAIR : (g + 1) * PAIR])
+        nc.sync.dma_start(srows[:].bitcast(I32)[ROWS0:P, :], compact(tab_scales))
+        nc.sync.dma_start(offsets[:], offs)
+        nc.sync.dma_start(table[:], tab_words[0].rearrange("p t i -> p (t i)").bitcast(I32))
+        for w, scales in ((KEY, wk4_scales), (VALUE, wv4_scales)):
+            cols = slice((PAIR + w * N) // 4, (PAIR + (w + 1) * N) // 4)
+            nc.scalar.dma_start(stage[:].bitcast(I32)[ROWS0:P, cols], compact(scales))
+        load_base(keep, KEY, wk4_words)
+        warm = keep.tile([P, 2], F32, name="warm")
+        nc.gpsimd.memset(warm[:, 0:1], 0.0)
+        nc.scalar.activation(warm[:, 1:2], warm[:, 0:1], SIGMOID)
+        nc.vector.memset(srows[:].bitcast(I32)[0:ROWS0, :], 0)
+        nc.vector.memset(planes[:].bitcast(I32), 0)
+        nc.gpsimd.memset(planes2[:].bitcast(I32), 0)
 
-        def entries(c, chunks=1):
-            return offsets[:, c * CH // GROUP : (c + chunks) * CH // GROUP]
+        rows0 = keep.tile([P, CH], U8, name="rows0", align_bytes=64)
+        rows23 = keep.tile([P, PAIR], U8, name="rows23", align_bytes=64)
+        with tc.tile_pool(name="window", bufs=1, side="right") as window:
+            rows1 = window.tile([P, CH], U8, name="rows1", align_bytes=64)
+            nc.vector.tensor_copy(rows0[:], srows[:].indirect(entries(0, CH)))
+            nc.vector.tensor_copy(rows1[:], srows[:].indirect(entries(CH, CH)))
+            nc.vector.tensor_copy(stage[:].bitcast(I32)[:, 0 : CH // 4], rows0[:].bitcast(I32))
+            nc.vector.tensor_copy(rows23[:, 0:CH], srows[:].indirect(entries(2 * CH, CH)))
+            nc.vector.tensor_copy(stage[:].bitcast(I32)[:, CH // 4 : PAIR // 4], rows1[:].bitcast(I32))
+            nc.vector.tensor_copy(rows23[:, CH:PAIR], srows[:].indirect(entries(3 * CH, CH)))
+            spread(planes, stage)
+        late = ctx.enter_context(tc.tile_pool(name="late", bufs=1, side="right"))
+        load_base(late, VALUE, wv4_words)
+        for w, wd in ((KEY, wkd), (VALUE, wvd)):
+            for a in range(PASSES):
+                raw[w, a] = late.tile([P, PACK, N], F32, name=f"raw{w}{a}", tag=f"raw{w}{a}", align_bytes=64)
+                rows = wd[a * K_PASS : (a + 1) * K_PASS, :]
+                nc.sync.dma_start(raw[w, a][:], rows.rearrange("(p i) n -> p i n", i=PACK))
+        load_rows("st01", st_of, st, 0, 2)
+        bias = late.tile([P, HALVES], F32, name="bias")
+        with nc.allow_non_contiguous_dma(reason="one bias value a partition"):
+            nc.sync.dma_start(bias[:], b.rearrange("(h p) -> p h", p=P))
+        spread(planes2, rows23)
+        load_rows("res0", res_of, res, 0, 1)
+        load_rows("st2", st_of, st, 2, 1)
+        load_rows("res1", res_of, res, 1, 1)
+        load_rows("st3", st_of, st, 3, 1)
+        load_rows("res2", res_of, res, 2, 1)
+        load_rows("res3", res_of, res, 3, 1)
 
-        def gather_words(c, tile):
-            picked[c] = tile
-            nc.vector.tensor_copy(tile[:], table[:].bitcast(U32).indirect(entries(c)))
+        spare = psum.tile([P, CH], F32, name="spare", tag="bank7")
+        for i in range(WARM_PASSES):
+            nc.tensor.matmul_mx(
+                out=spare[:],
+                lhsT=stage[:, 0 : 2 * P].bitcast(FP4X4),
+                lhsT_scale=stage[:, 0:P],
+                rhs=srows[:, 0 : 2 * CH].bitcast(FP4X4),
+                rhs_scale=stage[:, 0:CH],
+                start=True,
+                stop=True,
+            )
 
-        def part_words(c, tile, by_pass):
-            parted[c] = tile
-            dst = tile[:].bitcast(U16).rearrange("p (a j) -> p a j", a=PASSES)
-            src = picked[c][:].bitcast(U16).rearrange("p (j a) -> p a j", a=PASSES)
+        def gather_words(tile, j0, n):
+            nc.vector.tensor_copy(tile[:], table[:].bitcast(U32).indirect(entries(j0, n)))
+
+        def part_words(picked, j0, n, by_pass):
+            dst = parted[j0 // CH][:].bitcast(U16).rearrange("p (a j) -> p a j", a=PASSES)
+            dst = dst[:, :, j0 % CH : j0 % CH + n]
+            src = picked[:].bitcast(U16).rearrange("p (j a) -> p a j", a=PASSES)
             if by_pass:
                 for a in range(PASSES):
                     nc.vector.tensor_copy(dst[:, a, :], src[:, a, :])
@@ -98,7 +156,7 @@ def tile_list_engram_dl_dl_bsig_kernel(
                 nc.vector.tensor_copy(dst, src)
 
         def quantise(w, a):
-            grouped = keep.tile([P, PACK * N], BF16, name=f"grouped{w}{a}", tag=f"grouped{w}{a}", align_bytes=64)
+            grouped = keep.tile([P, PACK * N], BF16, name=f"grouped{w}{a}", align_bytes=64)
             nc.scalar.copy(
                 grouped[:].rearrange("p (m u i) -> p m i u", u=4, i=PACK),
                 raw[w, a][:].rearrange("p i (m u) -> p m i u", u=4),
@@ -107,180 +165,145 @@ def tile_list_engram_dl_dl_bsig_kernel(
             dscale[w, a] = keep.tile([P, N], U8, name=f"dscale{w}{a}", align_bytes=64)
             nc.vector.quantize_mx(out=codes[w, a][:].bitcast(FP8X4), scales=dscale[w, a][:], in_=grouped[:])
 
-        def moving(c, a):
-            words = parted[c][:, a * 2 * CH : (a + 1) * 2 * CH].bitcast(FP4X4)
-            if c == 0:
-                return words, planes[:, a * first_w : a * first_w + CH]
-            return words, planes_rest[:, a * rest_w + (c - 1) * CH : a * rest_w + c * CH]
-
-        def base_pass(c, w, h, a):
-            if a == 0:
-                slot = (2 * w + c if c < 2 else 2 * (c - 2) + w) * HALVES + h
-                bank[c, w, h] = psum.tile([P, CH], F32, name=f"bank{c}{w}{h}", tag=f"bank{slot}")
-            words, scale = moving(c, a)
-            n0 = a * N + h * P
-            s0 = a * first_w + CH + w * N + h * P
+        def one_pass(acc, w, h, a, delta, j0, n, start=False, stop=False):
+            c, o = divmod(j0, CH)
+            words = parted[c][:, 2 * (a * CH + o) : 2 * (a * CH + o + n)].bitcast(FP4X4)
+            if c < 2:
+                scale = planes[:, a * first_w + j0 : a * first_w + j0 + n]
+            else:
+                scale = planes2[:, a * PAIR + j0 - PAIR : a * PAIR + j0 - PAIR + n]
+            if delta:
+                lhsT = codes[w, a][:, h * P : (h + 1) * P].bitcast(FP8X4)
+                lhsT_scale = dscale[w, a][:, h * P : (h + 1) * P]
+            else:
+                n0 = a * N + h * P
+                s0 = a * first_w + PAIR + w * N + h * P
+                lhsT = w4[w][:, 2 * n0 : 2 * (n0 + P)].bitcast(FP4X4)
+                lhsT_scale = planes[:, s0 : s0 + P]
             nc.tensor.matmul_mx(
-                out=bank[c, w, h][:],
-                lhsT=w4[w][:, 2 * n0 : 2 * (n0 + P)].bitcast(FP4X4),
-                lhsT_scale=planes[:, s0 : s0 + P],
-                rhs=words,
-                rhs_scale=scale,
-                start=(a == 0),
-                stop=False,
+                out=acc, lhsT=lhsT, lhsT_scale=lhsT_scale, rhs=words, rhs_scale=scale, start=start, stop=stop
             )
 
-        def delta_pass(c, w, h, a):
-            words, scale = moving(c, a)
-            nc.tensor.matmul_mx(
-                out=bank[c, w, h][:],
-                lhsT=codes[w, a][:, h * P : (h + 1) * P].bitcast(FP8X4),
-                lhsT_scale=dscale[w, a][:, h * P : (h + 1) * P],
-                rhs=words,
-                rhs_scale=scale,
-                start=False,
-                stop=(a == PASSES - 1),
-            )
+        def open_bank(j0, n, w, h, slot):
+            bank[j0, w, h] = psum.tile([P, n], F32, name=f"bank{j0}_{w}{h}", tag=f"bank{slot}")
 
-        def cols_of(c):
-            return slice((c % 2) * CH, (c % 2 + 1) * CH)
+        first_banks = [(0, KEY, 0), (0, KEY, 1), (1, KEY, 0), (0, VALUE, 0), (0, VALUE, 1), (1, KEY, 1)]
+        first_banks = first_banks + [(1, VALUE, 0), (1, VALUE, 1)]
 
-        def make_gates(c):
-            for h in range(HALVES):
-                tag = f"gate2{h}" if c == CHUNKS - 1 else f"pre{c}{h}"
-                pre = keep.tile([P, CH], F32, name=f"pre{c}{h}", tag=tag, align_bytes=64)
-                nc.vector.tensor_tensor(pre[:], st_t[c // 2][:, h, cols_of(c)], bank[c, KEY, h][:], MULT)
-                gate[c, h] = keep.tile([P, CH], F32, name=f"gate{c}{h}", tag=f"gate{c}{h}", align_bytes=64)
-                nc.scalar.activation(gate[c, h][:], pre[:], SIGMOID, bias=bias[:, h : h + 1])
-
-        def gated(c, h, cols):
-            if cols.start == 0:
-                prod[c, h] = keep.tile([P, CH], F32, name=f"prod{c}{h}")
-            nc.vector.tensor_tensor(prod[c, h][:, cols], gate[c, h][:, cols], bank[c, VALUE, h][:, cols], MULT)
-
-        def add_store(c, h, cols, engine, total=None):
-            if total is None:
-                total = keep.tile([P, cols.stop - cols.start], F32, name=f"o{c}{h}{cols.start}")[:]
-            j0 = (c % 2) * CH
-            engine.tensor_tensor(total, prod[c, h][:, cols], res_t[c // 2][:, h, j0 + cols.start : j0 + cols.stop], ADD)
-            nc.sync.dma_start(out[h * P : (h + 1) * P, c * CH + cols.start : c * CH + cols.stop], total)
-
-        raw_bytes = PACK * N * 4
-        with tc.tile_pool(name="window", bufs=1, side="right") as window:
-            srows = window.tile([P, T], U8, name="srows", align_bytes=64)
-            nc.sync.dma_start(srows[:].bitcast(I32)[ROWS0:P, :], compact(tab_scales))
-            nc.sync.dma_start(offsets[:], offs)
-            nc.sync.dma_start(table[:], tab_words[0].rearrange("p t i -> p (t i)").bitcast(I32))
-            for w, scales in ((KEY, wk4_scales), (VALUE, wv4_scales)):
-                cols = slice((CH + w * N) // 4, (CH + (w + 1) * N) // 4)
-                nc.scalar.dma_start(stage[:].bitcast(I32)[ROWS0:P, cols], compact(scales))
-            load_base(keep.tile([P, PASSES * 2 * N], U8, name="w4k", align_bytes=64), KEY, wk4_words)
-            warm = keep.tile([P, 2], F32, name="warm")
-            nc.gpsimd.memset(warm[:, 0:1], 0.0)
-            nc.scalar.activation(warm[:, 1:2], warm[:, 0:1], SIGMOID)
-            nc.vector.memset(srows[:].bitcast(I32)[0:ROWS0, :], 0)
-            nc.vector.memset(planes[:].bitcast(I32), 0)
-            nc.gpsimd.memset(planes_rest[:].bitcast(I32), 0)
-
-            shared = ctx.enter_context(tc.tile_pool(name="shared", bufs=1))
-
-            def shared_tile(name, shape, dtype, offset):
-                return shared.tile(shape, dtype, name=name, align_bytes=64, offset=offset)
-
-            rows0 = shared_tile("rows0", [P, CH], U8, 768)
-            nc.vector.tensor_copy(rows0[:], srows[:].indirect(entries(0)))
-            nc.vector.tensor_copy(stage[:].bitcast(I32)[:, 0 : CH // 4], rows0[:].bitcast(I32))
-            spread(planes, stage)
-            load_delta(shared_tile("raw00", [P, PACK, N], F32, 1024), KEY, wkd, 0)
-            load_base(shared_tile("w4v", [P, PASSES * 2 * N], U8, 0), VALUE, wv4_words)
-            rows_rest = shared_tile("rows_rest", [P, rest_w], U8, 1024 + raw_bytes)
-            for c in range(1, CHUNKS):
-                nc.vector.tensor_copy(rows_rest[:, (c - 1) * CH : c * CH], srows[:].indirect(entries(c)))
-            spread(planes_rest, rows_rest)
-        late = ctx.enter_context(tc.tile_pool(name="late", bufs=1, side="right"))
-        for w, wd, a in ((KEY, wkd, 1), (VALUE, wvd, 0), (VALUE, wvd, 1)):
-            load_delta(late.tile([P, PACK, N], F32, name=f"raw{w}{a}", tag=f"raw{w}{a}", align_bytes=64), w, wd, a)
-        load_rows(late.tile([P, HALVES, PAIR], F32, name="st0"), st_t, st, 0)
-        bias = late.tile([P, HALVES], F32, name="bias")
-        with nc.allow_non_contiguous_dma(reason="one bias value a partition"):
-            nc.sync.dma_start(bias[:], b.rearrange("(h p) -> p h", p=P))
-        load_rows(late.tile([P, HALVES, PAIR], F32, name="res0"), res_t, res, 0)
-        load_rows(late.tile([P, HALVES, PAIR], F32, name="st1"), st_t, st, 1)
-        load_rows(late.tile([P, HALVES, PAIR], F32, name="res1"), res_t, res, 1)
-
-        spare = psum.tile([P, CH], F32, name="spare", tag="bank7")
-        for i in range(WARM_PASSES):
-            nc.tensor.matmul_mx(
-                out=spare[:],
-                lhsT=rows_rest[:, CH : CH + 2 * P].bitcast(FP4X4),
-                lhsT_scale=rows_rest[:, 0:P],
-                rhs=rows_rest[:, 0 : 2 * CH].bitcast(FP4X4),
-                rhs_scale=rows_rest[:, 0:CH],
-                start=True,
-                stop=True,
-            )
-
-        def base_passes(c):
+        def first_words(c):
+            j0 = c * CH
+            parted[c] = keep.tile([P, PASSES * 2 * CH], U8, name=f"parted{c}", align_bytes=64)
+            halves = [placed(f"picked{c}{u}", [P, HC], U32, (1 + u) * KIB) for u in range(2)]
+            for u in range(2):
+                gather_words(halves[u], j0 + u * HC, HC)
+            for u in range(2):
+                part_words(halves[u], j0 + u * HC, HC, (c, u) == (0, 0))
             for w in (KEY, VALUE):
+                for h in range(HALVES):
+                    open_bank(j0, CH, w, h, first_banks.index((c, w, h)))
+            for u in range(2):
                 for a in range(PASSES):
                     for h in range(HALVES):
-                        base_pass(c, w, h, a)
-
-        gather_words(0, keep.tile([P, CH], U32, name="picked0", align_bytes=64))
-        part_words(0, keep.tile([P, PASSES * 2 * CH], U8, name="parted0", align_bytes=64), True)
-        base_passes(0)
-        gather_words(1, keep.tile([P, CH], U32, name="picked1", tag="stage", align_bytes=64))
-        quantise(KEY, 0)
-        for h in range(HALVES):
-            delta_pass(0, KEY, h, 0)
-        part_words(1, shared_tile("parted1", [P, PASSES * 2 * CH], U8, 1024), True)
-        base_passes(1)
-        gather_words(2, shared_tile("picked2", [P, CH], U32, 1024 + 4 * CH))
-        quantise(KEY, 1)
-        gather_words(3, late.tile([P, CH], U32, name="picked3", tag="raw01", align_bytes=64))
-        quantise(VALUE, 0)
-        part_words(2, late.tile([P, PASSES * 2 * CH], U8, name="parted2", tag="raw10", align_bytes=64), False)
-        quantise(VALUE, 1)
-        part_words(3, late.tile([P, PASSES * 2 * CH], U8, name="parted3", tag="raw11", align_bytes=64), False)
-
-        whole = slice(0, CH)
-
-        for w in (KEY, VALUE):
+                        acc = bank[j0, KEY, h][:, u * HC : (u + 1) * HC]
+                        one_pass(acc, KEY, h, a, False, j0 + u * HC, HC, start=(u, a) == (0, 0))
             for a in range(PASSES):
-                for c in range(2):
-                    for h in range(HALVES):
-                        if (c, w, a) != (0, KEY, 0):
-                            delta_pass(c, w, h, a)
-        for c in range(2):
-            make_gates(c)
-        for c in range(2):
-            for h in range(HALVES):
-                gated(c, h, whole)
-                if c == 0:
-                    add_store(c, h, whole, nc.gpsimd)
+                for h in range(HALVES):
+                    one_pass(bank[j0, VALUE, h][:], VALUE, h, a, False, j0, CH, start=a == 0)
 
-        def all_passes(c, w):
-            for h in range(HALVES):
-                for a in range(PASSES):
-                    base_pass(c, w, h, a)
-                for a in range(PASSES):
-                    delta_pass(c, w, h, a)
+        def first_deltas(w, a):
+            for c in range(2):
+                for h in range(HALVES):
+                    one_pass(bank[c * CH, w, h][:], w, h, a, True, c * CH, CH, stop=a == PASSES - 1)
 
-        all_passes(2, KEY)
-        make_gates(2)
-        all_passes(2, VALUE)
-        after_values = keep.tile([P, CH], F32, name="after_values", tag="pre21", align_bytes=64)
-        for h, total in enumerate((st_t[1][:, 0, cols_of(2)], after_values[:])):
-            add_store(1, h, whole, nc.vector, total=total)
-            gated(2, h, whole)
+        first_words(0)
+        first_words(1)
+        picked2 = placed("picked2", [P, CH], U32, 0)
+        gather_words(picked2, 2 * CH, CH)
+        quantise(KEY, 0)
+        first_deltas(KEY, 0)
+        parted[2] = late.tile([P, PASSES * 2 * CH], U8, name="parted2", tag="raw00", align_bytes=64)
+        part_words(picked2, 2 * CH, CH, False)
+        quantise(KEY, 1)
+        first_deltas(KEY, 1)
+        picked3 = late.tile([P, CH], U32, name="picked3", tag="raw01", align_bytes=64)
+        gather_words(picked3, 3 * CH, CH)
+        quantise(VALUE, 0)
+        first_deltas(VALUE, 0)
+        parted[3] = late.tile([P, PASSES * 2 * CH], U8, name="parted3", tag="raw10", align_bytes=64)
+        part_words(picked3, 3 * CH, CH, False)
+        quantise(VALUE, 1)
+        first_deltas(VALUE, 1)
+
+        def make_gate(j0, n, h, pre=None):
+            if pre is None:
+                pre = keep.tile([P, n], F32, name=f"pre{j0}_{h}")
+            nc.vector.tensor_tensor(pre[:], rows_of(st_of, j0, n, h), bank[j0, KEY, h][:], MULT)
+            gate[j0, h] = keep.tile([P, n], F32, name=f"gate{j0}_{h}")
+            nc.scalar.activation(gate[j0, h][:], pre[:], SIGMOID, bias=bias[:, h : h + 1])
+
+        def gated(j0, n, h, tile=None, g0=None):
+            if tile is None:
+                tile = keep.tile([P, n], F32, name=f"prod{j0}_{h}")
+            prod[j0, h] = tile
+            g0 = j0 if g0 is None else g0
+            nc.vector.tensor_tensor(tile[:], gate[g0, h][:, j0 - g0 : j0 - g0 + n], bank[j0, VALUE, h][:], MULT)
+
+        def add_store(j0, n, h, engine, total=None):
+            if total is None:
+                total = keep.tile([P, n], F32, name=f"total{j0}_{h}")
+            engine.tensor_tensor(total[:], prod[j0, h][:], rows_of(res_of, j0, n, h), ADD)
+            nc.sync.dma_start(out[h * P : (h + 1) * P, j0 : j0 + n], total[:])
+
+        def whole_sum(j0, n, w, h, slot):
+            open_bank(j0, n, w, h, slot)
+            for delta in (False, True):
+                for a in range(PASSES):
+                    first, last = (delta, a) == (False, 0), (delta, a) == (True, PASSES - 1)
+                    one_pass(bank[j0, w, h][:], w, h, a, delta, j0, n, start=first, stop=last)
+
+        for c, w, h in first_banks:
+            if w == KEY:
+                pre = None
+                if (c, h) == (0, 0):
+                    pre = late.tile([P, CH], F32, name="pre00", tag="raw11", align_bytes=64)
+                make_gate(c * CH, CH, h, pre)
+            else:
+                gated(c * CH, CH, h)
+                if (c, h) != (1, 1):
+                    add_store(c * CH, CH, h, nc.gpsimd)
+
+        j2, ja, jb = 2 * CH, 3 * CH, 3 * CH + HC
+        whole_sum(j2, CH, KEY, 0, 0)
+        make_gate(j2, CH, 0)
+        whole_sum(j2, CH, KEY, 1, 1)
+        make_gate(j2, CH, 1, placed("pre21", [P, CH], F32, 4 * KIB))
+        whole_sum(j2, CH, VALUE, 0, 2)
+        gated(j2, CH, 0, placed("prod20", [P, CH], F32, 8 * KIB))
+        add_store(CH, CH, 1, nc.vector, placed("total11", [P, CH], F32, 4 * KIB))
+        add_store(j2, CH, 0, nc.gpsimd)
+        whole_sum(j2, CH, VALUE, 1, 3)
+        gated(j2, CH, 1)
+
+        whole_sum(ja, HC, KEY, 0, 4)
+        make_gate(ja, HC, 0, placed("preA0", [P, HC], F32, 10 * KIB))
+        whole_sum(ja, HC, KEY, 1, 5)
+        make_gate(ja, HC, 1)
+        add_store(j2, CH, 1, nc.vector, placed("total21", [P, CH], F32, 9 * KIB))
+        whole_sum(ja, HC, VALUE, 0, 6)
+        gated(ja, HC, 0)
+        add_store(ja, HC, 0, nc.gpsimd)
+        whole_sum(ja, HC, VALUE, 1, 7)
+        gated(ja, HC, 1, placed("prodA1", [P, HC], F32, 12 * KIB))
+        add_store(ja, HC, 1, nc.gpsimd)
         for h in range(HALVES):
-            add_store(2, h, whole, nc.gpsimd)
-        all_passes(3, KEY)
-        make_gates(3)
-        all_passes(3, VALUE)
-        parts = [slice(0, CH // 2), slice(CH // 2, CH)]
-        for h in range(HALVES):
-            for cols in parts:
-                gated(3, h, cols)
-            for cols in parts:
-                add_store(3, h, cols, nc.vector)
+            whole_sum(jb, HC, KEY, h, h)
+            make_gate(jb, HC, h)
+        whole_sum(jb, HC, VALUE, 0, 2)
+        gated(jb, HC, 0)
+        whole_sum(jb, P, VALUE, 1, 3)
+        gated(jb, P, 1)
+        add_store(jb, HC, 0, nc.vector, placed("totalB0", [P, HC], F32, 12 * KIB))
+        whole_sum(jb + P, P, VALUE, 1, 4)
+        gated(jb + P, P, 1, g0=jb)
+        add_store(jb, P, 1, nc.vector)
+        add_store(jb + P, P, 1, nc.vector)

@@ -29,8 +29,10 @@ GROUP = 16
 QUADRANT = 32
 LIVE = 4
 ROWS0 = P - QUADRANT
+BLOCKS = K_PASS // 32
+STAGE0 = 16
 KEY, VALUE = 0, 1
-WARM_PASSES = 6
+WARM_PASSES = 5
 KIB = 1024
 
 
@@ -49,12 +51,16 @@ def tile_list_engram_dl_dl_bsig_kernel(
         def compact(scales):
             return scales.bitcast(I32).rearrange("a q n -> q a n")
 
-        def spread(planes, rows):
-            dst = planes[:].bitcast(I32).rearrange("p (a n) -> p a n", a=PASSES)
-            src = rows[:].bitcast(I32)
-            for q in (0, 2, 1, 3):
-                first = ROWS0 + q * LIVE * PASSES
-                nc.sync.dma_start(dst[q * QUADRANT : q * QUADRANT + LIVE], src[first : first + LIVE * PASSES, :])
+        def blocks(tile):
+            return tile[:].bitcast(I32).rearrange("p (a n) -> p a n", a=PASSES)[STAGE0 : STAGE0 + BLOCKS]
+
+        def join(staged, rows, width):
+            nc.scalar.dma_start(blocks(staged)[:, :, 0 : width // 4], rows[:].bitcast(I32)[ROWS0:P, :])
+
+        def spread(planes, staged):
+            for r in range(LIVE):
+                src = staged[:].bitcast(I32)[STAGE0 + r : STAGE0 + BLOCKS : LIVE, :]
+                nc.sync.dma_start(planes[:].bitcast(I32)[r:P:QUADRANT, :], src)
 
         def entries(j0, n):
             return offsets[:, j0 // GROUP : (j0 + n) // GROUP]
@@ -63,7 +69,8 @@ def tile_list_engram_dl_dl_bsig_kernel(
         table = keep.tile([P, T], I32, name="table", align_bytes=64)
         srows = keep.tile([P, T], U8, name="srows", align_bytes=64)
         first_w = PAIR + 2 * N
-        stage = keep.tile([P, first_w], U8, name="stage", align_bytes=64)
+        stage = keep.tile([P, PASSES * first_w], U8, name="stage", align_bytes=64)
+        stage2 = keep.tile([P, PASSES * PAIR], U8, name="stage2", align_bytes=64)
         planes = keep.tile([P, PASSES * first_w], U8, name="planes", align_bytes=64)
         planes2 = keep.tile([P, PASSES * PAIR], U8, name="planes2", align_bytes=64)
         w4, raw, st_of, res_of = {}, {}, {}, {}
@@ -91,42 +98,42 @@ def tile_list_engram_dl_dl_bsig_kernel(
         nc.sync.dma_start(table[:], tab_words[0].rearrange("p t i -> p (t i)").bitcast(I32))
         for w, scales in ((KEY, wk4_scales), (VALUE, wv4_scales)):
             cols = slice((PAIR + w * N) // 4, (PAIR + (w + 1) * N) // 4)
-            nc.scalar.dma_start(stage[:].bitcast(I32)[ROWS0:P, cols], compact(scales))
+            nc.scalar.dma_start(blocks(stage)[:, :, cols], compact(scales))
         load_base(keep, KEY, wk4_words)
+        load_base(keep, VALUE, wv4_words)
         warm = keep.tile([P, 2], F32, name="warm")
         nc.gpsimd.memset(warm[:, 0:1], 0.0)
         nc.scalar.activation(warm[:, 1:2], warm[:, 0:1], SIGMOID)
         nc.vector.memset(srows[:].bitcast(I32)[0:ROWS0, :], 0)
+        b_rows = keep.tile([P, HALVES * QUADRANT], F32, name="b_rows", align_bytes=64)
+        nc.vector.memset(b_rows[:], 0.0)
+        nc.sync.dma_start(
+            b_rows[0:P:QUADRANT, :].rearrange("q (h c) -> q h c", h=HALVES),
+            b.rearrange("(h q c) -> q h c", h=HALVES, c=QUADRANT),
+        )
         nc.vector.memset(planes[:].bitcast(I32), 0)
         nc.gpsimd.memset(planes2[:].bitcast(I32), 0)
 
-        rows0 = keep.tile([P, CH], U8, name="rows0", align_bytes=64)
         rows23 = keep.tile([P, PAIR], U8, name="rows23", align_bytes=64)
         with tc.tile_pool(name="window", bufs=1, side="right") as window:
-            rows1 = window.tile([P, CH], U8, name="rows1", align_bytes=64)
-            nc.vector.tensor_copy(rows0[:], srows[:].indirect(entries(0, CH)))
-            nc.vector.tensor_copy(rows1[:], srows[:].indirect(entries(CH, CH)))
-            nc.vector.tensor_copy(stage[:].bitcast(I32)[:, 0 : CH // 4], rows0[:].bitcast(I32))
-            nc.vector.tensor_copy(rows23[:, 0:CH], srows[:].indirect(entries(2 * CH, CH)))
-            nc.vector.tensor_copy(stage[:].bitcast(I32)[:, CH // 4 : PAIR // 4], rows1[:].bitcast(I32))
-            nc.vector.tensor_copy(rows23[:, CH:PAIR], srows[:].indirect(entries(3 * CH, CH)))
+            rows01 = window.tile([P, PAIR], U8, name="rows01", align_bytes=64)
+            nc.vector.tensor_copy(rows01[:], srows[:].indirect(entries(0, PAIR)))
+            join(stage, rows01, PAIR)
+            for c in range(2):
+                nc.vector.tensor_copy(rows23[:, c * CH : (c + 1) * CH], srows[:].indirect(entries(PAIR + c * CH, CH)))
+            join(stage2, rows23, PAIR)
             spread(planes, stage)
         late = ctx.enter_context(tc.tile_pool(name="late", bufs=1, side="right"))
-        load_base(late, VALUE, wv4_words)
         for w, wd in ((KEY, wkd), (VALUE, wvd)):
             for a in range(PASSES):
                 raw[w, a] = late.tile([P, PACK, N], F32, name=f"raw{w}{a}", tag=f"raw{w}{a}", align_bytes=64)
                 rows = wd[a * K_PASS : (a + 1) * K_PASS, :]
                 nc.sync.dma_start(raw[w, a][:], rows.rearrange("(p i) n -> p i n", i=PACK))
         load_rows("st01", st_of, st, 0, 2)
-        bias = late.tile([P, HALVES], F32, name="bias")
-        with nc.allow_non_contiguous_dma(reason="one bias value a partition"):
-            nc.sync.dma_start(bias[:], b.rearrange("(h p) -> p h", p=P))
-        spread(planes2, rows23)
+        spread(planes2, stage2)
         load_rows("res0", res_of, res, 0, 1)
-        load_rows("st2", st_of, st, 2, 1)
+        load_rows("st23", st_of, st, 2, 2)
         load_rows("res1", res_of, res, 1, 1)
-        load_rows("st3", st_of, st, 3, 1)
         load_rows("res2", res_of, res, 2, 1)
         load_rows("res3", res_of, res, 3, 1)
 
@@ -134,10 +141,10 @@ def tile_list_engram_dl_dl_bsig_kernel(
         for i in range(WARM_PASSES):
             nc.tensor.matmul_mx(
                 out=spare[:],
-                lhsT=stage[:, 0 : 2 * P].bitcast(FP4X4),
-                lhsT_scale=stage[:, 0:P],
+                lhsT=rows23[:, 0 : 2 * P].bitcast(FP4X4),
+                lhsT_scale=rows23[:, 0:P],
                 rhs=srows[:, 0 : 2 * CH].bitcast(FP4X4),
-                rhs_scale=stage[:, 0:CH],
+                rhs_scale=rows23[:, 0:CH],
                 start=True,
                 stop=True,
             )
@@ -156,7 +163,7 @@ def tile_list_engram_dl_dl_bsig_kernel(
                 nc.vector.tensor_copy(dst, src)
 
         def quantise(w, a):
-            grouped = keep.tile([P, PACK * N], BF16, name=f"grouped{w}{a}", align_bytes=64)
+            grouped = keep.tile([P, PACK * N], BF16, name=f"grouped{w}{a}", tag=f"grouped{w}{a}", align_bytes=64)
             nc.scalar.copy(
                 grouped[:].rearrange("p (m u i) -> p m i u", u=4, i=PACK),
                 raw[w, a][:].rearrange("p i (m u) -> p m i u", u=4),
@@ -187,7 +194,7 @@ def tile_list_engram_dl_dl_bsig_kernel(
         def open_bank(j0, n, w, h, slot):
             bank[j0, w, h] = psum.tile([P, n], F32, name=f"bank{j0}_{w}{h}", tag=f"bank{slot}")
 
-        first_banks = [(0, KEY, 0), (0, KEY, 1), (1, KEY, 0), (0, VALUE, 0), (0, VALUE, 1), (1, KEY, 1)]
+        first_banks = [(0, KEY, 0), (0, KEY, 1), (1, KEY, 0), (0, VALUE, 0), (1, KEY, 1), (0, VALUE, 1)]
         first_banks = first_banks + [(1, VALUE, 0), (1, VALUE, 1)]
 
         def first_words(c):
@@ -197,7 +204,7 @@ def tile_list_engram_dl_dl_bsig_kernel(
             for u in range(2):
                 gather_words(halves[u], j0 + u * HC, HC)
             for u in range(2):
-                part_words(halves[u], j0 + u * HC, HC, (c, u) == (0, 0))
+                part_words(halves[u], j0 + u * HC, HC, True)
             for w in (KEY, VALUE):
                 for h in range(HALVES):
                     open_bank(j0, CH, w, h, first_banks.index((c, w, h)))
@@ -223,6 +230,10 @@ def tile_list_engram_dl_dl_bsig_kernel(
         first_deltas(KEY, 0)
         parted[2] = late.tile([P, PASSES * 2 * CH], U8, name="parted2", tag="raw00", align_bytes=64)
         part_words(picked2, 2 * CH, CH, False)
+        bias = keep.tile([P, HALVES * QUADRANT], F32, name="bias", tag="grouped00", align_bytes=64)
+        for h in range(HALVES):
+            cols = slice(h * QUADRANT, (h + 1) * QUADRANT)
+            nc.vector.transpose(bias[:, cols], b_rows[:, cols])
         quantise(KEY, 1)
         first_deltas(KEY, 1)
         picked3 = late.tile([P, CH], U32, name="picked3", tag="raw01", align_bytes=64)
@@ -239,7 +250,7 @@ def tile_list_engram_dl_dl_bsig_kernel(
                 pre = keep.tile([P, n], F32, name=f"pre{j0}_{h}")
             nc.vector.tensor_tensor(pre[:], rows_of(st_of, j0, n, h), bank[j0, KEY, h][:], MULT)
             gate[j0, h] = keep.tile([P, n], F32, name=f"gate{j0}_{h}")
-            nc.scalar.activation(gate[j0, h][:], pre[:], SIGMOID, bias=bias[:, h : h + 1])
+            nc.scalar.activation(gate[j0, h][:], pre[:], SIGMOID, bias=bias[:, h * QUADRANT : h * QUADRANT + 1])
 
         def gated(j0, n, h, tile=None, g0=None):
             if tile is None:
@@ -269,41 +280,30 @@ def tile_list_engram_dl_dl_bsig_kernel(
                 make_gate(c * CH, CH, h, pre)
             else:
                 gated(c * CH, CH, h)
-                if (c, h) != (1, 1):
+                if c == 0:
                     add_store(c * CH, CH, h, nc.gpsimd)
 
-        j2, ja, jb = 2 * CH, 3 * CH, 3 * CH + HC
+        j2, j3 = 2 * CH, 3 * CH
         whole_sum(j2, CH, KEY, 0, 0)
         make_gate(j2, CH, 0)
         whole_sum(j2, CH, KEY, 1, 1)
         make_gate(j2, CH, 1, placed("pre21", [P, CH], F32, 4 * KIB))
+        add_store(CH, CH, 0, nc.vector, rows_of(st_of, j2, CH, 0))
         whole_sum(j2, CH, VALUE, 0, 2)
-        gated(j2, CH, 0, placed("prod20", [P, CH], F32, 8 * KIB))
+        gated(j2, CH, 0)
         add_store(CH, CH, 1, nc.vector, placed("total11", [P, CH], F32, 4 * KIB))
         add_store(j2, CH, 0, nc.gpsimd)
         whole_sum(j2, CH, VALUE, 1, 3)
         gated(j2, CH, 1)
+        add_store(j2, CH, 1, nc.gpsimd)
 
-        whole_sum(ja, HC, KEY, 0, 4)
-        make_gate(ja, HC, 0, placed("preA0", [P, HC], F32, 10 * KIB))
-        whole_sum(ja, HC, KEY, 1, 5)
-        make_gate(ja, HC, 1)
-        add_store(j2, CH, 1, nc.vector, placed("total21", [P, CH], F32, 9 * KIB))
-        whole_sum(ja, HC, VALUE, 0, 6)
-        gated(ja, HC, 0)
-        add_store(ja, HC, 0, nc.gpsimd)
-        whole_sum(ja, HC, VALUE, 1, 7)
-        gated(ja, HC, 1, placed("prodA1", [P, HC], F32, 12 * KIB))
-        add_store(ja, HC, 1, nc.gpsimd)
         for h in range(HALVES):
-            whole_sum(jb, HC, KEY, h, h)
-            make_gate(jb, HC, h)
-        whole_sum(jb, HC, VALUE, 0, 2)
-        gated(jb, HC, 0)
-        whole_sum(jb, P, VALUE, 1, 3)
-        gated(jb, P, 1)
-        add_store(jb, HC, 0, nc.vector, placed("totalB0", [P, HC], F32, 12 * KIB))
-        whole_sum(jb + P, P, VALUE, 1, 4)
-        gated(jb + P, P, 1, g0=jb)
-        add_store(jb, P, 1, nc.vector)
-        add_store(jb + P, P, 1, nc.vector)
+            whole_sum(j3, CH, KEY, h, 4 + h)
+            make_gate(j3, CH, h)
+        pieces = [(h, j3 + u * HC) for h in range(HALVES) for u in range(2)]
+        for i, (h, j0) in enumerate(pieces):
+            whole_sum(j0, HC, VALUE, h, (6 + i) % 8)
+            gated(j0, HC, h, g0=j3)
+            if i > 0:
+                add_store(pieces[i - 1][1], HC, pieces[i - 1][0], nc.vector)
+        add_store(j3 + HC, HC, 1, nc.vector)

@@ -29,8 +29,6 @@ GROUP = 16
 QUADRANT = 32
 LIVE = 4
 ROWS0 = P - QUADRANT
-BLOCKS = K_PASS // 32
-STAGE0 = 16
 KEY, VALUE = 0, 1
 WARM_PASSES = 5
 KIB = 1024
@@ -51,16 +49,12 @@ def tile_list_engram_dl_dl_bsig_kernel(
         def compact(scales):
             return scales.bitcast(I32).rearrange("a q n -> q a n")
 
-        def blocks(tile):
-            return tile[:].bitcast(I32).rearrange("p (a n) -> p a n", a=PASSES)[STAGE0 : STAGE0 + BLOCKS]
-
-        def join(staged, rows, width):
-            nc.scalar.dma_start(blocks(staged)[:, :, 0 : width // 4], rows[:].bitcast(I32)[ROWS0:P, :])
-
-        def spread(planes, staged):
-            for r in range(LIVE):
-                src = staged[:].bitcast(I32)[STAGE0 + r : STAGE0 + BLOCKS : LIVE, :]
-                nc.sync.dma_start(planes[:].bitcast(I32)[r:P:QUADRANT, :], src)
+        def spread(planes, rows):
+            dst = planes[:].bitcast(I32).rearrange("p (a n) -> p a n", a=PASSES)
+            src = rows[:].bitcast(I32)
+            for q in (0, 2, 1, 3):
+                first = ROWS0 + q * LIVE * PASSES
+                nc.sync.dma_start(dst[q * QUADRANT : q * QUADRANT + LIVE], src[first : first + LIVE * PASSES, :])
 
         def entries(j0, n):
             return offsets[:, j0 // GROUP : (j0 + n) // GROUP]
@@ -69,8 +63,7 @@ def tile_list_engram_dl_dl_bsig_kernel(
         table = keep.tile([P, T], I32, name="table", align_bytes=64)
         srows = keep.tile([P, T], U8, name="srows", align_bytes=64)
         first_w = PAIR + 2 * N
-        stage = keep.tile([P, PASSES * first_w], U8, name="stage", align_bytes=64)
-        stage2 = keep.tile([P, PASSES * PAIR], U8, name="stage2", align_bytes=64)
+        stage = keep.tile([P, first_w], U8, name="stage", align_bytes=64)
         planes = keep.tile([P, PASSES * first_w], U8, name="planes", align_bytes=64)
         planes2 = keep.tile([P, PASSES * PAIR], U8, name="planes2", align_bytes=64)
         w4, raw, st_of, res_of = {}, {}, {}, {}
@@ -98,7 +91,7 @@ def tile_list_engram_dl_dl_bsig_kernel(
         nc.sync.dma_start(table[:], tab_words[0].rearrange("p t i -> p (t i)").bitcast(I32))
         for w, scales in ((KEY, wk4_scales), (VALUE, wv4_scales)):
             cols = slice((PAIR + w * N) // 4, (PAIR + (w + 1) * N) // 4)
-            nc.scalar.dma_start(blocks(stage)[:, :, cols], compact(scales))
+            nc.scalar.dma_start(stage[:].bitcast(I32)[ROWS0:P, cols], compact(scales))
         load_base(keep, KEY, wk4_words)
         load_base(keep, VALUE, wv4_words)
         warm = keep.tile([P, 2], F32, name="warm")
@@ -114,14 +107,16 @@ def tile_list_engram_dl_dl_bsig_kernel(
         nc.vector.memset(planes[:].bitcast(I32), 0)
         nc.gpsimd.memset(planes2[:].bitcast(I32), 0)
 
+        rows0 = keep.tile([P, CH], U8, name="rows0", align_bytes=64)
         rows23 = keep.tile([P, PAIR], U8, name="rows23", align_bytes=64)
         with tc.tile_pool(name="window", bufs=1, side="right") as window:
-            rows01 = window.tile([P, PAIR], U8, name="rows01", align_bytes=64)
-            nc.vector.tensor_copy(rows01[:], srows[:].indirect(entries(0, PAIR)))
-            join(stage, rows01, PAIR)
-            for c in range(2):
-                nc.vector.tensor_copy(rows23[:, c * CH : (c + 1) * CH], srows[:].indirect(entries(PAIR + c * CH, CH)))
-            join(stage2, rows23, PAIR)
+            rows1 = window.tile([P, CH], U8, name="rows1", align_bytes=64)
+            nc.vector.tensor_copy(rows0[:], srows[:].indirect(entries(0, CH)))
+            nc.vector.tensor_copy(rows1[:], srows[:].indirect(entries(CH, CH)))
+            nc.vector.tensor_copy(stage[:].bitcast(I32)[:, 0 : CH // 4], rows0[:].bitcast(I32))
+            nc.vector.tensor_copy(rows23[:, 0:CH], srows[:].indirect(entries(2 * CH, CH)))
+            nc.vector.tensor_copy(stage[:].bitcast(I32)[:, CH // 4 : PAIR // 4], rows1[:].bitcast(I32))
+            nc.vector.tensor_copy(rows23[:, CH:PAIR], srows[:].indirect(entries(3 * CH, CH)))
             spread(planes, stage)
         late = ctx.enter_context(tc.tile_pool(name="late", bufs=1, side="right"))
         for w, wd in ((KEY, wkd), (VALUE, wvd)):
@@ -130,7 +125,7 @@ def tile_list_engram_dl_dl_bsig_kernel(
                 rows = wd[a * K_PASS : (a + 1) * K_PASS, :]
                 nc.sync.dma_start(raw[w, a][:], rows.rearrange("(p i) n -> p i n", i=PACK))
         load_rows("st01", st_of, st, 0, 2)
-        spread(planes2, stage2)
+        spread(planes2, rows23)
         load_rows("res0", res_of, res, 0, 1)
         load_rows("st23", st_of, st, 2, 2)
         load_rows("res1", res_of, res, 1, 1)

@@ -30,7 +30,7 @@ QUADRANT = 32
 LIVE = 4
 ROWS0 = P - QUADRANT
 KEY, VALUE = 0, 1
-WARM_PASSES = 5
+WARM_PASSES = 6
 KIB = 1024
 
 
@@ -63,7 +63,7 @@ def tile_list_engram_dl_dl_bsig_kernel(
         table = keep.tile([P, T], I32, name="table", align_bytes=64)
         srows = keep.tile([P, T], U8, name="srows", align_bytes=64)
         first_w = PAIR + 2 * N
-        stage = keep.tile([P, first_w], U8, name="stage", align_bytes=64)
+        stage = keep.tile([P, first_w], U8, name="stage", tag="stage", align_bytes=64)
         planes = keep.tile([P, PASSES * first_w], U8, name="planes", align_bytes=64)
         planes2 = keep.tile([P, PASSES * PAIR], U8, name="planes2", align_bytes=64)
         w4, raw, st_of, res_of = {}, {}, {}, {}
@@ -98,24 +98,15 @@ def tile_list_engram_dl_dl_bsig_kernel(
         nc.gpsimd.memset(warm[:, 0:1], 0.0)
         nc.scalar.activation(warm[:, 1:2], warm[:, 0:1], SIGMOID)
         nc.vector.memset(srows[:].bitcast(I32)[0:ROWS0, :], 0)
-        b_rows = keep.tile([P, HALVES * QUADRANT], F32, name="b_rows", align_bytes=64)
-        nc.vector.memset(b_rows[:], 0.0)
-        nc.sync.dma_start(
-            b_rows[0:P:QUADRANT, :].rearrange("q (h c) -> q h c", h=HALVES),
-            b.rearrange("(h q c) -> q h c", h=HALVES, c=QUADRANT),
-        )
         nc.vector.memset(planes[:].bitcast(I32), 0)
         nc.gpsimd.memset(planes2[:].bitcast(I32), 0)
 
-        rows0 = keep.tile([P, CH], U8, name="rows0", align_bytes=64)
         rows23 = keep.tile([P, PAIR], U8, name="rows23", align_bytes=64)
         with tc.tile_pool(name="window", bufs=1, side="right") as window:
-            rows1 = window.tile([P, CH], U8, name="rows1", align_bytes=64)
-            nc.vector.tensor_copy(rows0[:], srows[:].indirect(entries(0, CH)))
-            nc.vector.tensor_copy(rows1[:], srows[:].indirect(entries(CH, CH)))
-            nc.vector.tensor_copy(stage[:].bitcast(I32)[:, 0 : CH // 4], rows0[:].bitcast(I32))
+            rows01 = window.tile([P, PAIR], U8, name="rows01", align_bytes=64)
+            nc.vector.tensor_copy(rows01[:], srows[:].indirect(entries(0, PAIR)))
             nc.vector.tensor_copy(rows23[:, 0:CH], srows[:].indirect(entries(2 * CH, CH)))
-            nc.vector.tensor_copy(stage[:].bitcast(I32)[:, CH // 4 : PAIR // 4], rows1[:].bitcast(I32))
+            nc.vector.tensor_copy(stage[:].bitcast(I32)[:, 0 : PAIR // 4], rows01[:].bitcast(I32))
             nc.vector.tensor_copy(rows23[:, CH:PAIR], srows[:].indirect(entries(3 * CH, CH)))
             spread(planes, stage)
         late = ctx.enter_context(tc.tile_pool(name="late", bufs=1, side="right"))
@@ -125,6 +116,9 @@ def tile_list_engram_dl_dl_bsig_kernel(
                 rows = wd[a * K_PASS : (a + 1) * K_PASS, :]
                 nc.sync.dma_start(raw[w, a][:], rows.rearrange("(p i) n -> p i n", i=PACK))
         load_rows("st01", st_of, st, 0, 2)
+        bias = late.tile([P, HALVES], F32, name="bias")
+        with nc.allow_non_contiguous_dma(reason="one bias value a partition"):
+            nc.sync.dma_start(bias[:], b.rearrange("(h p) -> p h", p=P))
         spread(planes2, rows23)
         load_rows("res0", res_of, res, 0, 1)
         load_rows("st23", st_of, st, 2, 2)
@@ -158,7 +152,7 @@ def tile_list_engram_dl_dl_bsig_kernel(
                 nc.vector.tensor_copy(dst, src)
 
         def quantise(w, a):
-            grouped = keep.tile([P, PACK * N], BF16, name=f"grouped{w}{a}", tag=f"grouped{w}{a}", align_bytes=64)
+            grouped = keep.tile([P, PACK * N], BF16, name=f"grouped{w}{a}", align_bytes=64)
             nc.scalar.copy(
                 grouped[:].rearrange("p (m u i) -> p m i u", u=4, i=PACK),
                 raw[w, a][:].rearrange("p i (m u) -> p m i u", u=4),
@@ -195,22 +189,15 @@ def tile_list_engram_dl_dl_bsig_kernel(
         def first_words(c):
             j0 = c * CH
             parted[c] = keep.tile([P, PASSES * 2 * CH], U8, name=f"parted{c}", align_bytes=64)
-            halves = [placed(f"picked{c}{u}", [P, HC], U32, (1 + u) * KIB) for u in range(2)]
-            for u in range(2):
-                gather_words(halves[u], j0 + u * HC, HC)
-            for u in range(2):
-                part_words(halves[u], j0 + u * HC, HC, True)
+            picked = keep.tile([P, CH], U32, name=f"picked{c}", tag=("picked0", "stage")[c], align_bytes=64)
+            gather_words(picked, j0, CH)
+            part_words(picked, j0, CH, True)
             for w in (KEY, VALUE):
-                for h in range(HALVES):
-                    open_bank(j0, CH, w, h, first_banks.index((c, w, h)))
-            for u in range(2):
                 for a in range(PASSES):
                     for h in range(HALVES):
-                        acc = bank[j0, KEY, h][:, u * HC : (u + 1) * HC]
-                        one_pass(acc, KEY, h, a, False, j0 + u * HC, HC, start=(u, a) == (0, 0))
-            for a in range(PASSES):
-                for h in range(HALVES):
-                    one_pass(bank[j0, VALUE, h][:], VALUE, h, a, False, j0, CH, start=a == 0)
+                        if a == 0:
+                            open_bank(j0, CH, w, h, first_banks.index((c, w, h)))
+                        one_pass(bank[j0, w, h][:], w, h, a, False, j0, CH, start=a == 0)
 
         def first_deltas(w, a):
             for c in range(2):
@@ -219,16 +206,12 @@ def tile_list_engram_dl_dl_bsig_kernel(
 
         first_words(0)
         first_words(1)
-        picked2 = placed("picked2", [P, CH], U32, 0)
+        picked2 = late.tile([P, CH], U32, name="picked2", tag="raw00", align_bytes=64)
         gather_words(picked2, 2 * CH, CH)
         quantise(KEY, 0)
         first_deltas(KEY, 0)
-        parted[2] = late.tile([P, PASSES * 2 * CH], U8, name="parted2", tag="raw00", align_bytes=64)
+        parted[2] = keep.tile([P, PASSES * 2 * CH], U8, name="parted2", align_bytes=64)
         part_words(picked2, 2 * CH, CH, False)
-        bias = keep.tile([P, HALVES * QUADRANT], F32, name="bias", tag="grouped00", align_bytes=64)
-        for h in range(HALVES):
-            cols = slice(h * QUADRANT, (h + 1) * QUADRANT)
-            nc.vector.transpose(bias[:, cols], b_rows[:, cols])
         quantise(KEY, 1)
         first_deltas(KEY, 1)
         picked3 = late.tile([P, CH], U32, name="picked3", tag="raw01", align_bytes=64)
@@ -245,7 +228,7 @@ def tile_list_engram_dl_dl_bsig_kernel(
                 pre = keep.tile([P, n], F32, name=f"pre{j0}_{h}")
             nc.vector.tensor_tensor(pre[:], rows_of(st_of, j0, n, h), bank[j0, KEY, h][:], MULT)
             gate[j0, h] = keep.tile([P, n], F32, name=f"gate{j0}_{h}")
-            nc.scalar.activation(gate[j0, h][:], pre[:], SIGMOID, bias=bias[:, h * QUADRANT : h * QUADRANT + 1])
+            nc.scalar.activation(gate[j0, h][:], pre[:], SIGMOID, bias=bias[:, h : h + 1])
 
         def gated(j0, n, h, tile=None, g0=None):
             if tile is None:

@@ -30,7 +30,7 @@ QUADRANT = 32
 LIVE = 4
 ROWS0 = P - QUADRANT
 KEY, VALUE = 0, 1
-WARM_PASSES = 6
+WARM_PASSES = 5
 KIB = 1024
 
 
@@ -61,11 +61,11 @@ def tile_list_engram_dl_dl_bsig_kernel(
 
         offsets = keep.tile([P, J // GROUP], U16, name="offsets")
         table = keep.tile([P, T], I32, name="table", align_bytes=64)
-        srows = keep.tile([P, T], U8, name="srows", align_bytes=64)
-        first_w = PAIR + 2 * N
+        first_w = CH + 2 * N
+        rest_w = J - CH
         stage = keep.tile([P, first_w], U8, name="stage", tag="stage", align_bytes=64)
         planes = keep.tile([P, PASSES * first_w], U8, name="planes", align_bytes=64)
-        planes2 = keep.tile([P, PASSES * PAIR], U8, name="planes2", align_bytes=64)
+        planes2 = keep.tile([P, PASSES * rest_w], U8, name="planes2", align_bytes=64)
         w4, raw, st_of, res_of = {}, {}, {}, {}
         parted, codes, dscale, bank, gate, prod = {}, {}, {}, {}, {}, {}
 
@@ -86,40 +86,50 @@ def tile_list_engram_dl_dl_bsig_kernel(
             tile, first = held[j0 // CH]
             return tile[:, h, first + j0 % CH : first + j0 % CH + n]
 
-        nc.sync.dma_start(srows[:].bitcast(I32)[ROWS0:P, :], compact(tab_scales))
-        nc.sync.dma_start(offsets[:], offs)
-        nc.sync.dma_start(table[:], tab_words[0].rearrange("p t i -> p (t i)").bitcast(I32))
-        for w, scales in ((KEY, wk4_scales), (VALUE, wv4_scales)):
-            cols = slice((PAIR + w * N) // 4, (PAIR + (w + 1) * N) // 4)
-            nc.scalar.dma_start(stage[:].bitcast(I32)[ROWS0:P, cols], compact(scales))
-        load_base(keep, KEY, wk4_words)
-        load_base(keep, VALUE, wv4_words)
-        warm = keep.tile([P, 2], F32, name="warm")
-        nc.gpsimd.memset(warm[:, 0:1], 0.0)
-        nc.scalar.activation(warm[:, 1:2], warm[:, 0:1], SIGMOID)
-        nc.vector.memset(srows[:].bitcast(I32)[0:ROWS0, :], 0)
-        nc.vector.memset(planes[:].bitcast(I32), 0)
-        nc.gpsimd.memset(planes2[:].bitcast(I32), 0)
+        def head(srows):
+            nc.sync.dma_start(srows[:].bitcast(I32)[ROWS0:P, :], compact(tab_scales))
+            nc.sync.dma_start(offsets[:], offs)
+            nc.sync.dma_start(table[:], tab_words[0].rearrange("p t i -> p (t i)").bitcast(I32))
+            for w, scales in ((KEY, wk4_scales), (VALUE, wv4_scales)):
+                cols = slice((CH + w * N) // 4, (CH + (w + 1) * N) // 4)
+                nc.scalar.dma_start(stage[:].bitcast(I32)[ROWS0:P, cols], compact(scales))
+            load_base(keep, KEY, wk4_words)
+            warm = keep.tile([P, 2], F32, name="warm")
+            nc.gpsimd.memset(warm[:, 0:1], 0.0)
+            nc.scalar.activation(warm[:, 1:2], warm[:, 0:1], SIGMOID)
+            nc.vector.memset(srows[:].bitcast(I32)[0:ROWS0, :], 0)
+            nc.vector.memset(planes[:].bitcast(I32), 0)
+            nc.gpsimd.memset(planes2[:].bitcast(I32), 0)
 
-        rows23 = keep.tile([P, PAIR], U8, name="rows23", align_bytes=64)
+        rows_rest = keep.tile([P, rest_w], U8, name="rows_rest", align_bytes=64)
+
+        def load_delta(pool, w, wd, a):
+            raw[w, a] = pool.tile([P, PACK, N], F32, name=f"raw{w}{a}", tag=f"raw{w}{a}", align_bytes=64)
+            rows = wd[a * K_PASS : (a + 1) * K_PASS, :]
+            nc.sync.dma_start(raw[w, a][:], rows.rearrange("(p i) n -> p i n", i=PACK))
+
         with tc.tile_pool(name="window", bufs=1, side="right") as window:
-            rows01 = window.tile([P, PAIR], U8, name="rows01", align_bytes=64)
-            nc.vector.tensor_copy(rows01[:], srows[:].indirect(entries(0, PAIR)))
-            nc.vector.tensor_copy(rows23[:, 0:CH], srows[:].indirect(entries(2 * CH, CH)))
-            nc.vector.tensor_copy(stage[:].bitcast(I32)[:, 0 : PAIR // 4], rows01[:].bitcast(I32))
-            nc.vector.tensor_copy(rows23[:, CH:PAIR], srows[:].indirect(entries(3 * CH, CH)))
-            spread(planes, stage)
+            srows = window.tile([P, T], U8, name="srows", align_bytes=64)
+            head(srows)
+            with tc.tile_pool(name="first", bufs=1) as first:
+                rows0 = first.tile([P, CH], U8, name="rows0", align_bytes=64)
+                nc.vector.tensor_copy(rows0[:], srows[:].indirect(entries(0, CH)))
+                nc.vector.tensor_copy(rows_rest[:, 0:CH], srows[:].indirect(entries(CH, CH)))
+                nc.vector.tensor_copy(stage[:].bitcast(I32)[:, 0 : CH // 4], rows0[:].bitcast(I32))
+                spread(planes, stage)
+            early = ctx.enter_context(tc.tile_pool(name="early", bufs=1))
+            load_delta(early, KEY, wkd, 0)
+            load_base(early, VALUE, wv4_words)
+            for c in (2, 3):
+                nc.vector.tensor_copy(rows_rest[:, (c - 1) * CH : c * CH], srows[:].indirect(entries(c * CH, CH)))
+            spread(planes2, rows_rest)
         late = ctx.enter_context(tc.tile_pool(name="late", bufs=1, side="right"))
-        for w, wd in ((KEY, wkd), (VALUE, wvd)):
-            for a in range(PASSES):
-                raw[w, a] = late.tile([P, PACK, N], F32, name=f"raw{w}{a}", tag=f"raw{w}{a}", align_bytes=64)
-                rows = wd[a * K_PASS : (a + 1) * K_PASS, :]
-                nc.sync.dma_start(raw[w, a][:], rows.rearrange("(p i) n -> p i n", i=PACK))
+        for w, wd, a in ((KEY, wkd, 1), (VALUE, wvd, 0), (VALUE, wvd, 1)):
+            load_delta(late, w, wd, a)
         load_rows("st01", st_of, st, 0, 2)
         bias = late.tile([P, HALVES], F32, name="bias")
         with nc.allow_non_contiguous_dma(reason="one bias value a partition"):
             nc.sync.dma_start(bias[:], b.rearrange("(h p) -> p h", p=P))
-        spread(planes2, rows23)
         load_rows("res0", res_of, res, 0, 1)
         load_rows("st23", st_of, st, 2, 2)
         load_rows("res1", res_of, res, 1, 1)
@@ -130,10 +140,10 @@ def tile_list_engram_dl_dl_bsig_kernel(
         for i in range(WARM_PASSES):
             nc.tensor.matmul_mx(
                 out=spare[:],
-                lhsT=rows23[:, 0 : 2 * P].bitcast(FP4X4),
-                lhsT_scale=rows23[:, 0:P],
-                rhs=srows[:, 0 : 2 * CH].bitcast(FP4X4),
-                rhs_scale=rows23[:, 0:CH],
+                lhsT=rows_rest[:, CH : CH + 2 * P].bitcast(FP4X4),
+                lhsT_scale=rows_rest[:, 0:P],
+                rhs=rows_rest[:, 0 : 2 * CH].bitcast(FP4X4),
+                rhs_scale=rows_rest[:, 0:CH],
                 start=True,
                 stop=True,
             )
@@ -152,7 +162,7 @@ def tile_list_engram_dl_dl_bsig_kernel(
                 nc.vector.tensor_copy(dst, src)
 
         def quantise(w, a):
-            grouped = keep.tile([P, PACK * N], BF16, name=f"grouped{w}{a}", align_bytes=64)
+            grouped = keep.tile([P, PACK * N], BF16, name=f"grouped{w}{a}", tag=f"grouped{w}{a}", align_bytes=64)
             nc.scalar.copy(
                 grouped[:].rearrange("p (m u i) -> p m i u", u=4, i=PACK),
                 raw[w, a][:].rearrange("p i (m u) -> p m i u", u=4),
@@ -164,16 +174,16 @@ def tile_list_engram_dl_dl_bsig_kernel(
         def one_pass(acc, w, h, a, delta, j0, n, start=False, stop=False):
             c, o = divmod(j0, CH)
             words = parted[c][:, 2 * (a * CH + o) : 2 * (a * CH + o + n)].bitcast(FP4X4)
-            if c < 2:
+            if c == 0:
                 scale = planes[:, a * first_w + j0 : a * first_w + j0 + n]
             else:
-                scale = planes2[:, a * PAIR + j0 - PAIR : a * PAIR + j0 - PAIR + n]
+                scale = planes2[:, a * rest_w + j0 - CH : a * rest_w + j0 - CH + n]
             if delta:
                 lhsT = codes[w, a][:, h * P : (h + 1) * P].bitcast(FP8X4)
                 lhsT_scale = dscale[w, a][:, h * P : (h + 1) * P]
             else:
                 n0 = a * N + h * P
-                s0 = a * first_w + PAIR + w * N + h * P
+                s0 = a * first_w + CH + w * N + h * P
                 lhsT = w4[w][:, 2 * n0 : 2 * (n0 + P)].bitcast(FP4X4)
                 lhsT_scale = planes[:, s0 : s0 + P]
             nc.tensor.matmul_mx(
@@ -183,45 +193,63 @@ def tile_list_engram_dl_dl_bsig_kernel(
         def open_bank(j0, n, w, h, slot):
             bank[j0, w, h] = psum.tile([P, n], F32, name=f"bank{j0}_{w}{h}", tag=f"bank{slot}")
 
-        first_banks = [(0, KEY, 0), (0, KEY, 1), (1, KEY, 0), (0, VALUE, 0), (1, KEY, 1), (0, VALUE, 1)]
-        first_banks = first_banks + [(1, VALUE, 0), (1, VALUE, 1)]
+        first_banks = [(c, w, h) for w in (KEY, VALUE) for c in range(2) for h in range(HALVES)]
 
-        def first_words(c):
+        def part_first(picked, c, cuts):
+            dst = parted[c][:].bitcast(U16).rearrange("p (a j) -> p a j", a=PASSES)
+            src = picked[:].bitcast(U16).rearrange("p (j a) -> p a j", a=PASSES)
+            for cols in cuts:
+                nc.vector.tensor_copy(dst[:, 0, cols], src[:, 0, cols])
+            nc.vector.tensor_copy(dst[:, 1, :], src[:, 1, :])
+
+        def first_bases(c, cuts):
             j0 = c * CH
-            parted[c] = keep.tile([P, PASSES * 2 * CH], U8, name=f"parted{c}", align_bytes=64)
-            picked = keep.tile([P, CH], U32, name=f"picked{c}", tag=("picked0", "stage")[c], align_bytes=64)
-            gather_words(picked, j0, CH)
-            part_words(picked, j0, CH, True)
             for w in (KEY, VALUE):
-                for a in range(PASSES):
-                    for h in range(HALVES):
-                        if a == 0:
-                            open_bank(j0, CH, w, h, first_banks.index((c, w, h)))
-                        one_pass(bank[j0, w, h][:], w, h, a, False, j0, CH, start=a == 0)
+                for h in range(HALVES):
+                    open_bank(j0, CH, w, h, first_banks.index((c, w, h)))
+            for cols in cuts:
+                for h in range(HALVES):
+                    n = cols.stop - cols.start
+                    one_pass(bank[j0, KEY, h][:, cols], KEY, h, 0, False, j0 + cols.start, n, start=cols.start == 0)
+            for w, a in ((KEY, 1), (VALUE, 0), (VALUE, 1)):
+                for h in range(HALVES):
+                    one_pass(bank[j0, w, h][:], w, h, a, False, j0, CH, start=a == 0)
 
-        def first_deltas(w, a):
-            for c in range(2):
+        def first_deltas(w, a, chunks=(0, 1)):
+            for c in chunks:
                 for h in range(HALVES):
                     one_pass(bank[c * CH, w, h][:], w, h, a, True, c * CH, CH, stop=a == PASSES - 1)
 
-        first_words(0)
-        first_words(1)
-        picked2 = late.tile([P, CH], U32, name="picked2", tag="raw00", align_bytes=64)
-        gather_words(picked2, 2 * CH, CH)
+        whole = [slice(0, CH)]
+        cuts = [slice(0, HC), slice(HC, CH)]
+        picked0 = keep.tile([P, CH], U32, name="picked0", align_bytes=64)
+        parted[0] = keep.tile([P, PASSES * 2 * CH], U8, name="parted0", align_bytes=64)
+        for cols in cuts:
+            gather_words(picked0[:, cols], cols.start, cols.stop - cols.start)
+        part_first(picked0, 0, cuts)
+        first_bases(0, cuts)
+        picked1 = keep.tile([P, CH], U32, name="picked1", tag="stage", align_bytes=64)
+        gather_words(picked1, CH, CH)
         quantise(KEY, 0)
-        first_deltas(KEY, 0)
-        parted[2] = keep.tile([P, PASSES * 2 * CH], U8, name="parted2", align_bytes=64)
-        part_words(picked2, 2 * CH, CH, False)
+        first_deltas(KEY, 0, (0,))
+        parted[1] = early.tile([P, PASSES * 2 * CH], U8, name="parted1", tag="raw00", align_bytes=64)
+        part_first(picked1, 1, whole)
+        first_bases(1, whole)
+        first_deltas(KEY, 0, (1,))
+        picked2 = keep.tile([P, CH], U32, name="picked2", tag="grouped00", align_bytes=64)
+        gather_words(picked2, 2 * CH, CH)
         quantise(KEY, 1)
         first_deltas(KEY, 1)
         picked3 = late.tile([P, CH], U32, name="picked3", tag="raw01", align_bytes=64)
         gather_words(picked3, 3 * CH, CH)
         quantise(VALUE, 0)
         first_deltas(VALUE, 0)
-        parted[3] = late.tile([P, PASSES * 2 * CH], U8, name="parted3", tag="raw10", align_bytes=64)
-        part_words(picked3, 3 * CH, CH, False)
+        parted[2] = late.tile([P, PASSES * 2 * CH], U8, name="parted2", tag="raw10", align_bytes=64)
+        part_words(picked2, 2 * CH, CH, False)
         quantise(VALUE, 1)
         first_deltas(VALUE, 1)
+        parted[3] = late.tile([P, PASSES * 2 * CH], U8, name="parted3", tag="raw11", align_bytes=64)
+        part_words(picked3, 3 * CH, CH, False)
 
         def make_gate(j0, n, h, pre=None):
             if pre is None:
@@ -252,10 +280,7 @@ def tile_list_engram_dl_dl_bsig_kernel(
 
         for c, w, h in first_banks:
             if w == KEY:
-                pre = None
-                if (c, h) == (0, 0):
-                    pre = late.tile([P, CH], F32, name="pre00", tag="raw11", align_bytes=64)
-                make_gate(c * CH, CH, h, pre)
+                make_gate(c * CH, CH, h)
             else:
                 gated(c * CH, CH, h)
                 if c == 0:

@@ -44,7 +44,7 @@ def tile_list_engram_dl_dl_bsig_kernel(
         psum = ctx.enter_context(tc.psum_pool(name="psum", bufs=1))
 
         def placed(name, shape, dtype, offset):
-            return ring.tile(shape, dtype, name=name, align_bytes=64, offset=offset)
+            return ring.tile(shape, dtype, name=name, align_bytes=256, offset=offset)
 
         def compact(scales):
             return scales.bitcast(I32).rearrange("a q n -> q a n")
@@ -60,17 +60,17 @@ def tile_list_engram_dl_dl_bsig_kernel(
             return offsets[:, j0 // GROUP : (j0 + n) // GROUP]
 
         offsets = keep.tile([P, J // GROUP], U16, name="offsets")
-        table = keep.tile([P, T], I32, name="table", align_bytes=64)
+        table = keep.tile([P, T], I32, name="table", align_bytes=256)
         first_w = CH + 2 * N
         rest_w = J - CH
-        stage = keep.tile([P, first_w], U8, name="stage", tag="stage", align_bytes=64)
-        planes = keep.tile([P, PASSES * first_w], U8, name="planes", align_bytes=64)
-        planes2 = keep.tile([P, PASSES * rest_w], U8, name="planes2", align_bytes=64)
+        stage = keep.tile([P, first_w], U8, name="stage", tag="stage", align_bytes=256)
+        planes = keep.tile([P, PASSES * first_w], U8, name="planes", align_bytes=256)
+        planes2 = keep.tile([P, PASSES * rest_w], U8, name="planes2", align_bytes=256)
         w4, raw, st_of, res_of = {}, {}, {}, {}
         parted, codes, dscale, bank, gate, prod = {}, {}, {}, {}, {}, {}
 
         def load_base(pool, w, words):
-            w4[w] = pool.tile([P, PASSES * 2 * N], U8, name=f"w4{w}", align_bytes=64)
+            w4[w] = pool.tile([P, PASSES * 2 * N], U8, name=f"w4{w}", align_bytes=256)
             nc.sync.dma_start(
                 w4[w][:].bitcast(I32).rearrange("p (a n) -> p a n", a=PASSES),
                 words.bitcast(I32).rearrange("a p n -> p a n"),
@@ -101,18 +101,18 @@ def tile_list_engram_dl_dl_bsig_kernel(
             nc.vector.memset(planes[:].bitcast(I32), 0)
             nc.gpsimd.memset(planes2[:].bitcast(I32), 0)
 
-        rows_rest = keep.tile([P, rest_w], U8, name="rows_rest", align_bytes=64)
+        rows_rest = keep.tile([P, rest_w], U8, name="rows_rest", align_bytes=256)
 
         def load_delta(pool, w, wd, a):
-            raw[w, a] = pool.tile([P, PACK, N], F32, name=f"raw{w}{a}", tag=f"raw{w}{a}", align_bytes=64)
+            raw[w, a] = pool.tile([P, PACK, N], F32, name=f"raw{w}{a}", tag=f"raw{w}{a}", align_bytes=256)
             rows = wd[a * K_PASS : (a + 1) * K_PASS, :]
             nc.sync.dma_start(raw[w, a][:], rows.rearrange("(p i) n -> p i n", i=PACK))
 
         with tc.tile_pool(name="window", bufs=1, side="right") as window:
-            srows = window.tile([P, T], U8, name="srows", align_bytes=64)
+            srows = window.tile([P, T], U8, name="srows", align_bytes=256)
             head(srows)
             with tc.tile_pool(name="first", bufs=1) as first:
-                rows0 = first.tile([P, CH], U8, name="rows0", align_bytes=64)
+                rows0 = first.tile([P, CH], U8, name="rows0", align_bytes=256)
                 nc.vector.tensor_copy(rows0[:], srows[:].indirect(entries(0, CH)))
                 nc.vector.tensor_copy(rows_rest[:, 0:CH], srows[:].indirect(entries(CH, CH)))
                 nc.vector.tensor_copy(stage[:].bitcast(I32)[:, 0 : CH // 4], rows0[:].bitcast(I32))
@@ -162,13 +162,13 @@ def tile_list_engram_dl_dl_bsig_kernel(
                 nc.vector.tensor_copy(dst, src)
 
         def quantise(w, a):
-            grouped = keep.tile([P, PACK * N], BF16, name=f"grouped{w}{a}", tag=f"grouped{w}{a}", align_bytes=64)
+            grouped = keep.tile([P, PACK * N], BF16, name=f"grouped{w}{a}", tag=f"grouped{w}{a}", align_bytes=256)
             nc.scalar.copy(
                 grouped[:].rearrange("p (m u i) -> p m i u", u=4, i=PACK),
                 raw[w, a][:].rearrange("p i (m u) -> p m i u", u=4),
             )
-            codes[w, a] = keep.tile([P, N], U32, name=f"codes{w}{a}", align_bytes=64)
-            dscale[w, a] = keep.tile([P, N], U8, name=f"dscale{w}{a}", align_bytes=64)
+            codes[w, a] = keep.tile([P, N], U32, name=f"codes{w}{a}", align_bytes=256)
+            dscale[w, a] = keep.tile([P, N], U8, name=f"dscale{w}{a}", align_bytes=256)
             nc.vector.quantize_mx(out=codes[w, a][:].bitcast(FP8X4), scales=dscale[w, a][:], in_=grouped[:])
 
         def one_pass(acc, w, h, a, delta, j0, n, start=False, stop=False):
@@ -222,33 +222,33 @@ def tile_list_engram_dl_dl_bsig_kernel(
 
         whole = [slice(0, CH)]
         cuts = [slice(0, HC), slice(HC, CH)]
-        picked0 = keep.tile([P, CH], U32, name="picked0", align_bytes=64)
-        parted[0] = keep.tile([P, PASSES * 2 * CH], U8, name="parted0", align_bytes=64)
+        picked0 = keep.tile([P, CH], U32, name="picked0", align_bytes=256)
+        parted[0] = keep.tile([P, PASSES * 2 * CH], U8, name="parted0", align_bytes=256)
         for cols in cuts:
             gather_words(picked0[:, cols], cols.start, cols.stop - cols.start)
         part_first(picked0, 0, cuts)
         first_bases(0, cuts)
-        picked1 = keep.tile([P, CH], U32, name="picked1", tag="stage", align_bytes=64)
+        picked1 = keep.tile([P, CH], U32, name="picked1", tag="stage", align_bytes=256)
         gather_words(picked1, CH, CH)
         quantise(KEY, 0)
         first_deltas(KEY, 0, (0,))
-        parted[1] = early.tile([P, PASSES * 2 * CH], U8, name="parted1", tag="raw00", align_bytes=64)
+        parted[1] = early.tile([P, PASSES * 2 * CH], U8, name="parted1", tag="raw00", align_bytes=256)
         part_first(picked1, 1, whole)
         first_bases(1, whole)
         first_deltas(KEY, 0, (1,))
-        picked2 = keep.tile([P, CH], U32, name="picked2", tag="grouped00", align_bytes=64)
+        picked2 = keep.tile([P, CH], U32, name="picked2", tag="grouped00", align_bytes=256)
         gather_words(picked2, 2 * CH, CH)
         quantise(KEY, 1)
         first_deltas(KEY, 1)
-        picked3 = late.tile([P, CH], U32, name="picked3", tag="raw01", align_bytes=64)
+        picked3 = late.tile([P, CH], U32, name="picked3", tag="raw01", align_bytes=256)
         gather_words(picked3, 3 * CH, CH)
         quantise(VALUE, 0)
         first_deltas(VALUE, 0)
-        parted[2] = late.tile([P, PASSES * 2 * CH], U8, name="parted2", tag="raw10", align_bytes=64)
+        parted[2] = late.tile([P, PASSES * 2 * CH], U8, name="parted2", tag="raw10", align_bytes=256)
         part_words(picked2, 2 * CH, CH, False)
         quantise(VALUE, 1)
         first_deltas(VALUE, 1)
-        parted[3] = late.tile([P, PASSES * 2 * CH], U8, name="parted3", tag="raw11", align_bytes=64)
+        parted[3] = late.tile([P, PASSES * 2 * CH], U8, name="parted3", tag="raw11", align_bytes=256)
         part_words(picked3, 3 * CH, CH, False)
 
         def make_gate(j0, n, h, pre=None):

@@ -89,17 +89,17 @@ def tile_list_engram_dl_dl_bsig_kernel(
         def head(srows):
             nc.sync.dma_start(srows[:].bitcast(I32)[ROWS0:P, :], compact(tab_scales))
             nc.sync.dma_start(offsets[:], offs)
-            nc.sync.dma_start(table[:], tab_words[0].rearrange("p t i -> p (t i)").bitcast(I32))
             for w, scales in ((KEY, wk4_scales), (VALUE, wv4_scales)):
                 cols = slice((CH + w * N) // 4, (CH + (w + 1) * N) // 4)
-                nc.scalar.dma_start(stage[:].bitcast(I32)[ROWS0:P, cols], compact(scales))
+                nc.sync.dma_start(stage[:].bitcast(I32)[ROWS0:P, cols], compact(scales))
+            nc.sync.dma_start(table[:], tab_words[0].rearrange("p t i -> p (t i)").bitcast(I32))
             load_base(keep, KEY, wk4_words)
             warm = keep.tile([P, 2], F32, name="warm")
             nc.gpsimd.memset(warm[:, 0:1], 0.0)
             nc.scalar.activation(warm[:, 1:2], warm[:, 0:1], SIGMOID)
             nc.vector.memset(srows[:].bitcast(I32)[0:ROWS0, :], 0)
             nc.vector.memset(planes[:].bitcast(I32), 0)
-            nc.gpsimd.memset(planes2[:].bitcast(I32), 0)
+            nc.vector.memset(planes2[:].bitcast(I32), 0)
 
         rows_rest = keep.tile([P, rest_w], U8, name="rows_rest", align_bytes=256)
 
@@ -272,10 +272,11 @@ def tile_list_engram_dl_dl_bsig_kernel(
             nc.sync.dma_start(out[h * P : (h + 1) * P, j0 : j0 + n], total[:])
 
         def whole_sum(j0, n, w, h, slot):
+            kinds = (True, False) if len(bank) % 2 == 0 else (False, True)
             open_bank(j0, n, w, h, slot)
-            for delta in (False, True):
+            for delta in kinds:
                 for a in range(PASSES):
-                    first, last = (delta, a) == (False, 0), (delta, a) == (True, PASSES - 1)
+                    first, last = (delta, a) == (kinds[0], 0), (delta, a) == (kinds[1], PASSES - 1)
                     one_pass(bank[j0, w, h][:], w, h, a, delta, j0, n, start=first, stop=last)
 
         for c, w, h in first_banks:

@@ -32,6 +32,7 @@ ROWS0 = P - QUADRANT
 KEY, VALUE = 0, 1
 WARM_PASSES = 5
 KIB = 1024
+LINE = 8
 
 
 def tile_list_engram_dl_dl_bsig_kernel(
@@ -151,15 +152,9 @@ def tile_list_engram_dl_dl_bsig_kernel(
         def gather_words(tile, j0, n):
             nc.vector.tensor_copy(tile[:], table[:].bitcast(U32).indirect(entries(j0, n)))
 
-        def part_words(picked, j0, n, by_pass):
-            dst = parted[j0 // CH][:].bitcast(U16).rearrange("p (a j) -> p a j", a=PASSES)
-            dst = dst[:, :, j0 % CH : j0 % CH + n]
-            src = picked[:].bitcast(U16).rearrange("p (j a) -> p a j", a=PASSES)
-            if by_pass:
-                for a in range(PASSES):
-                    nc.vector.tensor_copy(dst[:, a, :], src[:, a, :])
-            else:
-                nc.vector.tensor_copy(dst, src)
+        def part_words(picked, c):
+            dst = parted[c][:].bitcast(U16).rearrange("p (a m u) -> p m a u", a=PASSES, u=LINE)
+            nc.vector.tensor_copy(dst, picked.bitcast(U16).rearrange("p (m u a) -> p m a u", a=PASSES, u=LINE))
 
         def quantise(w, a):
             grouped = keep.tile([P, PACK * N], BF16, name=f"grouped{w}{a}", tag=f"grouped{w}{a}", align_bytes=256)
@@ -236,20 +231,19 @@ def tile_list_engram_dl_dl_bsig_kernel(
         part_first(picked1, 1, whole)
         first_bases(1, whole)
         first_deltas(KEY, 0, (1,))
-        picked2 = keep.tile([P, CH], U32, name="picked2", tag="grouped00", align_bytes=256)
-        gather_words(picked2, 2 * CH, CH)
+        both = keep.tile([P, PAIR], U32, name="picked23", tag="grouped00", align_bytes=256)
+        picked2, picked3 = both[:, 0:CH], both[:, CH:PAIR]
+        gather_words(both, 2 * CH, PAIR)
         quantise(KEY, 1)
         first_deltas(KEY, 1)
-        picked3 = late.tile([P, CH], U32, name="picked3", tag="raw01", align_bytes=256)
-        gather_words(picked3, 3 * CH, CH)
+        parted[2] = late.tile([P, PASSES * 2 * CH], U8, name="parted2", tag="raw01", align_bytes=256)
+        part_words(picked2, 2)
         quantise(VALUE, 0)
         first_deltas(VALUE, 0)
-        parted[2] = late.tile([P, PASSES * 2 * CH], U8, name="parted2", tag="raw10", align_bytes=256)
-        part_words(picked2, 2 * CH, CH, False)
+        parted[3] = late.tile([P, PASSES * 2 * CH], U8, name="parted3", tag="raw10", align_bytes=256)
+        part_words(picked3, 3)
         quantise(VALUE, 1)
         first_deltas(VALUE, 1)
-        parted[3] = late.tile([P, PASSES * 2 * CH], U8, name="parted3", tag="raw11", align_bytes=256)
-        part_words(picked3, 3 * CH, CH, False)
 
         def make_gate(j0, n, h, pre=None):
             if pre is None:
@@ -295,15 +289,16 @@ def tile_list_engram_dl_dl_bsig_kernel(
         add_store(CH, CH, 0, nc.vector, rows_of(st_of, j2, CH, 0))
         whole_sum(j2, CH, VALUE, 0, 2)
         gated(j2, CH, 0)
-        add_store(CH, CH, 1, nc.vector, placed("total11", [P, CH], F32, 4 * KIB))
+        add_store(CH, CH, 1, nc.vector, placed("total11", [P, CH], F32, 3 * KIB))
         add_store(j2, CH, 0, nc.gpsimd)
-        whole_sum(j2, CH, VALUE, 1, 3)
+        whole_sum(j3, CH, KEY, 0, 3)
+        make_gate(j3, CH, 0, placed("pre30", [P, CH], F32, 5 * KIB))
+        whole_sum(j2, CH, VALUE, 1, 4)
         gated(j2, CH, 1)
         add_store(j2, CH, 1, nc.gpsimd)
 
-        for h in range(HALVES):
-            whole_sum(j3, CH, KEY, h, 4 + h)
-            make_gate(j3, CH, h)
+        whole_sum(j3, CH, KEY, 1, 5)
+        make_gate(j3, CH, 1)
         pieces = [(h, j3 + u * HC) for h in range(HALVES) for u in range(2)]
         for i, (h, j0) in enumerate(pieces):
             whole_sum(j0, HC, VALUE, h, (6 + i) % 8)

@@ -31,8 +31,9 @@ LIVE = 4
 ROWS0 = P - QUADRANT
 KEY, VALUE = 0, 1
 WARM_PASSES = 5
-KIB = 1024
+BANKS = 8
 LINE = 8
+SHARE = 256
 
 
 def tile_list_engram_dl_dl_bsig_kernel(
@@ -41,21 +42,17 @@ def tile_list_engram_dl_dl_bsig_kernel(
     nc = tc.nc
     with ExitStack() as ctx:
         keep = ctx.enter_context(tc.tile_pool(name="keep", bufs=1))
-        ring = ctx.enter_context(tc.tile_pool(name="ring", bufs=1))
         psum = ctx.enter_context(tc.psum_pool(name="psum", bufs=1))
-
-        def placed(name, shape, dtype, offset):
-            return ring.tile(shape, dtype, name=name, align_bytes=256, offset=offset)
 
         def compact(scales):
             return scales.bitcast(I32).rearrange("a q n -> q a n")
 
-        def spread(planes, rows):
-            dst = planes[:].bitcast(I32).rearrange("p (a n) -> p a n", a=PASSES)
+        def spread(dst_planes, rows):
+            dst = dst_planes[:].bitcast(I32).rearrange("p (a n) -> p a n", a=PASSES)
             src = rows[:].bitcast(I32)
             for q in (0, 2, 1, 3):
-                first = ROWS0 + q * LIVE * PASSES
-                nc.sync.dma_start(dst[q * QUADRANT : q * QUADRANT + LIVE], src[first : first + LIVE * PASSES, :])
+                row = ROWS0 + q * LIVE * PASSES
+                nc.sync.dma_start(dst[q * QUADRANT : q * QUADRANT + LIVE], src[row : row + LIVE * PASSES, :])
 
         def entries(j0, n):
             return offsets[:, j0 // GROUP : (j0 + n) // GROUP]
@@ -67,8 +64,10 @@ def tile_list_engram_dl_dl_bsig_kernel(
         stage = keep.tile([P, first_w], U8, name="stage", tag="stage", align_bytes=256)
         planes = keep.tile([P, PASSES * first_w], U8, name="planes", align_bytes=256)
         planes2 = keep.tile([P, PASSES * rest_w], U8, name="planes2", align_bytes=256)
+        rows_rest = keep.tile([P, rest_w], U8, name="rows_rest", align_bytes=256)
+        bias = keep.tile([P, HALVES], F32, name="bias")
         w4, raw, st_of, res_of = {}, {}, {}, {}
-        parted, codes, dscale, bank, gate, prod = {}, {}, {}, {}, {}, {}
+        parted, codes, dscale, bank, gate = {}, {}, {}, {}, {}
 
         def load_base(pool, w, words):
             w4[w] = pool.tile([P, PASSES * 2 * N], U8, name=f"w4{w}", align_bytes=256)
@@ -77,18 +76,24 @@ def tile_list_engram_dl_dl_bsig_kernel(
                 words.bitcast(I32).rearrange("a p n -> p a n"),
             )
 
-        def load_rows(name, dst, src, c0, chunks):
-            tile = late.tile([P, HALVES, chunks * CH], F32, name=name)
-            nc.sync.dma_start(tile[:], src.rearrange("(h p) j -> p h j", p=P)[:, :, c0 * CH : (c0 + chunks) * CH])
-            for c in range(chunks):
-                dst[c0 + c] = (tile, c * CH)
+        def load_delta(pool, w, wd, a):
+            raw[w, a] = pool.tile([P, PACK, N], F32, name=f"raw{w}{a}", tag=f"raw{w}{a}", align_bytes=256)
+            rows = wd[a * K_PASS : (a + 1) * K_PASS, :]
+            nc.sync.dma_start(raw[w, a][:], rows.rearrange("(p i) n -> p i n", i=PACK))
 
-        def rows_of(held, j0, n, h):
-            tile, first = held[j0 // CH]
-            return tile[:, h, first + j0 % CH : first + j0 % CH + n]
+        def load_rows(name, dst, src, pair, h):
+            dst[pair, h] = late.tile([P, PAIR], F32, name=f"{name}{pair}{h}")
+            nc.sync.dma_start(dst[pair, h][:], src[h * P : (h + 1) * P, pair * PAIR : (pair + 1) * PAIR])
 
-        def head(srows):
+        def cols_of(held, j0, n, h):
+            pair, first = divmod(j0, PAIR)
+            return held[pair, h][:, first : first + n]
+
+        with tc.tile_pool(name="window", bufs=1, side="right") as window:
+            srows = window.tile([P, T], U8, name="srows", align_bytes=256)
             nc.sync.dma_start(srows[:].bitcast(I32)[ROWS0:P, :], compact(tab_scales))
+            with nc.allow_non_contiguous_dma(reason="one bias value a partition"):
+                nc.scalar.dma_start(bias[:], b.rearrange("(h p) -> p h", p=P))
             nc.sync.dma_start(offsets[:], offs)
             for w, scales in ((KEY, wk4_scales), (VALUE, wv4_scales)):
                 cols = slice((CH + w * N) // 4, (CH + (w + 1) * N) // 4)
@@ -101,17 +106,6 @@ def tile_list_engram_dl_dl_bsig_kernel(
             nc.vector.memset(srows[:].bitcast(I32)[0:ROWS0, :], 0)
             nc.vector.memset(planes[:].bitcast(I32), 0)
             nc.vector.memset(planes2[:].bitcast(I32), 0)
-
-        rows_rest = keep.tile([P, rest_w], U8, name="rows_rest", align_bytes=256)
-
-        def load_delta(pool, w, wd, a):
-            raw[w, a] = pool.tile([P, PACK, N], F32, name=f"raw{w}{a}", tag=f"raw{w}{a}", align_bytes=256)
-            rows = wd[a * K_PASS : (a + 1) * K_PASS, :]
-            nc.sync.dma_start(raw[w, a][:], rows.rearrange("(p i) n -> p i n", i=PACK))
-
-        with tc.tile_pool(name="window", bufs=1, side="right") as window:
-            srows = window.tile([P, T], U8, name="srows", align_bytes=256)
-            head(srows)
             with tc.tile_pool(name="first", bufs=1) as first:
                 rows0 = first.tile([P, CH], U8, name="rows0", align_bytes=256)
                 nc.vector.tensor_copy(rows0[:], srows[:].indirect(entries(0, CH)))
@@ -127,17 +121,16 @@ def tile_list_engram_dl_dl_bsig_kernel(
         late = ctx.enter_context(tc.tile_pool(name="late", bufs=1, side="right"))
         for w, wd, a in ((KEY, wkd, 1), (VALUE, wvd, 0), (VALUE, wvd, 1)):
             load_delta(late, w, wd, a)
-        load_rows("st01", st_of, st, 0, 2)
-        bias = late.tile([P, HALVES], F32, name="bias")
-        with nc.allow_non_contiguous_dma(reason="one bias value a partition"):
-            nc.sync.dma_start(bias[:], b.rearrange("(h p) -> p h", p=P))
-        load_rows("res0", res_of, res, 0, 1)
-        load_rows("st23", st_of, st, 2, 2)
-        load_rows("res1", res_of, res, 1, 1)
-        load_rows("res2", res_of, res, 2, 1)
-        load_rows("res3", res_of, res, 3, 1)
+        load_rows("st", st_of, st, 0, 0)
+        load_rows("st", st_of, st, 0, 1)
+        load_rows("res", res_of, res, 0, 0)
+        load_rows("st", st_of, st, 1, 0)
+        load_rows("res", res_of, res, 0, 1)
+        load_rows("st", st_of, st, 1, 1)
+        load_rows("res", res_of, res, 1, 0)
+        load_rows("res", res_of, res, 1, 1)
 
-        spare = psum.tile([P, CH], F32, name="spare", tag="bank7")
+        spare = psum.tile([P, CH], F32, name="spare", tag=f"bank{BANKS - 1}")
         for i in range(WARM_PASSES):
             nc.tensor.matmul_mx(
                 out=spare[:],
@@ -150,11 +143,18 @@ def tile_list_engram_dl_dl_bsig_kernel(
             )
 
         def gather_words(tile, j0, n):
-            nc.vector.tensor_copy(tile[:], table[:].bitcast(U32).indirect(entries(j0, n)))
+            nc.vector.tensor_copy(tile, table[:].bitcast(U32).indirect(entries(j0, n)))
 
-        def part_words(picked, c):
+        def part_pass(picked, c, a, cols):
+            dst = parted[c][:].bitcast(U16).rearrange("p (a j) -> p a j", a=PASSES)
+            src = picked.bitcast(U16).rearrange("p (j a) -> p a j", a=PASSES)
+            nc.vector.tensor_copy(dst[:, a, cols], src[:, a, cols])
+
+        def part_both(picked, c, cols):
+            lines = slice(cols.start // LINE, cols.stop // LINE)
             dst = parted[c][:].bitcast(U16).rearrange("p (a m u) -> p m a u", a=PASSES, u=LINE)
-            nc.vector.tensor_copy(dst, picked.bitcast(U16).rearrange("p (m u a) -> p m a u", a=PASSES, u=LINE))
+            src = picked.bitcast(U16).rearrange("p (m u a) -> p m a u", a=PASSES, u=LINE)
+            nc.vector.tensor_copy(dst[:, lines], src[:, lines])
 
         def quantise(w, a):
             grouped = keep.tile([P, PACK * N], BF16, name=f"grouped{w}{a}", tag=f"grouped{w}{a}", align_bytes=256)
@@ -188,121 +188,144 @@ def tile_list_engram_dl_dl_bsig_kernel(
         def open_bank(j0, n, w, h, slot):
             bank[j0, w, h] = psum.tile([P, n], F32, name=f"bank{j0}_{w}{h}", tag=f"bank{slot}")
 
-        first_banks = [(c, w, h) for w in (KEY, VALUE) for c in range(2) for h in range(HALVES)]
-
-        def part_first(picked, c, cuts):
-            dst = parted[c][:].bitcast(U16).rearrange("p (a j) -> p a j", a=PASSES)
-            src = picked[:].bitcast(U16).rearrange("p (j a) -> p a j", a=PASSES)
-            for cols in cuts:
-                nc.vector.tensor_copy(dst[:, 0, cols], src[:, 0, cols])
-            nc.vector.tensor_copy(dst[:, 1, :], src[:, 1, :])
+        first_order = [
+            (KEY, 0, 0),
+            (KEY, 0, 1),
+            (KEY, 1, 0),
+            (VALUE, 0, 0),
+            (KEY, 1, 1),
+            (VALUE, 0, 1),
+            (VALUE, 1, 0),
+            (VALUE, 1, 1),
+        ]
 
         def first_bases(c, cuts):
             j0 = c * CH
             for w in (KEY, VALUE):
                 for h in range(HALVES):
-                    open_bank(j0, CH, w, h, first_banks.index((c, w, h)))
+                    open_bank(j0, CH, w, h, first_order.index((w, h, c)))
             for cols in cuts:
+                n = cols.stop - cols.start
+                for a in range(PASSES):
+                    for h in range(HALVES):
+                        begin = cols.start == 0 and a == 0
+                        one_pass(bank[j0, KEY, h][:, cols], KEY, h, a, False, j0 + cols.start, n, start=begin)
+            for a in range(PASSES):
                 for h in range(HALVES):
-                    n = cols.stop - cols.start
-                    one_pass(bank[j0, KEY, h][:, cols], KEY, h, 0, False, j0 + cols.start, n, start=cols.start == 0)
-            for w, a in ((KEY, 1), (VALUE, 0), (VALUE, 1)):
-                for h in range(HALVES):
-                    one_pass(bank[j0, w, h][:], w, h, a, False, j0, CH, start=a == 0)
+                    one_pass(bank[j0, VALUE, h][:], VALUE, h, a, False, j0, CH, start=a == 0)
 
         def first_deltas(w, a, chunks=(0, 1)):
-            for c in chunks:
-                for h in range(HALVES):
+            for h in range(HALVES):
+                for c in chunks:
                     one_pass(bank[c * CH, w, h][:], w, h, a, True, c * CH, CH, stop=a == PASSES - 1)
 
-        whole = [slice(0, CH)]
-        cuts = [slice(0, HC), slice(HC, CH)]
+        whole = slice(0, CH)
+        low, high = slice(0, HC), slice(HC, CH)
         picked0 = keep.tile([P, CH], U32, name="picked0", align_bytes=256)
         parted[0] = keep.tile([P, PASSES * 2 * CH], U8, name="parted0", align_bytes=256)
-        for cols in cuts:
-            gather_words(picked0[:, cols], cols.start, cols.stop - cols.start)
-        part_first(picked0, 0, cuts)
-        first_bases(0, cuts)
+        gather_words(picked0[:, low], 0, HC)
+        gather_words(picked0[:, high], HC, HC)
+        for a in range(PASSES):
+            part_pass(picked0[:], 0, a, low)
+        part_both(picked0[:], 0, high)
+        first_bases(0, (low, high))
         picked1 = keep.tile([P, CH], U32, name="picked1", tag="stage", align_bytes=256)
-        gather_words(picked1, CH, CH)
+        gather_words(picked1[:], CH, CH)
         quantise(KEY, 0)
         first_deltas(KEY, 0, (0,))
         parted[1] = early.tile([P, PASSES * 2 * CH], U8, name="parted1", tag="raw00", align_bytes=256)
-        part_first(picked1, 1, whole)
-        first_bases(1, whole)
+        for a in range(PASSES):
+            part_pass(picked1[:], 1, a, whole)
+        first_bases(1, (whole,))
         first_deltas(KEY, 0, (1,))
         both = keep.tile([P, PAIR], U32, name="picked23", tag="grouped00", align_bytes=256)
-        picked2, picked3 = both[:, 0:CH], both[:, CH:PAIR]
-        gather_words(both, 2 * CH, PAIR)
+        gather_words(both[:], 2 * CH, PAIR)
         quantise(KEY, 1)
         first_deltas(KEY, 1)
         parted[2] = late.tile([P, PASSES * 2 * CH], U8, name="parted2", tag="raw01", align_bytes=256)
-        part_words(picked2, 2)
+        part_both(both[:, 0:CH], 2, whole)
         quantise(VALUE, 0)
         first_deltas(VALUE, 0)
         parted[3] = late.tile([P, PASSES * 2 * CH], U8, name="parted3", tag="raw10", align_bytes=256)
-        part_words(picked3, 3)
+        part_both(both[:, CH:PAIR], 3, whole)
         quantise(VALUE, 1)
         first_deltas(VALUE, 1)
 
-        def make_gate(j0, n, h, pre=None):
-            if pre is None:
-                pre = keep.tile([P, n], F32, name=f"pre{j0}_{h}")
-            nc.vector.tensor_tensor(pre[:], rows_of(st_of, j0, n, h), bank[j0, KEY, h][:], MULT)
-            gate[j0, h] = keep.tile([P, n], F32, name=f"gate{j0}_{h}")
+        prod, total = {}, {}
+        for h in range(HALVES):
+            prod[0, h] = keep.tile([P, PAIR], F32, name=f"prod0_{h}")
+            total[0, h] = keep.tile([P, PAIR], F32, name=f"total0_{h}")
+
+        def piece(held, name, j0, n, h):
+            if j0 < PAIR:
+                return held[0, h][:, j0 : j0 + n]
+            if (j0, h) not in held:
+                held[j0, h] = keep.tile([P, n], F32, name=f"{name}{j0}_{h}")
+            return held[j0, h][:]
+
+        def make_gate(j0, h):
+            pre = keep.tile([P, CH], F32, name=f"pre{j0}_{h}")
+            nc.vector.tensor_tensor(pre[:], cols_of(st_of, j0, CH, h), bank[j0, KEY, h][:], MULT)
+            gate[j0, h] = keep.tile([P, CH], F32, name=f"gate{j0}_{h}")
             nc.scalar.activation(gate[j0, h][:], pre[:], SIGMOID, bias=bias[:, h : h + 1])
 
-        def gated(j0, n, h, tile=None, g0=None):
-            if tile is None:
-                tile = keep.tile([P, n], F32, name=f"prod{j0}_{h}")
-            prod[j0, h] = tile
-            g0 = j0 if g0 is None else g0
-            nc.vector.tensor_tensor(tile[:], gate[g0, h][:, j0 - g0 : j0 - g0 + n], bank[j0, VALUE, h][:], MULT)
+        def gated(j0, n, h):
+            g0 = j0 // CH * CH
+            gate_cols = gate[g0, h][:, j0 - g0 : j0 - g0 + n]
+            nc.vector.tensor_tensor(piece(prod, "prod", j0, n, h), gate_cols, bank[j0, VALUE, h][:], MULT)
 
-        def add_store(j0, n, h, engine, total=None):
-            if total is None:
-                total = keep.tile([P, n], F32, name=f"total{j0}_{h}")
-            engine.tensor_tensor(total[:], prod[j0, h][:], rows_of(res_of, j0, n, h), ADD)
-            nc.sync.dma_start(out[h * P : (h + 1) * P, j0 : j0 + n], total[:])
+        def add(engine, j0, n, h):
+            summed = piece(total, "total", j0, n, h)
+            engine.tensor_tensor(summed, piece(prod, "prod", j0, n, h), cols_of(res_of, j0, n, h), ADD)
+
+        def store(j0, n, h):
+            nc.sync.dma_start(out[h * P : (h + 1) * P, j0 : j0 + n], piece(total, "total", j0, n, h))
 
         def whole_sum(j0, n, w, h, slot):
             kinds = (True, False) if len(bank) % 2 == 0 else (False, True)
-            open_bank(j0, n, w, h, slot)
+            open_bank(j0, n, w, h, slot % BANKS)
             for delta in kinds:
                 for a in range(PASSES):
-                    first, last = (delta, a) == (kinds[0], 0), (delta, a) == (kinds[1], PASSES - 1)
-                    one_pass(bank[j0, w, h][:], w, h, a, delta, j0, n, start=first, stop=last)
+                    begin, end = (delta, a) == (kinds[0], 0), (delta, a) == (kinds[1], PASSES - 1)
+                    one_pass(bank[j0, w, h][:], w, h, a, delta, j0, n, start=begin, stop=end)
 
-        for c, w, h in first_banks:
+        j1, j2, j3 = CH, 2 * CH, 3 * CH
+        for w, h, c in first_order[:-1]:
             if w == KEY:
-                make_gate(c * CH, CH, h)
+                make_gate(c * CH, h)
             else:
                 gated(c * CH, CH, h)
-                if c == 0:
-                    add_store(c * CH, CH, h, nc.gpsimd)
+                add(nc.gpsimd, c * CH, CH if h == 0 else SHARE, h)
+        store(0, PAIR, 0)
 
-        j2, j3 = 2 * CH, 3 * CH
         whole_sum(j2, CH, KEY, 0, 0)
-        make_gate(j2, CH, 0)
-        whole_sum(j2, CH, KEY, 1, 1)
-        make_gate(j2, CH, 1, placed("pre21", [P, CH], F32, 4 * KIB))
-        add_store(CH, CH, 0, nc.vector, rows_of(st_of, j2, CH, 0))
+        make_gate(j2, 0)
+        gated(j1, CH, 1)
+        whole_sum(j3, CH, KEY, 0, 1)
+        make_gate(j3, 0)
         whole_sum(j2, CH, VALUE, 0, 2)
         gated(j2, CH, 0)
-        add_store(CH, CH, 1, nc.vector, placed("total11", [P, CH], F32, 3 * KIB))
-        add_store(j2, CH, 0, nc.gpsimd)
-        whole_sum(j3, CH, KEY, 0, 3)
-        make_gate(j3, CH, 0, placed("pre30", [P, CH], F32, 5 * KIB))
-        whole_sum(j2, CH, VALUE, 1, 4)
-        gated(j2, CH, 1)
-        add_store(j2, CH, 1, nc.gpsimd)
-
+        add(nc.vector, SHARE, PAIR - SHARE, 1)
+        store(0, PAIR, 1)
+        add(nc.gpsimd, j2, CH, 0)
+        store(j2, CH, 0)
+        whole_sum(j2, CH, KEY, 1, 3)
+        make_gate(j2, 1)
+        whole_sum(j3, CH, VALUE, 0, 4)
+        gated(j3, CH, 0)
+        add(nc.gpsimd, j3, CH, 0)
+        store(j3, CH, 0)
         whole_sum(j3, CH, KEY, 1, 5)
-        make_gate(j3, CH, 1)
-        pieces = [(h, j3 + u * HC) for h in range(HALVES) for u in range(2)]
-        for i, (h, j0) in enumerate(pieces):
-            whole_sum(j0, HC, VALUE, h, (6 + i) % 8)
-            gated(j0, HC, h, g0=j3)
+        make_gate(j3, 1)
+
+        pieces = [j2 + u * HC for u in range(PAIR // HC)]
+        for j0, tag in ((j2, "raw01"), (j3, "raw10")):
+            total[j0, 1] = late.tile([P, HC], F32, name=f"total{j0}_1", tag=tag, align_bytes=256)
+        for i, j0 in enumerate(pieces):
+            whole_sum(j0, HC, VALUE, 1, 6 + i)
+            gated(j0, HC, 1)
             if i > 0:
-                add_store(pieces[i - 1][1], HC, pieces[i - 1][0], nc.vector)
-        add_store(j3 + HC, HC, 1, nc.vector)
+                add(nc.vector, pieces[i - 1], HC, 1)
+                store(pieces[i - 1], HC, 1)
+        add(nc.vector, pieces[-1], HC, 1)
+        store(pieces[-1], HC, 1)

@@ -65,7 +65,6 @@ def tile_list_engram_dl_dl_bsig_kernel(
         planes = keep.tile([P, PASSES * first_w], U8, name="planes", align_bytes=256)
         planes2 = keep.tile([P, PASSES * rest_w], U8, name="planes2", align_bytes=256)
         rows_rest = keep.tile([P, rest_w], U8, name="rows_rest", align_bytes=256)
-        bias = keep.tile([P, HALVES], F32, name="bias")
         w4, raw, st_of, res_of = {}, {}, {}, {}
         parted, codes, dscale, bank, gate = {}, {}, {}, {}, {}
 
@@ -92,8 +91,6 @@ def tile_list_engram_dl_dl_bsig_kernel(
         with tc.tile_pool(name="window", bufs=1, side="right") as window:
             srows = window.tile([P, T], U8, name="srows", align_bytes=256)
             nc.sync.dma_start(srows[:].bitcast(I32)[ROWS0:P, :], compact(tab_scales))
-            with nc.allow_non_contiguous_dma(reason="one bias value a partition"):
-                nc.scalar.dma_start(bias[:], b.rearrange("(h p) -> p h", p=P))
             nc.sync.dma_start(offsets[:], offs)
             for w, scales in ((KEY, wk4_scales), (VALUE, wv4_scales)):
                 cols = slice((CH + w * N) // 4, (CH + (w + 1) * N) // 4)
@@ -122,6 +119,9 @@ def tile_list_engram_dl_dl_bsig_kernel(
         for w, wd, a in ((KEY, wkd, 1), (VALUE, wvd, 0), (VALUE, wvd, 1)):
             load_delta(late, w, wd, a)
         load_rows("st", st_of, st, 0, 0)
+        bias = late.tile([P, HALVES], F32, name="bias")
+        with nc.allow_non_contiguous_dma(reason="one bias value a partition"):
+            nc.sync.dma_start(bias[:], b.rearrange("(h p) -> p h", p=P))
         load_rows("st", st_of, st, 0, 1)
         load_rows("res", res_of, res, 0, 0)
         load_rows("st", st_of, st, 1, 0)
@@ -214,8 +214,8 @@ def tile_list_engram_dl_dl_bsig_kernel(
                 for h in range(HALVES):
                     one_pass(bank[j0, VALUE, h][:], VALUE, h, a, False, j0, CH, start=a == 0)
 
-        def first_deltas(w, a, chunks=(0, 1)):
-            for h in range(HALVES):
+        def first_deltas(w, a, chunks=(0, 1), halves=(0, 1)):
+            for h in halves:
                 for c in chunks:
                     one_pass(bank[c * CH, w, h][:], w, h, a, True, c * CH, CH, stop=a == PASSES - 1)
 
@@ -245,11 +245,13 @@ def tile_list_engram_dl_dl_bsig_kernel(
         parted[2] = late.tile([P, PASSES * 2 * CH], U8, name="parted2", tag="raw01", align_bytes=256)
         part_both(both[:, 0:CH], 2, whole)
         quantise(VALUE, 0)
-        first_deltas(VALUE, 0)
+        first_deltas(VALUE, 0, halves=(0,))
         parted[3] = late.tile([P, PASSES * 2 * CH], U8, name="parted3", tag="raw10", align_bytes=256)
         part_both(both[:, CH:PAIR], 3, whole)
         quantise(VALUE, 1)
-        first_deltas(VALUE, 1)
+        first_deltas(VALUE, 1, halves=(0,))
+        for a in range(PASSES):
+            first_deltas(VALUE, a, halves=(1,))
 
         prod, total = {}, {}
         for h in range(HALVES):
@@ -264,7 +266,14 @@ def tile_list_engram_dl_dl_bsig_kernel(
             return held[j0, h][:]
 
         def make_gate(j0, h):
-            pre = keep.tile([P, CH], F32, name=f"pre{j0}_{h}")
+            if (j0, h) == (0, 0):
+                pre = late.tile([P, CH], F32, name="pre_first", tag="raw11", align_bytes=256)
+            elif (j0, h) == (CH, 0):
+                pre = keep.tile([P, CH], F32, name="pre_second", tag="grouped11", align_bytes=256)
+            elif j0 < PAIR:
+                pre = cols_of(st_of, 0, CH, j0 // CH)
+            else:
+                pre = keep.tile([P, CH], F32, name=f"pre{j0}_{h}")
             nc.vector.tensor_tensor(pre[:], cols_of(st_of, j0, CH, h), bank[j0, KEY, h][:], MULT)
             gate[j0, h] = keep.tile([P, CH], F32, name=f"gate{j0}_{h}")
             nc.scalar.activation(gate[j0, h][:], pre[:], SIGMOID, bias=bias[:, h : h + 1])

@@ -49,7 +49,7 @@ def tile_list_engram_dl_dl_bsig_kernel(
 
         def spread(dst_planes, rows):
             dst = dst_planes[:].bitcast(I32).rearrange("p (a n) -> p a n", a=PASSES)
-            src = rows[:].bitcast(I32)
+            src = rows.bitcast(I32)
             for q in (0, 2, 1, 3):
                 row = ROWS0 + q * LIVE * PASSES
                 nc.sync.dma_start(dst[q * QUADRANT : q * QUADRANT + LIVE], src[row : row + LIVE * PASSES, :])
@@ -63,7 +63,8 @@ def tile_list_engram_dl_dl_bsig_kernel(
         rest_w = J - CH
         stage = keep.tile([P, first_w], U8, name="stage", tag="stage", align_bytes=256)
         planes = keep.tile([P, PASSES * first_w], U8, name="planes", align_bytes=256)
-        planes2 = keep.tile([P, PASSES * rest_w], U8, name="planes2", align_bytes=256)
+        planes1 = keep.tile([P, PASSES * CH], U8, name="planes1", align_bytes=256)
+        planes23 = keep.tile([P, PASSES * PAIR], U8, name="planes23", align_bytes=256)
         rows_rest = keep.tile([P, rest_w], U8, name="rows_rest", align_bytes=256)
         w4, raw, st_of, res_of = {}, {}, {}, {}
         parted, codes, dscale, bank, gate = {}, {}, {}, {}, {}
@@ -102,19 +103,20 @@ def tile_list_engram_dl_dl_bsig_kernel(
             nc.scalar.activation(warm[:, 1:2], warm[:, 0:1], SIGMOID)
             nc.vector.memset(srows[:].bitcast(I32)[0:ROWS0, :], 0)
             nc.vector.memset(planes[:].bitcast(I32), 0)
-            nc.vector.memset(planes2[:].bitcast(I32), 0)
+            nc.vector.memset(planes1[:].bitcast(I32), 0)
+            nc.vector.memset(planes23[:].bitcast(I32), 0)
             with tc.tile_pool(name="first", bufs=1) as first:
                 rows0 = first.tile([P, CH], U8, name="rows0", align_bytes=256)
                 nc.vector.tensor_copy(rows0[:], srows[:].indirect(entries(0, CH)))
-                nc.vector.tensor_copy(rows_rest[:, 0:CH], srows[:].indirect(entries(CH, CH)))
+                nc.vector.tensor_copy(rows_rest[:, CH : 2 * CH], srows[:].indirect(entries(2 * CH, CH)))
                 nc.vector.tensor_copy(stage[:].bitcast(I32)[:, 0 : CH // 4], rows0[:].bitcast(I32))
-                spread(planes, stage)
+                spread(planes, stage[:])
             early = ctx.enter_context(tc.tile_pool(name="early", bufs=1))
             load_delta(early, KEY, wkd, 0)
             load_base(early, VALUE, wv4_words)
-            for c in (2, 3):
-                nc.vector.tensor_copy(rows_rest[:, (c - 1) * CH : c * CH], srows[:].indirect(entries(c * CH, CH)))
-            spread(planes2, rows_rest)
+            nc.vector.tensor_copy(rows_rest[:, 0:CH], srows[:].indirect(entries(CH, CH)))
+            spread(planes1, rows_rest[:, 0:CH])
+            nc.vector.tensor_copy(rows_rest[:, 2 * CH : 3 * CH], srows[:].indirect(entries(3 * CH, CH)))
         late = ctx.enter_context(tc.tile_pool(name="late", bufs=1, side="right"))
         for w, wd, a in ((KEY, wkd, 1), (VALUE, wvd, 0), (VALUE, wvd, 1)):
             load_delta(late, w, wd, a)
@@ -123,6 +125,7 @@ def tile_list_engram_dl_dl_bsig_kernel(
         with nc.allow_non_contiguous_dma(reason="one bias value a partition"):
             nc.sync.dma_start(bias[:], b.rearrange("(h p) -> p h", p=P))
         load_rows("st", st_of, st, 0, 1)
+        spread(planes23, rows_rest[:, CH:rest_w])
         load_rows("res", res_of, res, 0, 0)
         load_rows("st", st_of, st, 1, 0)
         load_rows("res", res_of, res, 0, 1)
@@ -171,8 +174,10 @@ def tile_list_engram_dl_dl_bsig_kernel(
             words = parted[c][:, 2 * (a * CH + o) : 2 * (a * CH + o + n)].bitcast(FP4X4)
             if c == 0:
                 scale = planes[:, a * first_w + j0 : a * first_w + j0 + n]
+            elif c == 1:
+                scale = planes1[:, a * CH + o : a * CH + o + n]
             else:
-                scale = planes2[:, a * rest_w + j0 - CH : a * rest_w + j0 - CH + n]
+                scale = planes23[:, a * PAIR + j0 - PAIR : a * PAIR + j0 - PAIR + n]
             if delta:
                 lhsT = codes[w, a][:, h * P : (h + 1) * P].bitcast(FP8X4)
                 lhsT_scale = dscale[w, a][:, h * P : (h + 1) * P]

@@ -30,7 +30,7 @@ QUADRANT = 32
 LIVE = 4
 ROWS0 = P - QUADRANT
 KEY, VALUE = 0, 1
-WARM_PASSES = 5
+WARM_PASSES = 6
 BANKS = 8
 LINE = 8
 SHARE = 256
@@ -108,15 +108,27 @@ def tile_list_engram_dl_dl_bsig_kernel(
             with tc.tile_pool(name="first", bufs=1) as first:
                 rows0 = first.tile([P, CH], U8, name="rows0", align_bytes=256)
                 nc.vector.tensor_copy(rows0[:], srows[:].indirect(entries(0, CH)))
-                nc.vector.tensor_copy(rows_rest[:, CH : 2 * CH], srows[:].indirect(entries(2 * CH, CH)))
+                nc.vector.tensor_copy(rows_rest[:, PAIR:rest_w], srows[:].indirect(entries(3 * CH, CH)))
                 nc.vector.tensor_copy(stage[:].bitcast(I32)[:, 0 : CH // 4], rows0[:].bitcast(I32))
                 spread(planes, stage[:])
             early = ctx.enter_context(tc.tile_pool(name="early", bufs=1))
             load_delta(early, KEY, wkd, 0)
             load_base(early, VALUE, wv4_words)
-            nc.vector.tensor_copy(rows_rest[:, 0:CH], srows[:].indirect(entries(CH, CH)))
+            nc.vector.tensor_copy(rows_rest[:, 0:PAIR], srows[:].indirect(entries(CH, PAIR)))
             spread(planes1, rows_rest[:, 0:CH])
-            nc.vector.tensor_copy(rows_rest[:, 2 * CH : 3 * CH], srows[:].indirect(entries(3 * CH, CH)))
+
+        spare = psum.tile([P, CH], F32, name="spare", tag=f"bank{BANKS - 1}")
+        for i in range(WARM_PASSES):
+            nc.tensor.matmul_mx(
+                out=spare[:],
+                lhsT=stage[:, 0 : 2 * P].bitcast(FP4X4),
+                lhsT_scale=stage[:, 0:P],
+                rhs=planes23[:, 0 : 2 * CH].bitcast(FP4X4),
+                rhs_scale=planes23[:, 2 * CH : 3 * CH],
+                start=True,
+                stop=True,
+            )
+
         late = ctx.enter_context(tc.tile_pool(name="late", bufs=1, side="right"))
         for w, wd, a in ((KEY, wkd, 1), (VALUE, wvd, 0), (VALUE, wvd, 1)):
             load_delta(late, w, wd, a)
@@ -132,18 +144,6 @@ def tile_list_engram_dl_dl_bsig_kernel(
         load_rows("st", st_of, st, 1, 1)
         load_rows("res", res_of, res, 1, 0)
         load_rows("res", res_of, res, 1, 1)
-
-        spare = psum.tile([P, CH], F32, name="spare", tag=f"bank{BANKS - 1}")
-        for i in range(WARM_PASSES):
-            nc.tensor.matmul_mx(
-                out=spare[:],
-                lhsT=rows_rest[:, CH : CH + 2 * P].bitcast(FP4X4),
-                lhsT_scale=rows_rest[:, 0:P],
-                rhs=rows_rest[:, 0 : 2 * CH].bitcast(FP4X4),
-                rhs_scale=rows_rest[:, 0:CH],
-                start=True,
-                stop=True,
-            )
 
         def gather_words(tile, j0, n):
             nc.vector.tensor_copy(tile, table[:].bitcast(U32).indirect(entries(j0, n)))

@@ -32,6 +32,8 @@ ROWS0 = P - QUADRANT
 KEY, VALUE = 0, 1
 WARM_PASSES = 6
 BANKS = 8
+SHIFT_SCALES = 64
+SHIFT_WEIGHTS = 128
 LINE = 8
 SHARE = 256
 
@@ -62,15 +64,20 @@ def tile_list_engram_dl_dl_bsig_kernel(
         first_w = CH + 2 * N
         rest_w = J - CH
         stage = keep.tile([P, first_w], U8, name="stage", tag="stage", align_bytes=256)
-        planes = keep.tile([P, PASSES * first_w], U8, name="planes", align_bytes=256)
-        planes1 = keep.tile([P, PASSES * CH], U8, name="planes1", align_bytes=256)
-        planes23 = keep.tile([P, PASSES * PAIR], U8, name="planes23", align_bytes=256)
+
+        def shifted(pool, name, width, dtype, shift, size):
+            tile = pool.tile([P, width + shift // size], dtype, name=name, align_bytes=256)
+            return tile[:, shift // size :]
+
+        planes = shifted(keep, "planes", PASSES * first_w, U8, SHIFT_SCALES, 1)
+        planes1 = shifted(keep, "planes1", PASSES * CH, U8, SHIFT_SCALES, 1)
+        planes23 = shifted(keep, "planes23", PASSES * PAIR, U8, SHIFT_SCALES, 1)
         rows_rest = keep.tile([P, rest_w], U8, name="rows_rest", align_bytes=256)
         w4, raw, st_of, res_of = {}, {}, {}, {}
         parted, codes, dscale, bank, gate = {}, {}, {}, {}, {}
 
         def load_base(pool, w, words):
-            w4[w] = pool.tile([P, PASSES * 2 * N], U8, name=f"w4{w}", align_bytes=256)
+            w4[w] = shifted(pool, f"w4{w}", PASSES * 2 * N, U8, SHIFT_WEIGHTS, 1)
             nc.sync.dma_start(
                 w4[w][:].bitcast(I32).rearrange("p (a n) -> p a n", a=PASSES),
                 words.bitcast(I32).rearrange("a p n -> p a n"),
@@ -165,8 +172,8 @@ def tile_list_engram_dl_dl_bsig_kernel(
                 grouped[:].rearrange("p (m u i) -> p m i u", u=4, i=PACK),
                 raw[w, a][:].rearrange("p i (m u) -> p m i u", u=4),
             )
-            codes[w, a] = keep.tile([P, N], U32, name=f"codes{w}{a}", align_bytes=256)
-            dscale[w, a] = keep.tile([P, N], U8, name=f"dscale{w}{a}", align_bytes=256)
+            codes[w, a] = shifted(keep, f"codes{w}{a}", N, U32, SHIFT_WEIGHTS, 4)
+            dscale[w, a] = shifted(keep, f"dscale{w}{a}", N, U8, SHIFT_SCALES, 1)
             nc.vector.quantize_mx(out=codes[w, a][:].bitcast(FP8X4), scales=dscale[w, a][:], in_=grouped[:])
 
         def one_pass(acc, w, h, a, delta, j0, n, start=False, stop=False):

from contextlib import ExitStack

import concourse.mybir as mybir

K, N, T, J = 1024, 256, 4096, 2048
FLOPS = 4 * 2 * K * N * J

F32 = mybir.dt.float32
BF16 = mybir.dt.bfloat16
I32 = mybir.dt.int32
U32 = mybir.dt.uint32
U16 = mybir.dt.uint16
U8 = mybir.dt.uint8
FP8X4 = mybir.dt.float8_e4m3fn_x4
FP4X4 = mybir.dt.float4_e2m1fn_x4
MULT = mybir.AluOpType.mult
ADD = mybir.AluOpType.add
SIGMOID = mybir.ActivationFunctionType.Sigmoid

P = 128
PACK = 4
K_PASS = P * PACK
PASSES = K // K_PASS
HALVES = N // P
CH = 512
HC = CH // 2
PAIR = 2 * CH
GROUP = 16
QUADRANT = 32
LIVE = 4
ROWS0 = P - QUADRANT
KEY, VALUE = 0, 1
WARM_PASSES = 6
BANKS = 8
SHIFT_SCALES = 64
SHIFT_WEIGHTS = 128
LINE = 8
SHARE = 256


def tile_list_engram_dl_dl_bsig_kernel(
    tc, tab_words, tab_scales, wk4_words, wk4_scales, wkd, wv4_words, wv4_scales, wvd, st, b, res, offs, out
):
    nc = tc.nc
    with ExitStack() as ctx:
        keep = ctx.enter_context(tc.tile_pool(name="keep", bufs=1))
        psum = ctx.enter_context(tc.psum_pool(name="psum", bufs=1))

        def compact(scales):
            return scales.bitcast(I32).rearrange("a q n -> q a n")

        def spread(dst_planes, rows):
            dst = dst_planes[:].bitcast(I32).rearrange("p (a n) -> p a n", a=PASSES)
            src = rows.bitcast(I32)
            for q in (0, 2, 1, 3):
                row = ROWS0 + q * LIVE * PASSES
                nc.sync.dma_start(dst[q * QUADRANT : q * QUADRANT + LIVE], src[row : row + LIVE * PASSES, :])

        def entries(j0, n):
            return offsets[:, j0 // GROUP : (j0 + n) // GROUP]

        offsets = keep.tile([P, J // GROUP], U16, name="offsets")
        table = keep.tile([P, T], I32, name="table", align_bytes=256)
        first_w = CH + 2 * N
        rest_w = J - CH
        stage = keep.tile([P, first_w], U8, name="stage", tag="stage", align_bytes=256)

        def shifted(pool, name, width, dtype, shift, size):
            tile = pool.tile([P, width + shift // size], dtype, name=name, align_bytes=256)
            return tile[:, shift // size :]

        planes = shifted(keep, "planes", PASSES * first_w, U8, SHIFT_SCALES, 1)
        planes1 = shifted(keep, "planes1", PASSES * CH, U8, SHIFT_SCALES, 1)
        planes23 = shifted(keep, "planes23", PASSES * PAIR, U8, SHIFT_SCALES, 1)
        rows_rest = keep.tile([P, rest_w], U8, name="rows_rest", align_bytes=256)
        w4, raw, st_of, res_of = {}, {}, {}, {}
        parted, codes, dscale, bank, gate = {}, {}, {}, {}, {}

        def load_base(pool, w, words):
            w4[w] = shifted(pool, f"w4{w}", PASSES * 2 * N, U8, SHIFT_WEIGHTS, 1)
            nc.sync.dma_start(
                w4[w][:].bitcast(I32).rearrange("p (a n) -> p a n", a=PASSES),
                words.bitcast(I32).rearrange("a p n -> p a n"),
            )

        def load_delta(pool, w, wd, a):
            raw[w, a] = pool.tile([P, PACK, N], F32, name=f"raw{w}{a}", tag=f"raw{w}{a}", align_bytes=256)
            rows = wd[a * K_PASS : (a + 1) * K_PASS, :]
            nc.sync.dma_start(raw[w, a][:], rows.rearrange("(p i) n -> p i n", i=PACK))

        def load_rows(name, dst, src, pair, h):
            dst[pair, h] = late.tile([P, PAIR], F32, name=f"{name}{pair}{h}")
            nc.sync.dma_start(dst[pair, h][:], src[h * P : (h + 1) * P, pair * PAIR : (pair + 1) * PAIR])

        def cols_of(held, j0, n, h):
            pair, first = divmod(j0, PAIR)
            return held[pair, h][:, first : first + n]

        with tc.tile_pool(name="window", bufs=1, side="right") as window:
            srows = window.tile([P, T], U8, name="srows", align_bytes=256)
            nc.sync.dma_start(srows[:].bitcast(I32)[ROWS0:P, :], compact(tab_scales))
            nc.sync.dma_start(offsets[:], offs)
            for w, scales in ((KEY, wk4_scales), (VALUE, wv4_scales)):
                cols = slice((CH + w * N) // 4, (CH + (w + 1) * N) // 4)
                nc.sync.dma_start(stage[:].bitcast(I32)[ROWS0:P, cols], compact(scales))
            nc.sync.dma_start(table[:], tab_words[0].rearrange("p t i -> p (t i)").bitcast(I32))
            load_base(keep, KEY, wk4_words)
            warm = keep.tile([P, 2], F32, name="warm")
            nc.gpsimd.memset(warm[:, 0:1], 0.0)
            nc.scalar.activation(warm[:, 1:2], warm[:, 0:1], SIGMOID)
            nc.vector.memset(srows[:].bitcast(I32)[0:ROWS0, :], 0)
            nc.vector.memset(planes[:].bitcast(I32), 0)
            nc.vector.memset(planes1[:].bitcast(I32), 0)
            nc.vector.memset(planes23[:].bitcast(I32), 0)
            with tc.tile_pool(name="first", bufs=1) as first:
                rows0 = first.tile([P, CH], U8, name="rows0", align_bytes=256)
                nc.vector.tensor_copy(rows0[:], srows[:].indirect(entries(0, CH)))
                nc.vector.tensor_copy(rows_rest[:, PAIR:rest_w], srows[:].indirect(entries(3 * CH, CH)))
                nc.vector.tensor_copy(stage[:].bitcast(I32)[:, 0 : CH // 4], rows0[:].bitcast(I32))
                spread(planes, stage[:])
            early = ctx.enter_context(tc.tile_pool(name="early", bufs=1))
            load_delta(early, KEY, wkd, 0)
            load_base(early, VALUE, wv4_words)
            nc.vector.tensor_copy(rows_rest[:, 0:PAIR], srows[:].indirect(entries(CH, PAIR)))
            spread(planes1, rows_rest[:, 0:CH])

        spare = psum.tile([P, CH], F32, name="spare", tag=f"bank{BANKS - 1}")
        for i in range(WARM_PASSES):
            nc.tensor.matmul_mx(
                out=spare[:],
                lhsT=stage[:, 0 : 2 * P].bitcast(FP4X4),
                lhsT_scale=stage[:, 0:P],
                rhs=planes23[:, 0 : 2 * CH].bitcast(FP4X4),
                rhs_scale=planes23[:, 2 * CH : 3 * CH],
                start=True,
                stop=True,
            )

        late = ctx.enter_context(tc.tile_pool(name="late", bufs=1, side="right"))
        for w, wd, a in ((KEY, wkd, 1), (VALUE, wvd, 0), (VALUE, wvd, 1)):
            load_delta(late, w, wd, a)
        load_rows("st", st_of, st, 0, 0)
        bias = late.tile([P, HALVES], F32, name="bias")
        with nc.allow_non_contiguous_dma(reason="one bias value a partition"):
            nc.sync.dma_start(bias[:], b.rearrange("(h p) -> p h", p=P))
        load_rows("st", st_of, st, 0, 1)
        spread(planes23, rows_rest[:, CH:rest_w])
        load_rows("res", res_of, res, 0, 0)
        load_rows("st", st_of, st, 1, 0)
        load_rows("res", res_of, res, 0, 1)
        load_rows("st", st_of, st, 1, 1)
        load_rows("res", res_of, res, 1, 0)
        load_rows("res", res_of, res, 1, 1)

        def gather_words(tile, j0, n):
            nc.vector.tensor_copy(tile, table[:].bitcast(U32).indirect(entries(j0, n)))

        def part_pass(picked, c, a, cols):
            dst = parted[c][:].bitcast(U16).rearrange("p (a j) -> p a j", a=PASSES)
            src = picked.bitcast(U16).rearrange("p (j a) -> p a j", a=PASSES)
            nc.vector.tensor_copy(dst[:, a, cols], src[:, a, cols])

        def part_both(picked, c, cols):
            lines = slice(cols.start // LINE, cols.stop // LINE)
            dst = parted[c][:].bitcast(U16).rearrange("p (a m u) -> p m a u", a=PASSES, u=LINE)
            src = picked.bitcast(U16).rearrange("p (m u a) -> p m a u", a=PASSES, u=LINE)
            nc.vector.tensor_copy(dst[:, lines], src[:, lines])

        def quantise(w, a):
            grouped = keep.tile([P, PACK * N], BF16, name=f"grouped{w}{a}", tag=f"grouped{w}{a}", align_bytes=256)
            nc.scalar.copy(
                grouped[:].rearrange("p (m u i) -> p m i u", u=4, i=PACK),
                raw[w, a][:].rearrange("p i (m u) -> p m i u", u=4),
            )
            codes[w, a] = shifted(keep, f"codes{w}{a}", N, U32, SHIFT_WEIGHTS, 4)
            dscale[w, a] = shifted(keep, f"dscale{w}{a}", N, U8, SHIFT_SCALES, 1)
            nc.vector.quantize_mx(out=codes[w, a][:].bitcast(FP8X4), scales=dscale[w, a][:], in_=grouped[:])

        def one_pass(acc, w, h, a, delta, j0, n, start=False, stop=False):
            c, o = divmod(j0, CH)
            words = parted[c][:, 2 * (a * CH + o) : 2 * (a * CH + o + n)].bitcast(FP4X4)
            if c == 0:
                scale = planes[:, a * first_w + j0 : a * first_w + j0 + n]
            elif c == 1:
                scale = planes1[:, a * CH + o : a * CH + o + n]
            else:
                scale = planes23[:, a * PAIR + j0 - PAIR : a * PAIR + j0 - PAIR + n]
            if delta:
                lhsT = codes[w, a][:, h * P : (h + 1) * P].bitcast(FP8X4)
                lhsT_scale = dscale[w, a][:, h * P : (h + 1) * P]
            else:
                n0 = a * N + h * P
                s0 = a * first_w + CH + w * N + h * P
                lhsT = w4[w][:, 2 * n0 : 2 * (n0 + P)].bitcast(FP4X4)
                lhsT_scale = planes[:, s0 : s0 + P]
            nc.tensor.matmul_mx(
                out=acc, lhsT=lhsT, lhsT_scale=lhsT_scale, rhs=words, rhs_scale=scale, start=start, stop=stop
            )

        def open_bank(j0, n, w, h, slot):
            bank[j0, w, h] = psum.tile([P, n], F32, name=f"bank{j0}_{w}{h}", tag=f"bank{slot}")

        first_order = [
            (KEY, 0, 0),
            (KEY, 0, 1),
            (KEY, 1, 0),
            (VALUE, 0, 0),
            (KEY, 1, 1),
            (VALUE, 0, 1),
            (VALUE, 1, 0),
            (VALUE, 1, 1),
        ]

        def first_bases(c, cuts):
            j0 = c * CH
            for w in (KEY, VALUE):
                for h in range(HALVES):
                    open_bank(j0, CH, w, h, first_order.index((w, h, c)))
            for cols in cuts:
                n = cols.stop - cols.start
                for a in range(PASSES):
                    for h in range(HALVES):
                        begin = cols.start == 0 and a == 0
                        one_pass(bank[j0, KEY, h][:, cols], KEY, h, a, False, j0 + cols.start, n, start=begin)
            for a in range(PASSES):
                for h in range(HALVES):
                    one_pass(bank[j0, VALUE, h][:], VALUE, h, a, False, j0, CH, start=a == 0)

        def first_deltas(w, a, chunks=(0, 1), halves=(0, 1)):
            for h in halves:
                for c in chunks:
                    one_pass(bank[c * CH, w, h][:], w, h, a, True, c * CH, CH, stop=a == PASSES - 1)

        whole = slice(0, CH)
        low, high = slice(0, HC), slice(HC, CH)
        picked0 = keep.tile([P, CH], U32, name="picked0", align_bytes=256)
        parted[0] = keep.tile([P, PASSES * 2 * CH], U8, name="parted0", align_bytes=256)
        gather_words(picked0[:, low], 0, HC)
        gather_words(picked0[:, high], HC, HC)
        for a in range(PASSES):
            part_pass(picked0[:], 0, a, low)
        part_both(picked0[:], 0, high)
        first_bases(0, (low, high))
        picked1 = keep.tile([P, CH], U32, name="picked1", tag="stage", align_bytes=256)
        gather_words(picked1[:], CH, CH)
        quantise(KEY, 0)
        first_deltas(KEY, 0, (0,))
        parted[1] = early.tile([P, PASSES * 2 * CH], U8, name="parted1", tag="raw00", align_bytes=256)
        for a in range(PASSES):
            part_pass(picked1[:], 1, a, whole)
        first_bases(1, (whole,))
        first_deltas(KEY, 0, (1,))
        both = keep.tile([P, PAIR], U32, name="picked23", tag="grouped00", align_bytes=256)
        gather_words(both[:], 2 * CH, PAIR)
        quantise(KEY, 1)
        first_deltas(KEY, 1)
        parted[2] = late.tile([P, PASSES * 2 * CH], U8, name="parted2", tag="raw01", align_bytes=256)
        part_both(both[:, 0:CH], 2, whole)
        quantise(VALUE, 0)
        first_deltas(VALUE, 0, halves=(0,))
        parted[3] = late.tile([P, PASSES * 2 * CH], U8, name="parted3", tag="raw10", align_bytes=256)
        part_both(both[:, CH:PAIR], 3, whole)
        quantise(VALUE, 1)
        first_deltas(VALUE, 1, halves=(0,))
        for a in range(PASSES):
            first_deltas(VALUE, a, halves=(1,))

        prod, total = {}, {}
        for h in range(HALVES):
            prod[0, h] = keep.tile([P, PAIR], F32, name=f"prod0_{h}")
            total[0, h] = keep.tile([P, PAIR], F32, name=f"total0_{h}")

        def piece(held, name, j0, n, h):
            if j0 < PAIR:
                return held[0, h][:, j0 : j0 + n]
            if (j0, h) not in held:
                held[j0, h] = keep.tile([P, n], F32, name=f"{name}{j0}_{h}")
            return held[j0, h][:]

        def make_gate(j0, h):
            if (j0, h) == (0, 0):
                pre = late.tile([P, CH], F32, name="pre_first", tag="raw11", align_bytes=256)
            elif (j0, h) == (CH, 0):
                pre = keep.tile([P, CH], F32, name="pre_second", tag="grouped11", align_bytes=256)
            elif j0 < PAIR:
                pre = cols_of(st_of, 0, CH, j0 // CH)
            else:
                pre = keep.tile([P, CH], F32, name=f"pre{j0}_{h}")
            nc.vector.tensor_tensor(pre[:], cols_of(st_of, j0, CH, h), bank[j0, KEY, h][:], MULT)
            gate[j0, h] = keep.tile([P, CH], F32, name=f"gate{j0}_{h}")
            nc.scalar.activation(gate[j0, h][:], pre[:], SIGMOID, bias=bias[:, h : h + 1])

        def gated(j0, n, h):
            g0 = j0 // CH * CH
            gate_cols = gate[g0, h][:, j0 - g0 : j0 - g0 + n]
            nc.vector.tensor_tensor(piece(prod, "prod", j0, n, h), gate_cols, bank[j0, VALUE, h][:], MULT)

        def add(engine, j0, n, h):
            summed = piece(total, "total", j0, n, h)
            engine.tensor_tensor(summed, piece(prod, "prod", j0, n, h), cols_of(res_of, j0, n, h), ADD)

        def store(j0, n, h):
            nc.sync.dma_start(out[h * P : (h + 1) * P, j0 : j0 + n], piece(total, "total", j0, n, h))

        def whole_sum(j0, n, w, h, slot):
            kinds = (True, False) if len(bank) % 2 == 0 else (False, True)
            open_bank(j0, n, w, h, slot % BANKS)
            for delta in kinds:
                for a in range(PASSES):
                    begin, end = (delta, a) == (kinds[0], 0), (delta, a) == (kinds[1], PASSES - 1)
                    one_pass(bank[j0, w, h][:], w, h, a, delta, j0, n, start=begin, stop=end)

        j1, j2, j3 = CH, 2 * CH, 3 * CH
        for w, h, c in first_order[:-1]:
            if w == KEY:
                make_gate(c * CH, h)
            else:
                gated(c * CH, CH, h)
                add(nc.gpsimd, c * CH, CH if h == 0 else SHARE, h)
        store(0, PAIR, 0)

        whole_sum(j2, CH, KEY, 0, 0)
        make_gate(j2, 0)
        gated(j1, CH, 1)
        whole_sum(j3, CH, KEY, 0, 1)
        make_gate(j3, 0)
        whole_sum(j2, CH, VALUE, 0, 2)
        gated(j2, CH, 0)
        add(nc.vector, SHARE, PAIR - SHARE, 1)
        store(0, PAIR, 1)
        add(nc.gpsimd, j2, CH, 0)
        store(j2, CH, 0)
        whole_sum(j2, CH, KEY, 1, 3)
        make_gate(j2, 1)
        whole_sum(j3, CH, VALUE, 0, 4)
        gated(j3, CH, 0)
        add(nc.gpsimd, j3, CH, 0)
        store(j3, CH, 0)
        whole_sum(j3, CH, KEY, 1, 5)
        make_gate(j3, 1)

        pieces = [j2 + u * HC for u in range(PAIR // HC)]
        for j0, tag in ((j2, "raw01"), (j3, "raw10")):
            total[j0, 1] = late.tile([P, HC], F32, name=f"total{j0}_1", tag=tag, align_bytes=256)
        for i, j0 in enumerate(pieces):
            whole_sum(j0, HC, VALUE, 1, 6 + i)
            gated(j0, HC, 1)
            if i > 0:
                add(nc.vector, pieces[i - 1], HC, 1)
                store(pieces[i - 1], HC, 1)
        add(nc.vector, pieces[-1], HC, 1)
        store(pieces[-1], HC, 1)
